import numpy as np, ml_dtypes
CORES = [51,54,179,182]
N = 4
BF = ml_dtypes.bfloat16
def gentries(a):
    return np.ascontiguousarray(a.reshape(8, 16, -1).transpose(0, 2, 1)).reshape(8, -1)
def gtable(e):
    e = np.asarray(e); return np.ascontiguousarray(e.reshape(8, -1, 16).transpose(0, 2, 1)).reshape(128, -1).astype(np.int32)
W, C, RO = 2048, 256, 4
LA, LB, LE, WD = 832, 1024, 1040, 32
def parts(rng):
    x = rng.integers(0, 256, (N, 8, 16, W)); a = rng.integers(0, W, (N, 8, C, 16)); p = rng.integers(0, W, (N, 8, C, 16))
    pool = rng.integers(0, W, (N, 8, 32)); hot = np.take_along_axis(pool, rng.integers(0, 32, (N, 8, C * 16)), 2).reshape(N, 8, C, 16)
    return x, a, np.where(rng.random((N, 8, C, 16)) < 0.3, hot, p)
def pack(x, a, p):
    return {"x0": np.ascontiguousarray(x.reshape(N, 128, W)).astype(np.float32).astype(BF), "ka": np.stack([gtable(v.reshape(8, -1)) for v in a]), "ph": np.stack([gtable(v.reshape(8, -1)) for v in p])}
def alike(rng, a, p, share):
    m = (rng.random((N, 8, C, 1)) < share) & (np.arange(16) == rng.integers(0, 16, (N, 8, C, 1)))
    return np.where(m, a, p)
def setup_inputs(rng):
    x, a, p = parts(rng)
    return pack(x, a, alike(rng, a, p, 0.08))
def setup_inputs_spread(rng):
    x, a, p = parts(rng)
    v = np.minimum((np.exp2(8 * rng.random((N, 8, 1, W))) * rng.random(x.shape)).astype(np.int64), 255)
    x = np.where(rng.random(x.shape) < 0.5, v, 255 - v)
    a = np.minimum((W * rng.random(a.shape) ** 2).astype(np.int64), W - 1); u = np.minimum((W * rng.random(a.shape) ** 3).astype(np.int64), W - 1)
    return pack(x, a, np.where(rng.random(a.shape) < 0.5, u, p))
def setup_inputs_ends(rng):
    x, a, p = parts(rng); x = 255 * rng.integers(0, 2, x.shape)
    h = rng.choice(np.array([3, 4, 4, 5, 16]), (N, 8)); h[N - 1, 7] = 16; h[0, 7] = 4; h[0, 0] = 4; h[0, 1] = 3; h[N - 1, 6] = 4
    for r in range(N):
        for g in range(8):
            w = x[r, g]; w[:, W - 1] = w[:, 0]; o = rng.permutation(16)[:h[r, g]]
            if h[r, g] == 16: w[:, 0] = 0
            w[o, W - 1] = 255 - w[o, 0]
    kind = rng.choice(np.array([0, 1, 2]), (N, 8, C, 1), p=[0.4, 0.34, 0.26]); kind[:, :, [0, 1, 3, C - 2, C - 1]] = 0
    e = rng.integers(0, 2, (N, 8, C, 1))
    a = np.where(kind == 0, e * (W - 1), np.where(kind == 1, (W - 1) * rng.integers(0, 2, a.shape), a))
    p = np.where(kind == 0, (1 - e) * (W - 1), np.where(kind == 1, (W - 1) * rng.integers(0, 2, a.shape), p))
    return pack(x, a, p)
def setup_inputs_corners(rng):
    x = np.zeros((N, 8, 16, W), np.int64); a = np.zeros((N, 8, C, 16), np.int64); p = np.zeros((N, 8, C, 16), np.int64)
    far = np.array([LA - 1, LA, LA + 1, LB - 1, LB, LB + 3, LB + 4, LB + 59, LB + 60]); h = W // 2; M = 36; lane = np.arange(16)
    signs = np.stack([np.ones(16, np.int64), -np.ones(16, np.int64), 1 - 2 * (lane & 1)])
    for g in range(8):
        q = rng.permutation(W); low = q[1:h]; high = q[h + M:]; mids = q[h:h + M]
        m0 = rng.choice(np.array([-1, 0, 15, 15, 6]), C); o = lane[None, :] == m0[:, None]; o = o ^ (rng.random((C, 1)) < 0.5)
        k = rng.integers(0, 16, C); k = np.where(k == m0, (k + 1) & 15, k); swap = rng.random(C) < 0.5
        for r in range(N):
            w = x[r, g]; w[:, low] = rng.integers(0, 31, (16, len(low))); w[:, high] = rng.integers(215, 256, (16, len(high)))
            b = rng.integers(100, 151, 16); w[:, q[0]] = b; T = rng.permutation(np.resize(far, M))
            am = T[None, :] // 16 + (lane[:, None] < T[None, :] % 16); w[:, mids] = b[:, None] + am * signs[rng.integers(0, 3, M)].T
            lo1 = low[rng.integers(0, len(low), (C, 16))]; lo2 = low[rng.integers(0, len(low), (C, 16))]; hi1 = high[rng.integers(0, len(high), (C, 16))]; hi2 = high[rng.integers(0, len(high), (C, 16))]
            u = np.where(o, hi1, lo1); v = np.where(o, lo2, hi2)
            n = (0, 16, 15, C, 1, 17, 14, 31)[(g + 3 * r) % 8]; oc = rng.permutation(C); die = oc[:n]; rest = oc[n:]
            v[die, k[die]] = np.where(o[die, k[die]], hi2[die, k[die]], lo2[die, k[die]])
            edge = die[1::2]; under = mids[T == LA - 1]; md = under[rng.integers(0, len(under), len(edge))]
            u[edge, k[edge]] = np.where(swap[edge], md, q[0]); v[edge, k[edge]] = np.where(swap[edge], q[0], md)
            over = mids[T >= LA]; md = over[rng.integers(0, len(over), len(rest))]
            u[rest, k[rest]] = np.where(swap[rest], md, q[0]); v[rest, k[rest]] = np.where(swap[rest], q[0], md)
            assert int(np.sum(np.min(np.add.reduce(np.abs(w[:, u] - w[:, v]), axis=0), axis=1) < LA)) == n
            a[r, g] = u; p[r, g] = v
    return pack(x, a, p)
def setup_inputs_full(rng):
    x, a, p = parts(rng); lane = np.arange(16); h = W // 2; u = W // 4; z = int(rng.integers(0, N)); dead = int(rng.integers(0, 8))
    for g in range(8):
        if g == dead: continue
        for r in range(N):
            w = x[r, g]; q = rng.permutation(W); right = q[:h]; left = q[h:h + u]; out = q[h + u:]; b = rng.integers(100, 151, (16, 1))
            w[:, right] = b + rng.integers(0, 4, (16, h))
            far = np.where(rng.random((16, u)) < 0.5, 78 + rng.integers(0, 3, (16, u)), -75 - rng.integers(0, 3, (16, u)))
            near = np.argsort(rng.random((16, u)), axis=0) < 4
            w[:, left] = b + np.where(near, rng.integers(-8, 12, (16, u)), far)
            w[:, out] = b + rng.integers(90, 100, (16, len(out))) * (1 - 2 * rng.integers(0, 2, (16, len(out))))
            i = (rng.permutation(h)[:C], np.full(C, int(rng.integers(0, h))), rng.integers(0, 6, C))[(g + r) % 3]
            here = lane[None, :] == rng.integers(0, 16, (C, 1))
            a[r, g] = np.where(here, left[rng.integers(0, u, (C, 16))], right[rng.integers(0, h, (C, 16))])
            p[r, g] = np.where(here, right[i][:, None], out[rng.integers(0, len(out), (C, 16))])
    q = rng.permutation(np.arange(1, W)); s1 = q[:h]; s2 = q[h:h + u]; s0 = np.append(q[h + u:], 0)
    a[:, dead] = 0; p[:, dead] = s0[rng.integers(0, len(s0), (N, C, 16))]
    far = np.array([LB - 1, LB, LB + 1, LB + 3, LB + 4, LB + 31, LB + 59, LB + 60]); T = far[np.arange(h) % 8]
    cl = np.minimum(rng.integers(0, 8, (C, 1)) + rng.integers(0, 3, (C, 16)), 7)
    a[(z - 2) % N, dead] = s1[cl + 8 * rng.integers(0, h // 8, (C, 16))]; p[(z + 2) % N, dead] = s2[rng.integers(0, u, (C, 16))]
    x[:, dead] = rng.integers(215, 256, (N, 16, W))
    for r in range(N):
        w = x[r, dead]; w[:, s1] = rng.integers(0, 31, (16, h))
        if r == z:
            b = rng.integers(100, 151, (16, 1)); w[:] = b + rng.integers(0, 4, (16, W)); w[:, s2] = b
            w[:, s1] = b + (T[None, :] // 16 + (lane[:, None] < T[None, :] % 16)) * (1 - 2 * rng.integers(0, 2, (16, h)))
    return pack(x, a, p)
def setup_inputs_ties(rng):
    x, a, p = parts(rng); x = rng.integers(0, 176, x.shape)
    pool = rng.integers(0, W, (N, 8, 8)); pool[..., 0] = 0; pool[..., 7] = W - 1
    hot = np.take_along_axis(pool, rng.integers(0, 8, (N, 8, C * 16)), 2).reshape(N, 8, C, 16); p[:, 1::2] = hot[:, 1::2]
    src = np.arange(16) % rng.choice(np.array([1, 1, 1, 2, 4, 16]), (N, 8, C, 1))
    return pack(x, np.take_along_axis(a, src, 3), np.take_along_axis(p, src, 3))
def check_inputs(d):
    bad = []
    for k, lo, hi in (("x0", 0, 255), ("ka", 0, W - 1), ("ph", 0, W - 1)):
        v = np.asarray(d[k]).astype(np.float64)
        if not (np.min(v) >= lo and np.max(v) <= hi): bad.append("range of " + k)
    v = np.asarray(d["x0"]).astype(np.float64)
    if np.any(v != np.floor(v)): bad.append("whole numbers of x0")
    return bad
def reference(x0, ka, ph):
    X = x0.astype(np.float32).astype(np.int32).reshape(N, 8, 16, W)
    K = np.stack([gentries(v) for v in ka]).astype(np.int64).reshape(N, 8, C, 16)
    P = np.stack([gentries(v) for v in ph]).astype(np.int64).reshape(N, 8, C, 16)
    A = np.zeros((N, 8, 1), np.int64); place = np.arange(16)
    for t in range(RO):
        if t > 0: K = np.roll(K, 1, axis=0); P = np.roll(P, -1, axis=0)
        for r in range(N):
            x, a, p = X[r], K[r].copy(), P[r].copy()
            s = np.take_along_axis(x, a.reshape(8, 1, C * 16), 2).reshape(8, 16, C, 16); y = np.take_along_axis(x, p.reshape(8, 1, C * 16), 2).reshape(8, 16, C, 16)
            D = np.add.reduce(np.abs(s - y), axis=1)
            k = np.argmin(D, axis=2)
            d = np.take_along_axis(D, k[:, :, None], 2)[:, :, 0]
            sk = np.take_along_axis(s, k[:, None, :, None], 3)[..., 0]; yk = np.take_along_axis(y, k[:, None, :, None], 3)[..., 0]
            kill = d < LA; prime = ~kill & (d < LB + 4 * (A[r] & 15))
            step = np.where(np.add.reduce(sk, axis=1) > np.add.reduce(yk, axis=1), 1, -1) * (1 + (d & 3))
            n = np.take_along_axis(p, ((k + step) & 15)[:, :, None], 2)[:, :, 0]
            xn = np.take_along_axis(x, n[:, None, :], 2)
            near = np.add.reduce(np.abs(s - xn[..., None]), axis=1) < LE
            m = np.where(np.any(near, axis=2), np.argmax(near, axis=2), -1)
            fresh = np.take_along_axis(a, np.clip(m[:, :, None] + place, 0, 15), 2); fresh[:, :, 0] = n
            v = np.take_along_axis(p, k[:, :, None], 2)[:, :, 0]; new = np.where(np.abs(sk - yk) <= WD, (yk + 128) & 255, yk)
            for g in range(8):
                c = np.nonzero(prime[g])[0]; w = c[np.unique(v[g, c], return_index=True)[1]]
                x[g][:, v[g, w]] = new[g][:, w]
            P[r] = np.where(kill[:, :, None], (((a * p) >> 5) + p) & (W - 1), p)
            K[r] = np.where(prime[:, :, None], fresh, a)
            A[r] = A[r] + np.add.reduce(kill.astype(np.int64), axis=1)[:, None]
    return {"yk": np.stack([gtable(v.reshape(8, -1)) for v in K]).astype(np.float32), "yp": np.stack([gtable(v.reshape(8, -1)) for v in P]).astype(np.float32), "yx": X.reshape(N, 128, W).astype(np.float32).astype(BF)}

@@ -1,0 +1,461 @@
+from concourse.mybir import AluOpType as Op, ActivationFunctionType as AF, AxisListType as AX
+
+RO = 4
+F, B, H, I, U = "float32", "bfloat16", "float16", "int32", "uint16"
+SCRATCH = {}
+for _n, _w, _d in (
+        ("xt0", 2304, B), ("xt1", 2304, B), ("nk", 256, I), ("np_", 256, I), ("yg", 4096, B), ("sg", 4096, B), ("eg", 4096, B),
+        ("kp", 256, F), ("p32", 256, F), ("sn", 256, F), ("code", 256, F), ("mi", 256, I),
+        ("v8", 16, I), ("l8", 16, U), ("kf", 16, B), ("lt", 16, F), ("fl", 16, F), ("fl16", 16, U),
+        ("nsel", 256, H), ("ksel", 256, H), ("nb", 256, U), ("ns", 256, F), ("pks", 256, F),
+        ("pa", 256, F), ("pt", 256, I), ("pn", 256, I), ("yp32", 256, F),
+        ("npx", 16, F), ("o1", 16, F), ("o2", 16, F), ("o16", 16, U), ("nfix", 256, F), ("kh", 128, H),
+        ("wt0", 4096, F), ("wt1", 4096, F), ("fr", 256, F),
+        ("yk32", 256, F), ("ew", 256, F), ("ms", 256, F), ("zf", 256, F),
+        ("rr", 256, H), ("ol", 16, F), ("eq", 4096, B), ("cs", 256, B), ("v1", 16, F), ("v2", 16, F), ("w16", 16, U),
+        ("kk", 16, I), ("ok", 16, I), ("ok16", 16, U), ("yk_", 256, B), ("dk", 256, B), ("adk", 256, B), ("sgn", 256, B),
+        ("c1", 256, B), ("tt", 256, B), ("ca", 1, F), ("aa", 1, I), ("ab", 1, I), ("thr", 1, F),
+        ("pi", 2, I), ("li", 2, I), ("lf", 2, F), ("pf", 2, F), ("pl", 2, F), ("i1", 2048, I), ("i2", 2048, I), ("st", 2048, B),
+        ("dg_", 2048, B), ("ones", 128, B), ("gm", 128, B), ("tri", 128, B), ("idn", 128, B),
+        ("z1", 143, B), ("z64", 143, B), ("cj", 256, B), ("rst", 256, F), ("rs2", 256, F),
+        ("q16", 16, F), ("cf", 16, F), ("c16", 16, I), ("cd", 16, F), ("cw", 16, F),
+        ("lk", 256, I), ("lz", 256, I), ("ls", 256, I), ("l3", 256, I),
+        ("lutf", 256, B), ("lutk", 256, B), ("lutm", 16, F), ("luto", 16, F), ("lutp", 16, F)):
+    SCRATCH[_n] = ("sbuf", [128, _w], _d)
+for _n in ("d3", "a3", "ae"):
+    SCRATCH[_n] = ("sbuf", [128, 16, 256], B)
+SCRATCH["kd"] = ("dram", [8, 32, 128], F)
+for _t in range(RO):
+    for _h in range(2):
+        SCRATCH["k16_%d_%d" % (_t, _h)] = ("sbuf", [128, 128], U)
+        SCRATCH["ks_%d_%d" % (_t, _h)] = ("sbuf", [128, 128], U)
+    SCRATCH["p16_%d" % _t] = ("sbuf", [128, 256], U)
+    SCRATCH["ps_%d" % _t] = ("sbuf", [128, 256], U)
+ORDER = """ts0 da0 dc2 ts1 da1 sn0 ds0 ds1 sg0 dc3 ts2 le0 pl1 ts3 he0 sg1 da2 da3 ds2 sn1 n0 ds3 na0 sg2 n1 le1 fa he1 pk kh n2 nl0
+    sh0 sg3 sh1 wr ph sh2 eq yk al na1 nl1 n3 va ar0 co na2 na3 sh3 sh4 nl2 ch sc y0 y1 nl3 y2 p32 y3 ar1 pl0 dc0 dc1 w0"""
+PSUM = ("bT", "bT2", "bD", "bD2", "bN", "bM", "bC", "bZ")
+for _n in PSUM:
+    SCRATCH[_n] = ("psum", [128, 512], F)
+SEMAPHORES = (["v", "s", "p", "g", "lx", "lp", "lk", "oy", "ok", "op", "sent", "kz", "kd", "wd"]
+              + ["ka%d_%d" % (t, h) for t in range(1, RO) for h in range(2)] + ["pa%d" % t for t in range(1, RO)]
+              + ["xc%d" % t for t in range(RO)])
+
+
+def rank_program(g, core, T, topo):
+    rank = T.rank_of(core)
+    if rank is None:
+        return
+    n_ranks = len(T.cores)
+    Q = {"v": g.vector, "s": g.scalar, "p": g.tensor, "g": g, "y": g.sync}
+    cnt = {"v": 0, "s": 0, "p": 0, "g": 0}
+    seen = {q: {} for q in Q}
+    snap, hist = {}, {}
+
+    def a(name, lo=0, hi=None, step=None):
+        hi = SCRATCH[name][1][1] if hi is None else hi
+        return (T[name][:, lo:hi] if step is None else T[name][:, lo:hi:step], name, lo, hi)
+
+    def a3(name, q0, q1, c0=None, c1=None):
+        return (T[name][:, q0:q1, :] if c0 is None else T[name][:, q0:q1, c0:c1], name, 256 * q0, 256 * q1)
+
+    def row(name, q):
+        return (T[name][:, q], name, 256 * q, 256 * q + 256)
+
+    def ind(win, off):
+        return (win[0].indirect(off[0]), win, off)
+
+    def need(q, outs, ins):
+        want = {}
+        for kind, lst in (("w", outs), ("r", ins)):
+            for _, name, lo, hi in lst:
+                bank = name in PSUM
+                for k2, l2, h2, q2, sem, val in hist.get(name, ()):
+                    if q2 == q and q != "dma" and (k2 == "r" or q == "p" and kind == "w"):
+                        continue
+                    if not (bank and q2 != q) and (k2 == kind == "r" or h2 <= lo or l2 >= hi):
+                        continue
+                    want[sem] = max(want.get(sem, 0), val)
+        return want
+
+    def waits(q, want):
+        for sem, val in sorted(want.items()):
+            if seen[q].get(sem, 0) < val:
+                Q[q].wait_ge(T.sem[sem], val)
+                seen[q][sem] = val
+                for s2, v2 in snap.get((sem, val), {}).items():
+                    seen[q][s2] = max(seen[q].get(s2, 0), v2)
+
+    def note(q, sem, val, outs, ins, known):
+        snap[(sem, val)] = dict(known)
+        for kind, lst in (("w", outs), ("r", ins)):
+            for _, name, lo, hi in lst:
+                h = hist.setdefault(name, [])
+                if kind == "w":
+                    h[:] = [e for e in h if not (e[1] >= lo and e[2] <= hi)]
+                h.append((kind, lo, hi, q, sem, val))
+
+    def flat(lst):
+        r = []
+        for x in lst:
+            r += [x] if isinstance(x[1], str) else [x[1], x[2]]
+        return r
+
+    def do(q, fn, outs, ins):
+        o, i = flat(outs), flat(ins)
+        waits(q, need(q, o, i))
+        cnt[q] += 1
+        fn().then_inc(T.sem[q], 1)
+        note(q, q, cnt[q], o, i, seen[q])
+
+    def dma(q, sem, out, in_, outs, ins):
+        waits(q, need("dma", outs, ins))
+        Q[q].dma_start(out, in_).then_inc(T.sem[sem], 16)
+        note("dma", sem, 16, outs, ins, seen[q])
+
+    V, S, P = g.vector, g.scalar, g.tensor
+
+    def copy(out, in_):
+        do("v", lambda: V.tensor_copy(out[0], in_[0]), [out], [in_])
+
+    def tt(out, x, y, op):
+        if isinstance(out[1], tuple):
+            do("v", lambda: V.tensor_tensor(out[0], x[0], y[0], op), [out[1]], [x, y, out[2]])
+        else:
+            do("v", lambda: V.tensor_tensor(out[0], x[0], y[0], op), [out], [x, y])
+
+    def ts(out, x, s1, op0, s2=None, op1=None):
+        ins = [x] + [s for s in (s1, s2) if isinstance(s, tuple)]
+        c = [s[0] if isinstance(s, tuple) else s for s in (s1, s2)]
+        if op1 is None:
+            do("v", lambda: V.tensor_scalar(out[0], x[0], c[0], None, op0), [out], ins)
+        else:
+            do("v", lambda: V.tensor_scalar(out[0], x[0], c[0], c[1], op0, op1), [out], ins)
+
+    def scan(out, d0, d1, op0, op1):
+        do("v", lambda: V.tensor_tensor_scan(out[0], d0[0], d1[0], 1000000.0, op0, op1), [out], [d0, d1])
+
+    def fill(out, val):
+        do("v", lambda: V.memset(out[0], val), [out], [])
+
+    def act(out, in_, func, **kw):
+        do("s", lambda: S.activation(out[0], in_[0], func, **kw), [out], [in_])
+
+    def mm(out, l, r, start, stop):
+        do("p", lambda: P.matmul(out[0], l[0], r[0], start, stop), [out], [l, r])
+
+    def iota(out, pattern, base, cm, **kw):
+        do("g", lambda: g.iota(out[0], pattern, base, cm, **kw), [out], [])
+
+    def asel(out, in_, pattern, cop, base, cm):
+        do("g", lambda: g.affine_select(out[0], in_[0], pattern, cop, 0.0, base, cm), [out], [in_])
+
+    dma("y", "lp", T.np_[:], T.ph[:], [a("np_")], [])
+    dma("s", "lk", T.nk[:], T.ka[:], [a("nk")], [])
+    dma("y", "lx", T.xt0[:, 0:2048], T.x0[:], [a("xt0", 0, 2048)], [])
+
+    small = dict(allow_small_or_imprecise_dtypes=True)
+    iota(a("pi"), [[0, 2]], 0, 1)
+    fill(a("ones"), 1.0)
+    asel(a("gm"), a("ones"), [[-16, 8], [0, 16]], Op.is_ge, 0, 1)
+    asel(a("gm"), a("gm"), [[16, 8], [0, 16]], Op.is_ge, 15, -1)
+    asel(a("idn"), a("ones"), [[1, 128]], Op.is_equal, 0, -1)
+    iota(a("cj"), [[0, 16], [4, 16]], 1, 0, **small)
+    iota(a("lk"), [[0, 4], [1, 16], [0, 4]], 0, 0)
+    iota(a("lz"), [[1, 4], [0, 64]], 1, 0)
+    iota(a("ls"), [[0, 64], [2, 2], [0, 2]], -1, 0)
+    iota(a("q16"), [[16, 16]], 0, 0, **small)
+    asel(a("tri"), a("gm"), [[1, 128]], Op.is_gt, 0, -1)
+    iota(a("i1"), [[1, 16], [0, 8], [1, 16]], -1, 0)
+    iota(a("i2"), [[256, 16], [1, 128]], 0, 0)
+    fill(a("z1"), 0.0)
+    fill(a("zf"), 0.0)
+    fill(a("xt0", 2048, 2304), 0.0)
+    fill(a("xt1", 2048, 2304), 0.0)
+    ts(a("li"), a("pi"), 15, Op.bitwise_and)
+    copy(a("lf"), a("li"))
+    copy(a("z1", 15, 143, 16), a("gm", 0, 128, 16))
+    ts(a("z64"), a("z1"), 64.0, Op.mult)
+    fill(a("rst"), 0.0)
+    fill(a("rst", 0, 256, 16), 1000000.0)
+    fill(a("thr"), 65536.0)
+    fill(a("aa"), 0)
+    fill(a("wt0", 0, 2048), 0.0)
+    copy(a("p16_0"), a("np_"))
+    for h in range(2):
+        copy(a("k16_0_%d" % h), a("nk", 128 * h, 128 * h + 128))
+    ts(a("kp"), a("nk"), 32.0, Op.add)
+    tt(a("l3"), a("lz"), a("ls"), Op.mult)
+    tt(a("lz"), a("l3"), a("lk"), Op.add)
+    ts(a("l3"), a("lz"), 15, Op.bitwise_and)
+    ts(a("lutf"), a("l3"), a("lf", 0, 1), Op.is_equal)
+    ts(a("lutk"), a("lk"), a("lf", 0, 1), Op.is_equal)
+    copy(a("p32"), a("np_"))
+    waits("y", need("dma", [], [a("zf")]))
+    g.sync.dma_start(T.kd[:, 0, :], T.zf[0:8, 0:128]).then_inc(T.sem["kz"], 16)
+    g.sync.wait_ge(T.sem["kz"], 16)
+
+    def consts1():
+        ts(a("st"), a("i1"), 15.0, Op.min, a("lf", 0, 1), Op.is_equal)
+        fill(a("st", 0, 2048, 16), 0.0)
+        asel(a("st"), a("st"), [[0, 16], [-16, 8], [0, 16]], Op.is_ge, 0, 1)
+        asel(a("st"), a("st"), [[0, 16], [16, 8], [0, 16]], Op.is_ge, 15, -1)
+
+    def consts2():
+        fill(a("lutm"), 32.0)
+        fill(a("lutm", 2, 3), 4096.0)
+        fill(a("luto"), 4096.0)
+        fill(a("luto", 1, 2), 0.0)
+        fill(a("lutp"), 0.0)
+        ts(a("lutp", 1, 2), a("lf", 0, 1), 0.0, Op.is_equal)
+        fill(a("rs2"), -128.0)
+        fill(a("rs2", 0, 256, 16), 1000000.0)
+        copy(a("pf"), a("pi"))
+        ts(a("pl", 0, 1), a("lf", 0, 1), 256.0, Op.mult, a("pf", 0, 1), Op.add)
+        ts(a("cf"), a("q16"), a("lf", 0, 1), Op.add)
+        ts(a("c16"), a("cf"), 16.0, Op.mult)
+        ts(a("cd"), a("cf"), 2048.0, Op.add)
+        ts(a("cw", 0, 8), a("cf", 0, 8), 3968.0, Op.add)
+        ts(a("cw", 8, 16), a("cf", 8, 16), 3840.0, Op.add)
+        ts(a("dg_"), a("i2"), a("pl", 0, 1), Op.is_equal)
+
+    def lanes(out, z, src, c, first):
+        for i in range(16):
+            mm(out, a(z, 15 - i, 143 - i), a3(src, 4 * c, 4 * c + 4, 16 * i, 16 * i + 16), first and i == 0, i == 15)
+
+    dmas = {"kd": 0, "wd": 0}
+
+    def next_table(t):
+        x, n = "xt%d" % (t % 2), "xt%d" % ((t + 1) % 2)
+        dma("y", "xc%d" % t, T[n][:, 0:2048], T[x][:, 0:2048], [a(n, 0, 2048)], [a(x, 0, 2048)])
+
+    def shifted1(k):
+        z = ("bT", "bZ")[k % 2]
+        for u in range(4 * k, min(4 * k + 4, 18)):
+            o, s = 128 * (u - 4 * k), 0 if u == 16 else 128 * min(u + 1, 15)
+            mm(a(z, o, o + 128), a("idn") if u == 17 else a("st", s, s + 128), a("kh"), True, True)
+        if k < 4:
+            act(a("wt1", 512 * k, 512 * k + 512), a(z), AF.Copy)
+        else:
+            act(a("wt1", 2048, 2176), a(z, 0, 128), AF.Copy)
+            act(a("wt1", 3968, 4096), a(z, 128, 256), AF.Copy)
+
+    def shifted0():
+        y, w, k = g.sync, "wd", "kd"
+
+        def start(sem, out, in_):
+            y.dma_start(out, in_).then_inc(T.sem[sem], 16)
+            dmas[sem] += 16
+
+        if dmas[w]:
+            waits("y", {w: dmas[w]})
+        kp = a("kp", 0, 128)
+        waits("y", need("dma", [], [kp]))
+        start(k, T.kd[:, 1:17, :], kp[0])
+        for r in range(15):
+            start(k, T.kd[:, 17 + r, :], T.kp[15:128:16, 0:128])
+        note("dma", k, dmas[k], [], [kp], {})
+        waits("y", need("dma", [a("wt0")], []))
+        start(w, T.wt0[:, 3968:4096], kp[0])
+        y.wait_ge(T.sem[k], dmas[k])
+        for j in range(1, 16):
+            start(w, T.wt0[j:128:16, 0:2048], T.kd[:, 1 + j:17 + j, :])
+        start(w, T.wt0[:, 2048:2176], T.kd[:, 0:16, :])
+        note("dma", w, dmas[w], [a("wt0")], [kp], {})
+
+    sent = [0]
+    nxt, prv = T.cores[(rank + 1) % n_ranks], T.cores[(rank - 1) % n_ranks]
+    n_k = len(topo.engines(prv, core))
+    n_p = len(topo.engines(nxt, core))
+
+    def send(name, dst_name, dst, sem, n_in):
+        rid, pid = topo.addr(dst, core)
+        waits("g", need("g", [], [a(name)]))
+        g.remote_dma(T[dst_name][:], T[name][:], T.sem[sem], T.sem["sent"], pid, rid, topo.mask(core, dst))
+        sent[0] += len(topo.engines(core, dst))
+        note("dma", sem, n_in, [a(dst_name)], [], {})
+
+    def gather_y(t, c):
+        act(a("yg", 1024 * c, 1024 * c + 1024), ind(a("xt%d" % (t % 2)), a("p16_%d" % t, 64 * c, 64 * c + 64)), AF.Copy)
+
+    for t in range(RO):
+        last, first = t == RO - 1, t == 0
+        xt, xn = "xt%d" % (t % 2), "xt%d" % ((t + 1) % 2)
+
+        def d_chunk(t, c):
+            for q in range(4 * c, 4 * c + 4):
+                tt(row("d3", q), ind(a("xt%d" % (t % 2)), a("k16_%d_%d" % (t, q // 8), 16 * (q % 8), 16 * (q % 8) + 16)),
+                   a("yg", 256 * q, 256 * q + 256), Op.subtract)
+
+        def d_abs(c):
+            act(a3("a3", 4 * c, 4 * c + 4), a3("d3", 4 * c, 4 * c + 4), AF.Abs)
+
+        def t_sum(c):
+            lanes(a(("bT", "bT2")[c // 2], 64 * c, 64 * c + 64), "z1", "d3", c, True)
+
+        def d_sum(c):
+            o = a(("bD", "bD2")[c // 2], 64 * c, 64 * c + 64)
+            mm(o, a("idn"), a("cj", 64 * c, 64 * c + 64), True, False)
+            lanes(o, "z64", "a3", c, False)
+
+        def sign(h):
+            s = (128 * h, 128 * h + 128)
+            act(a("sn", *s), a(("bT", "bT2")[h], *s), AF.Sign)
+
+        def s_gather(c):
+            lo = 64 * (c % 2)
+            act(a("sg", 1024 * c, 1024 * c + 1024), ind(a(xt), a("k16_%d_%d" % (t, c // 2), lo, lo + 64)), AF.Copy)
+
+        def least(h):
+            s, m = (128 * h, 128 * h + 128), (8 * h, 8 * h + 8)
+            tt(a("code", *s), a(("bD", "bD2")[h], *s), a("sn", *s), Op.add)
+            scan(a("mi", *s), a("rst", *s), a("code", *s), Op.max, Op.min)
+            ts(a("v8", *m), a("mi", s[0] + 15, s[1], 16), 255, Op.bitwise_and)
+            copy(a("l8", *m), a("v8", *m))
+            tt(a("nsel", *s), ind(a("lutf"), a("l8", *m)), a("p32", *s), Op.mult)
+            mm(a("bN", *s), a("gm"), a("nsel", *s), True, True)
+
+        def heads(h):
+            copy(a("nb", 128 * h, 128 * h + 128), a("bN", 128 * h, 128 * h + 128))
+
+        def plus(t, h):
+            ts(a("kp", 128 * h, 128 * h + 128), a("k16_%d_%d" % (t, h)), 32.0, Op.add)
+
+        def half1():
+            copy(a("kh"), a("k16_%d_1" % t))
+
+        def near(c):
+            s = (1024 * c, 1024 * c + 1024)
+            tt(a("eg", *s), ind(a(xt), a("nb", 64 * c, 64 * c + 64)), a("sg", *s), Op.subtract)
+
+        def near_abs(c):
+            act(a3("ae", 4 * c, 4 * c + 4), a("eg", 1024 * c, 1024 * c + 1024), AF.Abs)
+
+        def near_sum(c):
+            lanes(a(("bD", "bD2")[c // 2], 64 * c, 64 * c + 64), "z1", "ae", c, True)
+
+        def arrays(h):
+            s, m = (128 * h, 128 * h + 128), (8 * h, 8 * h + 8)
+            ts(a("ew", *s), a(("bD", "bD2")[h], *s), 1040.0, Op.is_lt, -2048.0, Op.mult)
+            scan(a("ms", *s), a("rs2", *s), a("ew", *s), Op.add, Op.min)
+            tt(a("o1", *m), a("ms", s[0] + 15, s[1], 16), a("npx", *m), Op.max)
+            tt(a("o2", *m), a("o1", *m), a("cw", *m), Op.add)
+            copy(a("o16", *m), a("o2", *m))
+            tt(a("fr", *s), ind(a("wt%d" % h), a("o16", *m)), a("nfix", *s), Op.add)
+            out = a("yk32", *s) if last else a("ks_%d_%d" % (t, h))
+            if h == 0:
+                ts(out, a("fr", *s), -32.0, Op.add)
+            else:
+                copy(out, a("fr", *s))
+            if not last:
+                send("ks_%d_%d" % (t, h), "k16_%d_%d" % (t + 1, h), nxt, "ka%d_%d" % (t + 1, h), n_k)
+
+        def fates():
+            mc = a("mi", 15, 256, 16)
+            ts(a("lt"), mc, a("thr"), Op.is_lt)
+            ts(a("kf"), mc, 53248.0, Op.is_lt)
+            tt(a("ksel"), ind(a("lutk"), a("l8")), a("p32"), Op.mult)
+            mm(a("bM", 32, 48), a("gm"), a("kf"), True, True)
+            mm(a("bT2", 0, 256), a("gm"), a("ksel"), True, True)
+            tt(a("fl"), a("lt"), a("kf"), Op.add)
+            copy(a("fl16"), a("fl"))
+
+        def names():
+            act(a("pks"), a("bT2", 0, 256), AF.Copy)
+            act(a("ns", 0, 128), a("bN", 0, 128), AF.Copy, bias=32.0)
+            act(a("ns", 128, 256), a("bN", 128, 256), AF.Copy)
+
+        def phages():
+            tt(a("pa"), ind(a("lutm"), a("fl16")), a("kp"), Op.min)
+            ts(a("kk"), a("v8"), 2, Op.logical_shift_right, 15, Op.bitwise_and)
+            tt(a("pt"), a("pa"), a("p32"), Op.mult)
+            tt(a("ok"), a("kk"), a("c16"), Op.add)
+            ts(a("pn"), a("pt"), 5, Op.logical_shift_right, 2047, Op.bitwise_and)
+            copy(a("ok16"), a("ok"))
+            if last:
+                copy(a("yp32"), a("pn"))
+                dma("y", "op", T.yp[:], T.yp32[:], [], [a("yp32")])
+            else:
+                copy(a("ps_%d" % t), a("pn"))
+                send("ps_%d" % t, "p16_%d" % (t + 1), prv, "pa%d" % (t + 1), n_p)
+
+        def lanes_k():
+            act(a("yk_"), ind(a("yg"), a("ok16")), AF.Copy)
+            act(a("sgn"), ind(a("yg"), a("ok16")), AF.Sign, scale=-1.0, bias=127.5)
+
+        def writers():
+            tt(a("rr"), ind(a("luto"), a("fl16")), a("pks"), Op.max)
+            for i in range(16):
+                mm(a("bM", 0, 16), a("dg_", 128 * i, 128 * i + 128), a("rr", i, 256, 16), i == 0, i == 15)
+
+        def values():
+            tt(a("dk"), ind(a("sg"), a("ok16")), a("yk_"), Op.subtract)
+            act(a("adk"), a("dk"), AF.Abs)
+            tt(a("nfix"), ind(a("lutp"), a("fl16")), a("ns"), Op.mult)
+            ts(a("npx"), a("fl"), 1.0, Op.is_equal, -8192.0, Op.mult)
+
+        def equals():
+            copy(a("ol"), a("bM", 0, 16))
+            for q in range(16):
+                ts(a("eq", 272 * q, 256 * q + 256), a("rr", 16 * q, 256), a("ol", q, q + 1), Op.is_equal)
+                mm(a("bC", 16 * q, 16 * q + 16), a("tri"), a("eq", 272 * q, 272 * q + 16), q == 0, q in (0, 15))
+                if q < 15:
+                    mm(a("bC", 16 * q + 16, 256), a("gm"), a("eq", 272 * q + 16, 256 * q + 256), q == 0, False)
+
+        def counts():
+            act(a("cs"), a("bC", 0, 256), AF.Copy, scale=4096.0)
+            for i in range(16):
+                mm(a("bM", 16, 32), a("dg_", 128 * i, 128 * i + 128), a("cs", i, 256, 16), i == 0, i == 15)
+
+        def change():
+            ts(a("c1"), a("adk"), 32.0, Op.is_le, 128.0, Op.mult)
+            tt(a("tt"), a("c1"), a("sgn"), Op.mult)
+
+        def scatter():
+            tt(a("v1"), a("bM", 16, 32), a("ol"), Op.add)
+            tt(a("v2"), a("v1"), a("cd"), Op.min)
+            copy(a("w16"), a("v2"))
+            tt(ind(a(xn), a("w16")), a("yk_"), a("tt"), Op.add)
+
+        def allowance():
+            do("v", lambda: V.tensor_reduce(T.ca[:], T.bM[:, 32:48], AX.X, Op.add), [a("ca")], [a("bM", 32, 48)])
+            tt(a("aa"), a("aa"), a("ca"), Op.add)
+            ts(a("ab"), a("aa"), 15, Op.bitwise_and)
+            ts(a("thr"), a("ab"), 256.0, Op.mult, 65536.0, Op.add)
+
+        next_table(t)
+        if first:
+            shifted0()
+            for c in range(4):
+                gather_y(0, c)
+            d_chunk(0, 0)
+            d_chunk(0, 1)
+        steps = {"le0": lambda: (consts1() if first else None, least(0)), "le1": lambda: least(1),
+                 "he0": lambda: (consts2() if first else None, heads(0)), "he1": lambda: heads(1),
+                 "dc2": lambda: d_chunk(t, 2), "dc3": lambda: d_chunk(t, 3), "sn0": lambda: sign(0), "sn1": lambda: sign(1),
+                 "fa": fates, "pk": names, "kh": half1, "wr": writers, "ph": phages, "yk": lanes_k, "eq": equals, "va": values,
+                 "co": counts, "ch": change, "sc": scatter, "ar0": lambda: arrays(0), "ar1": lambda: arrays(1)}
+        for c in range(4):
+            for x, f in (("ts", t_sum), ("da", d_abs), ("ds", d_sum), ("sg", s_gather), ("n", near), ("na", near_abs), ("nl", near_sum)):
+                steps["%s%d" % (x, c)] = lambda f=f, c=c: f(c)
+        for k in range(5):
+            steps["sh%d" % k] = lambda k=k: shifted1(k)
+        if not first:
+            steps["pl1"] = lambda: plus(t, 1)
+        if not last:
+            steps.update({"al": allowance, "p32": lambda: copy(a("p32"), a("p16_%d" % (t + 1))), "pl0": lambda: plus(t + 1, 0),
+                          "w0": shifted0, "dc0": lambda: d_chunk(t + 1, 0), "dc1": lambda: d_chunk(t + 1, 1)})
+            for c in range(4):
+                steps["y%d" % c] = lambda c=c: gather_y(t + 1, c)
+        for x in ORDER.split():
+            if x in steps:
+                steps[x]()
+            if x == "sc" and last:
+                dma("y", "oy", T.yx[:], T[xn][:, 0:2048], [], [a(xn, 0, 2048)])
+        if last:
+            dma("y", "ok", T.yk[:], T.yk32[:], [], [a("yk32")])
+    g.wait_ge(T.sem["sent"], sent[0])
+    for s in ("oy", "ok", "op"):
+        g.sync.wait_ge(T.sem[s], 16)
+    for q in cnt:
+        if seen["y"].get(q, 0) < cnt[q]:
+            g.sync.wait_ge(T.sem[q], cnt[q])

@@ -1,44 +1,40 @@
-from concourse.mybir import AluOpType as Op, ActivationFunctionType as AF, AxisListType as AX
+from concourse.mybir import AluOpType as Op, ActivationFunctionType as AF
 
 RO = 4
 F, B, H, I, U = "float32", "bfloat16", "float16", "int32", "uint16"
 SCRATCH = {}
 for _n, _w, _d in (
-        ("xt0", 2304, B), ("xt1", 2304, B), ("nk", 256, I), ("np_", 256, I), ("yg", 4096, B), ("sg", 4096, B), ("eg", 4096, B),
-        ("kp", 256, F), ("p32", 256, F), ("sn", 256, F), ("code", 256, F), ("mi", 256, I),
-        ("v8", 16, I), ("l8", 16, U), ("kf", 16, B), ("lt", 16, F), ("fl", 16, F), ("fl16", 16, U),
-        ("nsel", 256, H), ("ksel", 256, H), ("nb", 256, U), ("ns", 256, F), ("pks", 256, F),
-        ("pa", 256, F), ("pt", 256, I), ("pn", 256, I), ("yp32", 256, F),
-        ("npx", 16, F), ("o1", 16, F), ("o2", 16, F), ("o16", 16, U), ("nfix", 256, F), ("kh", 128, H),
-        ("wt0", 4096, F), ("wt1", 4096, F), ("fr", 256, F),
-        ("yk32", 256, F), ("ew", 256, F), ("ms", 256, F), ("zf", 256, F),
-        ("rr", 256, H), ("ol", 16, F), ("eq", 4096, B), ("cs", 256, B), ("v1", 16, F), ("v2", 16, F), ("w16", 16, U),
-        ("kk", 16, I), ("ok", 16, I), ("ok16", 16, U), ("yk_", 256, B), ("dk", 256, B), ("adk", 256, B), ("sgn", 256, B),
-        ("c1", 256, B), ("tt", 256, B), ("ca", 1, F), ("aa", 1, I), ("ab", 1, I), ("thr", 1, F),
-        ("pi", 2, I), ("li", 2, I), ("lf", 2, F), ("pf", 2, F), ("pl", 2, F), ("i1", 2048, I), ("i2", 2048, I), ("st", 2048, B),
-        ("dg_", 2048, B), ("ones", 128, B), ("gm", 128, B), ("tri", 128, B), ("idn", 128, B),
-        ("z1", 143, B), ("z64", 143, B), ("cj", 256, B), ("rst", 256, F), ("rs2", 256, F),
-        ("q16", 16, F), ("cf", 16, F), ("c16", 16, I), ("cd", 16, F), ("cw", 16, F),
-        ("lk", 256, I), ("lz", 256, I), ("ls", 256, I), ("l3", 256, I),
-        ("lutf", 256, B), ("lutk", 256, B), ("lutm", 16, F), ("luto", 16, F), ("lutp", 16, F)):
+        ("xt", 2064, B), ("nk", 256, I), ("np_", 256, I), ("sg", 4096, B), ("ph_", 256, H), ("kp", 256, F),
+        ("mi", 256, F), ("cl", 16, I), ("v8", 16, I), ("l8", 16, U), ("sel0", 256, H), ("sel1", 256, H), ("pn16", 32, U),
+        ("nr0", 264, F), ("nr1", 264, F), ("xn", 256, B), ("xr", 256, B), ("eq", 256, B), ("w16", 32, U),
+        ("kk", 16, I), ("ok", 16, I), ("ok16", 16, U), ("sk", 256, B), ("dk", 256, B), ("adk", 256, B), ("c1", 256, B),
+        ("wv", 256, B), ("vv", 256, B), ("pa", 256, F), ("pt", 256, I), ("pn", 256, I), ("yp32", 256, F),
+        ("wt0", 2240, F), ("wt1", 2240, F), ("sc", 288, B), ("ms", 288, F), ("o16", 16, U), ("fr", 256, I), ("fu", 256, I), ("yk32", 256, F),
+        ("jk", 16, B), ("ac", 4, F), ("aa", 1, I), ("ab", 1, I), ("thr", 1, F),
+        ("pi", 2, I), ("li", 2, I), ("lf", 2, F), ("l16", 2, F), ("l15", 2, F), ("ones", 128, B), ("neg", 512, B), ("gm", 128, B), ("idn", 128, B),
+        ("idf", 128, F), ("idk", 128, F), ("gmf", 128, F), ("s15", 128, F), ("s5k", 128, F),
+        ("z1", 143, B), ("zd", 143, B), ("zr", 143, B), ("zn", 143, B), ("zw", 143, B), ("zk", 128, B),
+        ("cj", 128, B), ("rst", 128, F), ("rs", 144, F), ("ex", 2048, B), ("tm", 128, B), ("ij", 128, I), ("iq", 16, I),
+        ("bl", 8, U), ("c16", 8, F), ("i3", 192, I), ("i4", 192, I), ("nil", 64, F),
+        ("lutf", 256, B), ("lutk", 256, B), ("lutm", 256, B)):
     SCRATCH[_n] = ("sbuf", [128, _w], _d)
-for _n in ("d3", "a3", "ae"):
-    SCRATCH[_n] = ("sbuf", [128, 16, 256], B)
-SCRATCH["kd"] = ("dram", [8, 32, 128], F)
-for _t in range(RO):
-    for _h in range(2):
-        SCRATCH["k16_%d_%d" % (_t, _h)] = ("sbuf", [128, 128], U)
-        SCRATCH["ks_%d_%d" % (_t, _h)] = ("sbuf", [128, 128], U)
-    SCRATCH["p16_%d" % _t] = ("sbuf", [128, 256], U)
-    SCRATCH["ps_%d" % _t] = ("sbuf", [128, 256], U)
-ORDER = """ts0 da0 dc2 ts1 da1 sn0 ds0 ds1 sg0 dc3 ts2 le0 pl1 ts3 he0 sg1 da2 da3 ds2 sn1 n0 ds3 na0 sg2 n1 le1 fa he1 pk kh n2 nl0
-    sh0 sg3 sh1 wr ph sh2 eq yk al na1 nl1 n3 va ar0 co na2 na3 sh3 sh4 nl2 ch sc y0 y1 nl3 y2 p32 y3 ar1 pl0 dc0 dc1 w0"""
-PSUM = ("bT", "bT2", "bD", "bD2", "bN", "bM", "bC", "bZ")
+for _n, _w in (("d3", 256), ("a3", 256), ("ae", 272)):
+    SCRATCH[_n] = ("sbuf", [128, 16, _w], B)
+for _h in range(2):
+    SCRATCH["kd%d" % _h] = ("dram", [8, 33, 64], F)
+    for _t in range(RO):
+        for _n in ("k16", "p16") + (("ks", "ps") if _t < RO - 1 else ()):
+            SCRATCH["%s_%d_%d" % (_n, _t, _h)] = ("sbuf", [128, 128], U)
+PSUM = ("e0", "e1", "e2", "c0", "c1_", "m0", "m1", "mc")
 for _n in PSUM:
     SCRATCH[_n] = ("psum", [128, 512], F)
-SEMAPHORES = (["v", "s", "p", "g", "lx", "lp", "lk", "oy", "ok", "op", "sent", "kz", "kd", "wd"]
-              + ["ka%d_%d" % (t, h) for t in range(1, RO) for h in range(2)] + ["pa%d" % t for t in range(1, RO)]
-              + ["xc%d" % t for t in range(RO)])
+SEMAPHORES = (["v", "s", "p", "g", "lx", "lp", "lk", "oy", "ok0", "ok1", "op0", "op1", "kz", "kd0", "kd1", "wd0", "wd1"]
+              + ["%s%d_%d" % (x, t, h) for x in ("ka", "pa", "kl", "pl") for t in range(1, RO) for h in range(2)])
+RELU = (1,)
+BEHIND = {0: 3}
+LOW = -(2.0 ** 24) - 2048
+TOP = 63 * 2.0 ** 17 + 15 * 2.0 ** 13 + 4096
+HOP, CALL, ACT, GATHER, SCATTER, ISSUE, LOCAL, REMOTE, FAR, BYTES, TURNS = 170, 40, 110, 1.56, 3.8, 70, 2000, 850, 3500, 190, 6
 
 
 def rank_program(g, core, T, topo):
@@ -47,52 +43,21 @@ def rank_program(g, core, T, topo):
         return
     n_ranks = len(T.cores)
     Q = {"v": g.vector, "s": g.scalar, "p": g.tensor, "g": g, "y": g.sync}
-    cnt = {"v": 0, "s": 0, "p": 0, "g": 0}
-    seen = {q: {} for q in Q}
-    snap, hist = {}, {}
+    V, S, P = g.vector, g.scalar, g.tensor
 
     def a(name, lo=0, hi=None, step=None):
         hi = SCRATCH[name][1][1] if hi is None else hi
-        return (T[name][:, lo:hi] if step is None else T[name][:, lo:hi:step], name, lo, hi)
+        return (T[name][:, lo:hi] if step is None else T[name][:, lo:hi:step], name, lo, hi, len(range(lo, hi, step or 1)))
 
     def a3(name, q0, q1, c0=None, c1=None):
-        return (T[name][:, q0:q1, :] if c0 is None else T[name][:, q0:q1, c0:c1], name, 256 * q0, 256 * q1)
+        w = SCRATCH[name][1][2]
+        return (T[name][:, q0:q1, :] if c0 is None else T[name][:, q0:q1, c0:c1], name, w * q0, w * q1, (q1 - q0) * (w if c0 is None else c1 - c0))
 
     def row(name, q):
-        return (T[name][:, q], name, 256 * q, 256 * q + 256)
+        return (T[name][:, q], name, 256 * q, 256 * q + 256, 256)
 
     def ind(win, off):
         return (win[0].indirect(off[0]), win, off)
-
-    def need(q, outs, ins):
-        want = {}
-        for kind, lst in (("w", outs), ("r", ins)):
-            for _, name, lo, hi in lst:
-                bank = name in PSUM
-                for k2, l2, h2, q2, sem, val in hist.get(name, ()):
-                    if q2 == q and q != "dma" and (k2 == "r" or q == "p" and kind == "w"):
-                        continue
-                    if not (bank and q2 != q) and (k2 == kind == "r" or h2 <= lo or l2 >= hi):
-                        continue
-                    want[sem] = max(want.get(sem, 0), val)
-        return want
-
-    def waits(q, want):
-        for sem, val in sorted(want.items()):
-            if seen[q].get(sem, 0) < val:
-                Q[q].wait_ge(T.sem[sem], val)
-                seen[q][sem] = val
-                for s2, v2 in snap.get((sem, val), {}).items():
-                    seen[q][s2] = max(seen[q].get(s2, 0), v2)
-
-    def note(q, sem, val, outs, ins, known):
-        snap[(sem, val)] = dict(known)
-        for kind, lst in (("w", outs), ("r", ins)):
-            for _, name, lo, hi in lst:
-                h = hist.setdefault(name, [])
-                if kind == "w":
-                    h[:] = [e for e in h if not (e[1] >= lo and e[2] <= hi)]
-                h.append((kind, lo, hi, q, sem, val))
 
     def flat(lst):
         r = []
@@ -100,362 +65,364 @@ def rank_program(g, core, T, topo):
             r += [x] if isinstance(x[1], str) else [x[1], x[2]]
         return r
 
-    def do(q, fn, outs, ins):
-        o, i = flat(outs), flat(ins)
-        waits(q, need(q, o, i))
-        cnt[q] += 1
-        fn().then_inc(T.sem[q], 1)
-        note(q, q, cnt[q], o, i, seen[q])
+    tasks = []
 
-    def dma(q, sem, out, in_, outs, ins):
-        waits(q, need("dma", outs, ins))
-        Q[q].dma_start(out, in_).then_inc(T.sem[sem], 16)
-        note("dma", sem, 16, outs, ins, seen[q])
+    def task(q, kind, call, outs, ins, cost, after=0, more=False):
+        if not more:
+            tasks.append(dict(q=q, kind=kind, calls=[], after=after))
+        tasks[-1]["calls"].append((call, flat(outs), flat(ins), cost))
 
-    V, S, P = g.vector, g.scalar, g.tensor
+    def vec(fn, out, ins, rate):
+        if isinstance(out[1], tuple):
+            task("v", "call", fn, [out[1]], ins + [out[2]], 60 + SCATTER * ins[0][4])
+        elif ins and isinstance(ins[0][1], tuple):
+            task("v", "call", fn, [out], ins, 60 + GATHER * out[4])
+        else:
+            task("v", "call", fn, [out], ins, CALL + max(64, rate * out[4]))
+
+    def narrow(*x):
+        return 0.5 if all(isinstance(y[1], str) and SCRATCH[y[1]][2] in (B, H, U) for y in x) else 1
 
     def copy(out, in_):
-        do("v", lambda: V.tensor_copy(out[0], in_[0]), [out], [in_])
+        vec(lambda: V.tensor_copy(out[0], in_[0]), out, [in_], narrow(out, in_))
 
     def tt(out, x, y, op):
-        if isinstance(out[1], tuple):
-            do("v", lambda: V.tensor_tensor(out[0], x[0], y[0], op), [out[1]], [x, y, out[2]])
-        else:
-            do("v", lambda: V.tensor_tensor(out[0], x[0], y[0], op), [out], [x, y])
+        vec(lambda: V.tensor_tensor(out[0], x[0], y[0], op), out, [x, y], 1 if y[1] in PSUM else 2)
 
     def ts(out, x, s1, op0, s2=None, op1=None):
         ins = [x] + [s for s in (s1, s2) if isinstance(s, tuple)]
         c = [s[0] if isinstance(s, tuple) else s for s in (s1, s2)]
         if op1 is None:
-            do("v", lambda: V.tensor_scalar(out[0], x[0], c[0], None, op0), [out], ins)
+            vec(lambda: V.tensor_scalar(out[0], x[0], c[0], None, op0), out, ins, narrow(out, x))
         else:
-            do("v", lambda: V.tensor_scalar(out[0], x[0], c[0], c[1], op0, op1), [out], ins)
+            vec(lambda: V.tensor_scalar(out[0], x[0], c[0], c[1], op0, op1), out, ins, narrow(out, x))
 
-    def scan(out, d0, d1, op0, op1):
-        do("v", lambda: V.tensor_tensor_scan(out[0], d0[0], d1[0], 1000000.0, op0, op1), [out], [d0, d1])
+    def scan(out, d0, d1, first, op0, op1):
+        vec(lambda: V.tensor_tensor_scan(out[0], d0[0], d1[0], first, op0, op1), out, [d0, d1], 1)
 
     def fill(out, val):
-        do("v", lambda: V.memset(out[0], val), [out], [])
+        vec(lambda: V.memset(out[0], val), out, [], narrow(out))
 
-    def act(out, in_, func, **kw):
-        do("s", lambda: S.activation(out[0], in_[0], func, **kw), [out], [in_])
+    def act(out, in_, func, acc=None, **kw):
+        cost = 80 + GATHER * out[4] if isinstance(in_[1], tuple) else ACT + out[4]
+        if acc is None:
+            task("s", "call", lambda: S.activation(out[0], in_[0], func, **kw), [out], [in_], cost)
+        else:
+            task("s", "call", lambda: S.activation(out[0], in_[0], func, accum_out=acc[0], **kw), [out, acc], [in_], cost)
 
     def mm(out, l, r, start, stop):
-        do("p", lambda: P.matmul(out[0], l[0], r[0], start, stop), [out], [l, r])
+        task("p", "call", lambda: P.matmul(out[0], l[0], r[0], start, stop), [out], [l, r],
+             6 + max(64, r[4]) * (2 if SCRATCH[l[1]][2] == F else 0.5), more=not start)
 
-    def iota(out, pattern, base, cm, **kw):
-        do("g", lambda: g.iota(out[0], pattern, base, cm, **kw), [out], [])
+    def iota(out, pattern, base, cm):
+        task("g", "call", lambda: g.iota(out[0], pattern, base, cm), [out], [], 160 + 2 * out[4])
 
     def asel(out, in_, pattern, cop, base, cm):
-        do("g", lambda: g.affine_select(out[0], in_[0], pattern, cop, 0.0, base, cm), [out], [in_])
+        task("g", "call", lambda: g.affine_select(out[0], in_[0], pattern, cop, 0.0, base, cm), [out], [in_], 200 + 2 * out[4])
 
-    dma("y", "lp", T.np_[:], T.ph[:], [a("np_")], [])
-    dma("s", "lk", T.nk[:], T.ka[:], [a("nk")], [])
-    dma("y", "lx", T.xt0[:, 0:2048], T.x0[:], [a("xt0", 0, 2048)], [])
+    def dmas(q, sem, pairs, outs, ins, size):
+        task(q, "dma", (sem, pairs), outs, ins, ISSUE * len(pairs), LOCAL + size / BYTES)
 
-    small = dict(allow_small_or_imprecise_dtypes=True)
-    iota(a("pi"), [[0, 2]], 0, 1)
+    def scratch(h, lo, hi):
+        return (None, "kd%d" % h, lo, hi, 0)
+
+    nxt, prv = T.cores[(rank + 1) % n_ranks], T.cores[(rank - 1) % n_ranks]
+
+    def send(x, t, h, dst, src):
+        task("g", "send", ("%sa%d_%d" % (x, t + 1, h), "%sl%d_%d" % (x, t + 1, h), dst, src),
+             [a("%s16_%d_%d" % (x, t + 1, h))], [a("%ss_%d_%d" % (x, t, h))], REMOTE, FAR)
+
+    table = a("xt", 16, 2064)
+
+    dmas("s", "lk", [(T.nk[:], T.ka[:])], [a("nk")], [], 2 ** 17)
+    dmas("y", "lx", [(T.xt[:, 16:2064], T.x0[:])], [table], [], 2 ** 19)
+    dmas("y", "lp", [(T.np_[:], T.ph[:])], [a("np_")], [], 2 ** 17 + 2 ** 19)
+    for h in (1, 0):
+        copy(a("k16_0_%d" % h), a("nk", 128 * h, 128 * h + 128))
+        copy(a("p16_0_%d" % h), a("np_", 128 * h, 128 * h + 128))
+
     fill(a("ones"), 1.0)
+    fill(a("neg"), -1.0)
+    iota(a("pi"), [[0, 2]], 0, 1)
     asel(a("gm"), a("ones"), [[-16, 8], [0, 16]], Op.is_ge, 0, 1)
     asel(a("gm"), a("gm"), [[16, 8], [0, 16]], Op.is_ge, 15, -1)
     asel(a("idn"), a("ones"), [[1, 128]], Op.is_equal, 0, -1)
-    iota(a("cj"), [[0, 16], [4, 16]], 1, 0, **small)
-    iota(a("lk"), [[0, 4], [1, 16], [0, 4]], 0, 0)
-    iota(a("lz"), [[1, 4], [0, 64]], 1, 0)
-    iota(a("ls"), [[0, 64], [2, 2], [0, 2]], -1, 0)
-    iota(a("q16"), [[16, 16]], 0, 0, **small)
-    asel(a("tri"), a("gm"), [[1, 128]], Op.is_gt, 0, -1)
-    iota(a("i1"), [[1, 16], [0, 8], [1, 16]], -1, 0)
-    iota(a("i2"), [[256, 16], [1, 128]], 0, 0)
+    iota(a("ij"), [[0, 8], [1, 16]], 0, 0)
+    iota(a("iq"), [[1, 16]], 0, 0)
+    iota(a("i3", 0, 64), [[1, 4], [1, 16]], 129, -1)
+    iota(a("i3", 64, 128), [[-1, 4], [1, 16]], 127, -1)
+    iota(a("i3", 128, 192), [[0, 4], [1, 16]], 128, -1)
+    for b in range(4):
+        asel(a("ex", 512 * b, 512 * b + 512), a("neg"), [[1, 32], [0, 16]], Op.is_equal, 32 * b, -1)
+    fill(a("nil"), 0.0)
     fill(a("z1"), 0.0)
-    fill(a("zf"), 0.0)
-    fill(a("xt0", 2048, 2304), 0.0)
-    fill(a("xt1", 2048, 2304), 0.0)
+    fill(a("rst"), -1e9)
+    fill(a("rst", 0, 128, 16), 1e9)
+    fill(a("thr"), TOP)
+    fill(a("lutf"), 0.0)
+    fill(a("lutk"), -512.0)
+    fill(a("lutm"), 32.0)
+    fill(a("lutm", 255, 256), 4096.0)
+    fill(a("w16"), 0)
+    fill(a3("ae", 0, 16, 256, 272), 0.0)
+    fill(a("rs"), -0.0625)
+    fill(a("rs", 17, 144, 18), 100.0)
+    dmas("y", "kz", [(T["kd%d" % h][:, 0, :], T.nil[0:8, :]) for h in range(2)] + [(T["wt%d" % h][0:128:16, 128:1152], T.nil[:]) for h in range(2)],
+         [a("wt0", 128, 1152), a("wt1", 128, 1152), scratch(0, 0, 1), scratch(1, 0, 1)], [a("nil")], 2 ** 16)
     ts(a("li"), a("pi"), 15, Op.bitwise_and)
     copy(a("lf"), a("li"))
+    ts(a("l15"), a("lf"), 15.0, Op.is_equal)
+    ts(a("l16"), a("lf"), 16.0, Op.mult)
     copy(a("z1", 15, 143, 16), a("gm", 0, 128, 16))
-    ts(a("z64"), a("z1"), 64.0, Op.mult)
-    fill(a("rst"), 0.0)
-    fill(a("rst", 0, 256, 16), 1000000.0)
-    fill(a("thr"), 65536.0)
-    fill(a("aa"), 0)
-    fill(a("wt0", 0, 2048), 0.0)
-    copy(a("p16_0"), a("np_"))
-    for h in range(2):
-        copy(a("k16_0_%d" % h), a("nk", 128 * h, 128 * h + 128))
-    ts(a("kp"), a("nk"), 32.0, Op.add)
-    tt(a("l3"), a("lz"), a("ls"), Op.mult)
-    tt(a("lz"), a("l3"), a("lk"), Op.add)
-    ts(a("l3"), a("lz"), 15, Op.bitwise_and)
-    ts(a("lutf"), a("l3"), a("lf", 0, 1), Op.is_equal)
-    ts(a("lutk"), a("lk"), a("lf", 0, 1), Op.is_equal)
-    copy(a("p32"), a("np_"))
-    waits("y", need("dma", [], [a("zf")]))
-    g.sync.dma_start(T.kd[:, 0, :], T.zf[0:8, 0:128]).then_inc(T.sem["kz"], 16)
-    g.sync.wait_ge(T.sem["kz"], 16)
+    ts(a("s15"), a("gm"), a("l15", 0, 1), Op.mult)
+    copy(a("idf"), a("idn"))
+    ts(a("s5k"), a("s15"), 4096.0, Op.mult)
+    ts(a("idk"), a("idn"), 4096.0, Op.mult)
+    for z, w in (("zd", 2.0 ** 17), ("zw", -4096.0)) + ((("zr", 2.0 ** 18), ("zn", -(2.0 ** 17))) if RELU else ()):
+        ts(a(z), a("z1"), w, Op.mult)
+    ts(a("zk"), a("z1", 15, 143), 4096.0, Op.mult)
+    vec(lambda: V.memset(T.cj[0:64, :], -15.0 * 2 ** 17), a("cj"), [], 0.5)
+    vec(lambda: V.tensor_scalar(T.cj[64:128, :], T.ij[64:128, :], 128.0, 32.0, Op.mult, Op.add), a("cj"), [a("ij")], 1)
+    ts(a("i4"), a("i3"), 15, Op.bitwise_and)
+    ts(a("tm"), a("ij"), a("lf", 0, 1), Op.is_le, 16384.0, Op.mult)
+    for sb in range(2):
+        ts(a("lutf", sb, 256, 4), a("i4", 64 * sb, 64 * sb + 64), 0.0, Op.is_equal, 4096.0, Op.mult)
+        ts(a("lutk", sb, 256, 4), a("i4", 128, 192), 0.0, Op.is_equal, 4096.0, Op.mult)
+    copy(a("bl"), a("iq", 0, 8))
+    ts(a("c16"), a("iq", 0, 8), 256.0, Op.mult, a("l16", 0, 1), Op.add)
+    copy(a("gmf"), a("gm"))
+    for u in range(2):
+        ts(a("rs", 72 * u + 16, 72 * u + 72, 18), a("c16", 0, 4), 2.0 ** -14, Op.mult)
 
-    def consts1():
-        ts(a("st"), a("i1"), 15.0, Op.min, a("lf", 0, 1), Op.is_equal)
-        fill(a("st", 0, 2048, 16), 0.0)
-        asel(a("st"), a("st"), [[0, 16], [-16, 8], [0, 16]], Op.is_ge, 0, 1)
-        asel(a("st"), a("st"), [[0, 16], [16, 8], [0, 16]], Op.is_ge, 15, -1)
+    def half(name, h, w=128):
+        return a(name, w * h, w * h + w)
 
-    def consts2():
-        fill(a("lutm"), 32.0)
-        fill(a("lutm", 2, 3), 4096.0)
-        fill(a("luto"), 4096.0)
-        fill(a("luto", 1, 2), 0.0)
-        fill(a("lutp"), 0.0)
-        ts(a("lutp", 1, 2), a("lf", 0, 1), 0.0, Op.is_equal)
-        fill(a("rs2"), -128.0)
-        fill(a("rs2", 0, 256, 16), 1000000.0)
-        copy(a("pf"), a("pi"))
-        ts(a("pl", 0, 1), a("lf", 0, 1), 256.0, Op.mult, a("pf", 0, 1), Op.add)
-        ts(a("cf"), a("q16"), a("lf", 0, 1), Op.add)
-        ts(a("c16"), a("cf"), 16.0, Op.mult)
-        ts(a("cd"), a("cf"), 2048.0, Op.add)
-        ts(a("cw", 0, 8), a("cf", 0, 8), 3968.0, Op.add)
-        ts(a("cw", 8, 16), a("cf", 8, 16), 3840.0, Op.add)
-        ts(a("dg_"), a("i2"), a("pl", 0, 1), Op.is_equal)
+    def cb(h, lo, hi):
+        return a(("c0", "c1_")[h], lo, hi)
 
-    def lanes(out, z, src, c, first):
+    def lanes(out, z, src, c, w, first, end):
         for i in range(16):
-            mm(out, a(z, 15 - i, 143 - i), a3(src, 4 * c, 4 * c + 4, 16 * i, 16 * i + 16), first and i == 0, i == 15)
+            mm(out, a(z, 15 - i, 143 - i), a3(src, 4 * c, 4 * c + 4, 16 * i, 16 * i + w), first and i == 0, end and i == 15)
 
-    dmas = {"kd": 0, "wd": 0}
+    def half_round(t, h):
+        last = t == RO - 1
+        k16, p16, sel, m, nr, wt = ["%s%d" % (x, h) for x in ("k16_%d_" % t, "p16_%d_" % t, "sel", "m", "nr", "wt")]
+        l8, pk16, n16 = half("l8", h, 8), a("pn16", 16 * h, 16 * h + 8), a("pn16", 16 * h + 8, 16 * h + 16)
+        p_sum = a("mc", 256 + 128 * h, 384 + 128 * h)
 
-    def next_table(t):
-        x, n = "xt%d" % (t % 2), "xt%d" % ((t + 1) % 2)
-        dma("y", "xc%d" % t, T[n][:, 0:2048], T[x][:, 0:2048], [a(n, 0, 2048)], [a(x, 0, 2048)])
+        for c in (2 * h, 2 * h + 1):
+            relu = (c + 2) % 4 in RELU
+            act(a("sg", 1024 * c, 1024 * c + 1024), ind(table, half(k16, c % 2, 64)), AF.Copy)
+            if c in BEHIND:
+                tasks[-1]["calls"][0][2].append(a3("a3", 4 * BEHIND[c], 4 * BEHIND[c] + 4))
+            for q in range(4 * c, 4 * c + 4):
+                tt(row("d3", q), ind(table, half(p16, q % 8, 16)), half("sg", q, 256), Op.subtract)
+            if relu:
+                ts(a3("a3", 4 * c, 4 * c + 4), a3("d3", 4 * c, 4 * c + 4), 0.0, Op.max)
+            else:
+                act(a3("a3", 4 * c, 4 * c + 4), a3("d3", 4 * c, 4 * c + 4), AF.Abs)
+            o = cb(h, 64 * (c % 2), 64 * (c % 2) + 64)
+            mm(o, a("ones"), a("cj", 0, 64), True, False)
+            if relu:
+                lanes(o, "zn", "d3", c, 16, False, False)
+            lanes(o, "zr" if relu else "zd", "a3", c, 16, False, False)
+            lanes(o, "z1", "d3", c, 16, False, True)
 
-    def shifted1(k):
-        z = ("bT", "bZ")[k % 2]
-        for u in range(4 * k, min(4 * k + 4, 18)):
-            o, s = 128 * (u - 4 * k), 0 if u == 16 else 128 * min(u + 1, 15)
-            mm(a(z, o, o + 128), a("idn") if u == 17 else a("st", s, s + 128), a("kh"), True, True)
-        if k < 4:
-            act(a("wt1", 512 * k, 512 * k + 512), a(z), AF.Copy)
+        ts(half("kp", h), a(k16), 32.0, Op.add)
+        for u, (x, y) in enumerate((("s15", "s5k"), ("idf", "idk"))):
+            mm(half("mc", 2 * h + u, 64), a(x), half("kp", 2 * h, 64), True, False)
+            mm(half("mc", 2 * h + u, 64), a(y), half("kp", 2 * h + 1, 64), False, True)
+        act(a(wt, 0, 128), half("mc", h), AF.Copy, bias=-32.0 * 4097)
+        w, k = T[wt], T["kd%d" % h]
+        dmas("y", "kd%d" % h, [(k[:, 1:17, :], w[:, 64:128]), (k[:, 17:33, :], w[:, 0:64])], [scratch(h, 1, 33)], [a(wt, 0, 128)], 2 ** 16)
+        dmas("y", "wd%d" % h, [(w[j:128:16, 128:1152], k[:, 1 + j:17 + j, :]) for j in range(1, 16)] + [(w[:, 2176:2240], k[:, 0:16, :])],
+             [a(wt, 128, 2240)], [scratch(h, 0, 33)], 2 ** 19)
+
+        copy(half("ph_", h), a(p16))
+        mm(p_sum, a("idn"), half("ph_", h), True, True)
+        scan(half("mi", h), a("rst"), cb(h, 0, 128), 1e9, Op.max, Op.min)
+        ts(half("cl", h, 8), a("mi", 128 * h + 15, 128 * h + 128, 16), LOW, Op.max, a("thr"), Op.min)
+        ts(half("v8", h, 8), half("cl", h, 8), 11, Op.arith_shift_right, 255, Op.bitwise_and)
+        copy(l8, half("v8", h, 8))
+        tt(a(sel, 128, 256), ind(a("lutf"), l8), half("ph_", h), Op.min)
+        tt(a(sel, 0, 128), ind(a("lutk"), l8), half("ph_", h), Op.min)
+        mm(a(m, 0, 64), a("z1", 15, 143), a(sel, 128, 192), True, True)
+        mm(a(m, 64, 128), a("zk"), a(sel, 192, 256), True, True)
+        mm(a(m, 128, 256), a("idn"), a("tm"), True, False)
+        mm(a(m, 128, 256), a("gm"), a(sel, 0, 128), False, True)
+        for i in range(16):
+            mm(a(m, 256, 272), a("z1", 15 - i, 143 - i), a(sel, i, 256, 16), i == 0, i == 15)
+        copy(half("pn16", h, 16), a(m, 256, 272))
+        act(a(nr), a(m, 0, 264), AF.Copy)
+
+        act(half("xn", h), ind(table, n16), AF.Copy)
+        mm(cb(h, 384, 512), half("xn", h), a("idn"), True, True)
+        act(half("xr", h), cb(h, 384, 512), AF.Copy)
+        for b in range(4 * h, 4 * h + 4):
+            e = a("e%d" % ((8 * t + (b + 4) % 8) % 3))
+            mm(e, a("idn"), half("sg", b, 512), True, False)
+            mm(e, half("xr", h), half("ex", b % 4, 512), False, True)
+            act(a3("ae", 2 * b, 2 * b + 2, 0, 256), e, AF.Abs)
+            if b % 2:
+                lanes(cb(h, 128 + 72 * (b // 2 % 2), 200 + 72 * (b // 2 % 2)), "z1", "ae", b // 2, 18, True, True)
+        act(half("sc", h, 144), cb(h, 128, 272), AF.Sign, bias=-1039.5)
+        act(a("sc", 144 * h + 16, 144 * h + 144, 18), a(nr, 256, 264), AF.Copy, scale=33.0 / 2 ** 17)
+        scan(half("ms", h, 144), half("sc", h, 144), a("rs"), 100.0, Op.min, Op.add)
+        ts(half("o16", h, 8), a("ms", 144 * h + 16, 144 * h + 144, 18), 1024.0, Op.mult, 2176.0, Op.add)
+        tt(half("fr", h), ind(a(wt), half("o16", h, 8)), a(nr, 0, 128), Op.add)
+        ts(half("fu", 2 * h, 64), half("fr", 2 * h, 64), 4095, Op.bitwise_and)
+        ts(half("fu", 2 * h + 1, 64), half("fr", 2 * h + 1, 64), 12, Op.logical_shift_right)
+        if last:
+            copy(half("yk32", h), half("fu", h))
+            dmas("y", "ok%d" % h, [(T.yk[:, 128 * h:128 * h + 128], half("yk32", h)[0])], [], [half("yk32", h)], 2 ** 16)
         else:
-            act(a("wt1", 2048, 2176), a(z, 0, 128), AF.Copy)
-            act(a("wt1", 3968, 4096), a(z, 128, 256), AF.Copy)
+            copy(a("ks_%d_%d" % (t, h)), half("fu", h))
+            send("k", t, h, nxt, prv)
 
-    def shifted0():
-        y, w, k = g.sync, "wd", "kd"
+        tt(half("pa", h), ind(a("lutm"), l8), half("kp", h), Op.min)
+        tt(half("pt", h), half("pa", h), p_sum, Op.mult)
+        ts(half("pn", h), half("pt", h), 5, Op.logical_shift_right, 2047, Op.bitwise_and)
+        if last:
+            copy(half("yp32", h), half("pn", h))
+            dmas("y", "op%d" % h, [(T.yp[:, 128 * h:128 * h + 128], half("yp32", h)[0])], [], [half("yp32", h)], 2 ** 16)
+        else:
+            copy(a("ps_%d_%d" % (t, h)), half("pn", h))
+            send("p", t, h, prv, nxt)
 
-        def start(sem, out, in_):
-            y.dma_start(out, in_).then_inc(T.sem[sem], 16)
-            dmas[sem] += 16
-
-        if dmas[w]:
-            waits("y", {w: dmas[w]})
-        kp = a("kp", 0, 128)
-        waits("y", need("dma", [], [kp]))
-        start(k, T.kd[:, 1:17, :], kp[0])
-        for r in range(15):
-            start(k, T.kd[:, 17 + r, :], T.kp[15:128:16, 0:128])
-        note("dma", k, dmas[k], [], [kp], {})
-        waits("y", need("dma", [a("wt0")], []))
-        start(w, T.wt0[:, 3968:4096], kp[0])
-        y.wait_ge(T.sem[k], dmas[k])
-        for j in range(1, 16):
-            start(w, T.wt0[j:128:16, 0:2048], T.kd[:, 1 + j:17 + j, :])
-        start(w, T.wt0[:, 2048:2176], T.kd[:, 0:16, :])
-        note("dma", w, dmas[w], [a("wt0")], [kp], {})
-
-    sent = [0]
-    nxt, prv = T.cores[(rank + 1) % n_ranks], T.cores[(rank - 1) % n_ranks]
-    n_k = len(topo.engines(prv, core))
-    n_p = len(topo.engines(nxt, core))
-
-    def send(name, dst_name, dst, sem, n_in):
-        rid, pid = topo.addr(dst, core)
-        waits("g", need("g", [], [a(name)]))
-        g.remote_dma(T[dst_name][:], T[name][:], T.sem[sem], T.sem["sent"], pid, rid, topo.mask(core, dst))
-        sent[0] += len(topo.engines(core, dst))
-        note("dma", sem, n_in, [a(dst_name)], [], {})
-
-    def gather_y(t, c):
-        act(a("yg", 1024 * c, 1024 * c + 1024), ind(a("xt%d" % (t % 2)), a("p16_%d" % t, 64 * c, 64 * c + 64)), AF.Copy)
+        ts(half("kk", h, 8), half("cl", h, 8), 13, Op.arith_shift_right, 15, Op.bitwise_and)
+        tt(half("ok", h, 8), half("kk", h, 8), a("c16"), Op.add)
+        copy(half("ok16", h, 8), half("ok", h, 8))
+        act(half("sk", h), ind(half("sg", h, 2048), half("ok16", h, 8)), AF.Copy)
+        tt(half("dk", h), ind(table, pk16), half("sk", h), Op.subtract)
+        act(half("adk", h), half("dk", h), AF.Abs)
+        ts(half("c1", h), half("adk", h), 32.0, Op.is_le, 128.0, Op.mult)
+        tt(half("wv", h), ind(table, pk16), half("c1", h), Op.subtract)
+        ts(half("vv", h), half("wv", h), 0.0, Op.is_lt, 256.0, Op.mult)
+        tt(half("eq", h), ind(a(nr, 256, 264), a("bl")), a(nr, 128, 256), Op.is_equal)
+        mm(a(m, 272, 280), a("idf"), a(nr, 256, 264), True, False)
+        for i in range(16):
+            mm(a(m, 272, 280), a("zw", 15 - i, 143 - i), a("eq", 128 * h + i, 128 * h + 128, 16), False, i == 15)
+        ts(a("w16", 16 * h, 16 * h + 16, 2), a(m, 272, 280), 16.0, Op.add, a("lf", 0, 1), Op.max)
 
     for t in range(RO):
-        last, first = t == RO - 1, t == 0
-        xt, xn = "xt%d" % (t % 2), "xt%d" % ((t + 1) % 2)
-
-        def d_chunk(t, c):
-            for q in range(4 * c, 4 * c + 4):
-                tt(row("d3", q), ind(a("xt%d" % (t % 2)), a("k16_%d_%d" % (t, q // 8), 16 * (q % 8), 16 * (q % 8) + 16)),
-                   a("yg", 256 * q, 256 * q + 256), Op.subtract)
-
-        def d_abs(c):
-            act(a3("a3", 4 * c, 4 * c + 4), a3("d3", 4 * c, 4 * c + 4), AF.Abs)
-
-        def t_sum(c):
-            lanes(a(("bT", "bT2")[c // 2], 64 * c, 64 * c + 64), "z1", "d3", c, True)
-
-        def d_sum(c):
-            o = a(("bD", "bD2")[c // 2], 64 * c, 64 * c + 64)
-            mm(o, a("idn"), a("cj", 64 * c, 64 * c + 64), True, False)
-            lanes(o, "z64", "a3", c, False)
-
-        def sign(h):
-            s = (128 * h, 128 * h + 128)
-            act(a("sn", *s), a(("bT", "bT2")[h], *s), AF.Sign)
-
-        def s_gather(c):
-            lo = 64 * (c % 2)
-            act(a("sg", 1024 * c, 1024 * c + 1024), ind(a(xt), a("k16_%d_%d" % (t, c // 2), lo, lo + 64)), AF.Copy)
-
-        def least(h):
-            s, m = (128 * h, 128 * h + 128), (8 * h, 8 * h + 8)
-            tt(a("code", *s), a(("bD", "bD2")[h], *s), a("sn", *s), Op.add)
-            scan(a("mi", *s), a("rst", *s), a("code", *s), Op.max, Op.min)
-            ts(a("v8", *m), a("mi", s[0] + 15, s[1], 16), 255, Op.bitwise_and)
-            copy(a("l8", *m), a("v8", *m))
-            tt(a("nsel", *s), ind(a("lutf"), a("l8", *m)), a("p32", *s), Op.mult)
-            mm(a("bN", *s), a("gm"), a("nsel", *s), True, True)
-
-        def heads(h):
-            copy(a("nb", 128 * h, 128 * h + 128), a("bN", 128 * h, 128 * h + 128))
-
-        def plus(t, h):
-            ts(a("kp", 128 * h, 128 * h + 128), a("k16_%d_%d" % (t, h)), 32.0, Op.add)
-
-        def half1():
-            copy(a("kh"), a("k16_%d_1" % t))
-
-        def near(c):
-            s = (1024 * c, 1024 * c + 1024)
-            tt(a("eg", *s), ind(a(xt), a("nb", 64 * c, 64 * c + 64)), a("sg", *s), Op.subtract)
-
-        def near_abs(c):
-            act(a3("ae", 4 * c, 4 * c + 4), a("eg", 1024 * c, 1024 * c + 1024), AF.Abs)
-
-        def near_sum(c):
-            lanes(a(("bD", "bD2")[c // 2], 64 * c, 64 * c + 64), "z1", "ae", c, True)
-
-        def arrays(h):
-            s, m = (128 * h, 128 * h + 128), (8 * h, 8 * h + 8)
-            ts(a("ew", *s), a(("bD", "bD2")[h], *s), 1040.0, Op.is_lt, -2048.0, Op.mult)
-            scan(a("ms", *s), a("rs2", *s), a("ew", *s), Op.add, Op.min)
-            tt(a("o1", *m), a("ms", s[0] + 15, s[1], 16), a("npx", *m), Op.max)
-            tt(a("o2", *m), a("o1", *m), a("cw", *m), Op.add)
-            copy(a("o16", *m), a("o2", *m))
-            tt(a("fr", *s), ind(a("wt%d" % h), a("o16", *m)), a("nfix", *s), Op.add)
-            out = a("yk32", *s) if last else a("ks_%d_%d" % (t, h))
-            if h == 0:
-                ts(out, a("fr", *s), -32.0, Op.add)
-            else:
-                copy(out, a("fr", *s))
-            if not last:
-                send("ks_%d_%d" % (t, h), "k16_%d_%d" % (t + 1, h), nxt, "ka%d_%d" % (t + 1, h), n_k)
-
-        def fates():
-            mc = a("mi", 15, 256, 16)
-            ts(a("lt"), mc, a("thr"), Op.is_lt)
-            ts(a("kf"), mc, 53248.0, Op.is_lt)
-            tt(a("ksel"), ind(a("lutk"), a("l8")), a("p32"), Op.mult)
-            mm(a("bM", 32, 48), a("gm"), a("kf"), True, True)
-            mm(a("bT2", 0, 256), a("gm"), a("ksel"), True, True)
-            tt(a("fl"), a("lt"), a("kf"), Op.add)
-            copy(a("fl16"), a("fl"))
-
-        def names():
-            act(a("pks"), a("bT2", 0, 256), AF.Copy)
-            act(a("ns", 0, 128), a("bN", 0, 128), AF.Copy, bias=32.0)
-            act(a("ns", 128, 256), a("bN", 128, 256), AF.Copy)
-
-        def phages():
-            tt(a("pa"), ind(a("lutm"), a("fl16")), a("kp"), Op.min)
-            ts(a("kk"), a("v8"), 2, Op.logical_shift_right, 15, Op.bitwise_and)
-            tt(a("pt"), a("pa"), a("p32"), Op.mult)
-            tt(a("ok"), a("kk"), a("c16"), Op.add)
-            ts(a("pn"), a("pt"), 5, Op.logical_shift_right, 2047, Op.bitwise_and)
-            copy(a("ok16"), a("ok"))
-            if last:
-                copy(a("yp32"), a("pn"))
-                dma("y", "op", T.yp[:], T.yp32[:], [], [a("yp32")])
-            else:
-                copy(a("ps_%d" % t), a("pn"))
-                send("ps_%d" % t, "p16_%d" % (t + 1), prv, "pa%d" % (t + 1), n_p)
-
-        def lanes_k():
-            act(a("yk_"), ind(a("yg"), a("ok16")), AF.Copy)
-            act(a("sgn"), ind(a("yg"), a("ok16")), AF.Sign, scale=-1.0, bias=127.5)
-
-        def writers():
-            tt(a("rr"), ind(a("luto"), a("fl16")), a("pks"), Op.max)
-            for i in range(16):
-                mm(a("bM", 0, 16), a("dg_", 128 * i, 128 * i + 128), a("rr", i, 256, 16), i == 0, i == 15)
-
-        def values():
-            tt(a("dk"), ind(a("sg"), a("ok16")), a("yk_"), Op.subtract)
-            act(a("adk"), a("dk"), AF.Abs)
-            tt(a("nfix"), ind(a("lutp"), a("fl16")), a("ns"), Op.mult)
-            ts(a("npx"), a("fl"), 1.0, Op.is_equal, -8192.0, Op.mult)
-
-        def equals():
-            copy(a("ol"), a("bM", 0, 16))
-            for q in range(16):
-                ts(a("eq", 272 * q, 256 * q + 256), a("rr", 16 * q, 256), a("ol", q, q + 1), Op.is_equal)
-                mm(a("bC", 16 * q, 16 * q + 16), a("tri"), a("eq", 272 * q, 272 * q + 16), q == 0, q in (0, 15))
-                if q < 15:
-                    mm(a("bC", 16 * q + 16, 256), a("gm"), a("eq", 272 * q + 16, 256 * q + 256), q == 0, False)
-
-        def counts():
-            act(a("cs"), a("bC", 0, 256), AF.Copy, scale=4096.0)
-            for i in range(16):
-                mm(a("bM", 16, 32), a("dg_", 128 * i, 128 * i + 128), a("cs", i, 256, 16), i == 0, i == 15)
-
-        def change():
-            ts(a("c1"), a("adk"), 32.0, Op.is_le, 128.0, Op.mult)
-            tt(a("tt"), a("c1"), a("sgn"), Op.mult)
-
-        def scatter():
-            tt(a("v1"), a("bM", 16, 32), a("ol"), Op.add)
-            tt(a("v2"), a("v1"), a("cd"), Op.min)
-            copy(a("w16"), a("v2"))
-            tt(ind(a(xn), a("w16")), a("yk_"), a("tt"), Op.add)
-
-        def allowance():
-            do("v", lambda: V.tensor_reduce(T.ca[:], T.bM[:, 32:48], AX.X, Op.add), [a("ca")], [a("bM", 32, 48)])
-            tt(a("aa"), a("aa"), a("ca"), Op.add)
+        for h in (1, 0):
+            half_round(t, h)
+        for q in range(15, -1, -1):
+            tt(ind(a("xt"), a("w16", 2 * q, 2 * q + 1)), half("wv", q, 16), half("vv", q, 16), Op.add)
+        if t == RO - 1:
+            dmas("y", "oy", [(T.yx[:], table[0])], [], [table], 2 ** 19)
+        else:
+            act(a("jk"), a("mi", 15, 256, 16), AF.Sign, acc=a("ac", t, t + 1), scale=-1.0, bias=LOW)
+            for u in range(t + 1):
+                mm(a("m1", 288, 289), a("gmf"), a("ac", u, u + 1), u == 0, u == t)
+            ts(a("aa"), a("m1", 288, 289), 0.5, Op.mult, 128.0 * (t + 1), Op.add)
             ts(a("ab"), a("aa"), 15, Op.bitwise_and)
-            ts(a("thr"), a("ab"), 256.0, Op.mult, 65536.0, Op.add)
+            ts(a("thr"), a("ab"), 2.0 ** 19, Op.mult, TOP, Op.add)
 
-        next_table(t)
-        if first:
-            shifted0()
-            for c in range(4):
-                gather_y(0, c)
-            d_chunk(0, 0)
-            d_chunk(0, 1)
-        steps = {"le0": lambda: (consts1() if first else None, least(0)), "le1": lambda: least(1),
-                 "he0": lambda: (consts2() if first else None, heads(0)), "he1": lambda: heads(1),
-                 "dc2": lambda: d_chunk(t, 2), "dc3": lambda: d_chunk(t, 3), "sn0": lambda: sign(0), "sn1": lambda: sign(1),
-                 "fa": fates, "pk": names, "kh": half1, "wr": writers, "ph": phages, "yk": lanes_k, "eq": equals, "va": values,
-                 "co": counts, "ch": change, "sc": scatter, "ar0": lambda: arrays(0), "ar1": lambda: arrays(1)}
-        for c in range(4):
-            for x, f in (("ts", t_sum), ("da", d_abs), ("ds", d_sum), ("sg", s_gather), ("n", near), ("na", near_abs), ("nl", near_sum)):
-                steps["%s%d" % (x, c)] = lambda f=f, c=c: f(c)
-        for k in range(5):
-            steps["sh%d" % k] = lambda k=k: shifted1(k)
-        if not first:
-            steps["pl1"] = lambda: plus(t, 1)
-        if not last:
-            steps.update({"al": allowance, "p32": lambda: copy(a("p32"), a("p16_%d" % (t + 1))), "pl0": lambda: plus(t + 1, 0),
-                          "w0": shifted0, "dc0": lambda: d_chunk(t + 1, 0), "dc1": lambda: d_chunk(t + 1, 1)})
-            for c in range(4):
-                steps["y%d" % c] = lambda c=c: gather_y(t + 1, c)
-        for x in ORDER.split():
-            if x in steps:
-                steps[x]()
-            if x == "sc" and last:
-                dma("y", "oy", T.yx[:], T[xn][:, 0:2048], [], [a(xn, 0, 2048)])
-        if last:
-            dma("y", "ok", T.yk[:], T.yk32[:], [], [a("yk32")])
-    g.wait_ge(T.sem["sent"], sent[0])
-    for s in ("oy", "ok", "op"):
-        g.sync.wait_ge(T.sem[s], 16)
-    for q in cnt:
-        if seen["y"].get(q, 0) < cnt[q]:
-            g.sync.wait_ge(T.sem[q], cnt[q])
+    def clash(hist, q, outs, ins, banks):
+        for kind, lst in (("w", outs), ("r", ins)):
+            for x in lst:
+                for k2, lo, hi, q2, who in hist.get(x[1], ()):
+                    same = q2 == q and q != "dma"
+                    if banks and x[1] in PSUM and not same or not (k2 == kind == "r" or hi <= x[2] or lo >= x[3]):
+                        yield who, same and q == "p"
+
+    def note(hist, q, outs, ins, who):
+        for kind, lst in (("w", outs), ("r", ins)):
+            for x in lst:
+                e = hist.setdefault(x[1], [])
+                e[:] = [y for y in e if not (y[1] >= x[2] and y[2] <= x[3] and (kind == "w" or y[0] == "r" and y[3] == q != "dma"))]
+                e.append((kind, x[2], x[3], q, who))
+
+    hist = {}
+    for n, x in enumerate(tasks):
+        q = x["q"] if x["kind"] == "call" else "dma"
+        x["needs"], x["next"], x["banks"], at = {}, [], set(), 0
+        for call, outs, ins, cost in x["calls"]:
+            for who, free in clash(hist, q, outs, ins, False):
+                if who != n:
+                    x["needs"][who] = max(x["needs"].get(who, -1e9), (0 if free else HOP) - at)
+            note(hist, q, outs, ins, n)
+            x["banks"].update(y[1] for y in outs + ins if y[1] in PSUM)
+            at += cost
+        x["cost"] = at
+        for who in x["needs"]:
+            tasks[who]["next"].append(n)
+    before = [{w: d + tasks[w]["after"] for w, d in x["needs"].items()} for x in tasks]
+    behind = [{w: before[w][n] for w in x["next"]} for n, x in enumerate(tasks)]
+
+    def in_order(needs, nexts, key):
+        order, open_ = [], [len(x) for x in needs]
+        ready = [n for n, k in enumerate(open_) if not k]
+        while ready:
+            n = min(ready, key=key)
+            ready.remove(n)
+            order.append(n)
+            for w in nexts[n]:
+                open_[w] -= 1
+                if not open_[w]:
+                    ready.append(w)
+        return order
+
+    def place(needs, nexts, key, first):
+        end, busy = {}, {}
+        for n in in_order(needs, nexts, key):
+            x = tasks[n]
+            at = max([first[n]] + [end[w] + d for w, d in needs[n].items()])
+            held = sorted(busy.get(x["q"], []) + [(lo - HOP, hi + HOP) for b in x["banks"] for lo, hi, q in busy.get(b, []) if q != x["q"]])
+            for lo, hi in held:
+                if hi > at:
+                    if lo >= at + x["cost"]:
+                        break
+                    at = hi
+            end[n] = at + x["cost"]
+            busy.setdefault(x["q"], []).append((at, end[n]))
+            for b in x["banks"]:
+                busy.setdefault(b, []).append((at, end[n], x["q"]))
+        return end
+
+    way = [0] * len(tasks)
+    for n in range(len(tasks) - 1, -1, -1):
+        way[n] = tasks[n]["cost"] + max([tasks[n]["after"]] + [way[w] + d for w, d in behind[n].items()])
+    ends = place(before, behind, lambda n: -way[n], [0] * len(tasks))
+    order = in_order(before, behind, lambda n: ends[n] - tasks[n]["cost"])
+
+    hist, seen, known, count, left = {}, {q: {} for q in Q}, {}, {}, []
+
+    def waits(q, needs):
+        want = {}
+        for (sem, val), free_ in needs:
+            if not free_:
+                want[sem] = max(want.get(sem, 0), val)
+        for sem, val in sorted(want.items()):
+            if seen[q].get(sem, 0) < val:
+                Q[q].wait_ge(T.sem[sem], val)
+                seen[q][sem] = val
+                for s2, v2 in known.get((sem, val), {}).items():
+                    seen[q][s2] = max(seen[q].get(s2, 0), v2)
+
+    for n in order:
+        q, kind = tasks[n]["q"], tasks[n]["kind"]
+        for call, outs, ins, cost in tasks[n]["calls"]:
+            waits(q, clash(hist, q if kind == "call" else "dma", outs, ins, True))
+            if kind == "call":
+                sem, count[q] = q, count.get(q, 0) + 1
+                call().then_inc(T.sem[q], 1)
+            elif kind == "dma":
+                sem = call[0]
+                for out, in_ in call[1]:
+                    Q[q].dma_start(out, in_).then_inc(T.sem[sem], 16)
+                    count[sem] = count.get(sem, 0) + 16
+            else:
+                sem, gone, dst, src = call
+                rid, pid = topo.addr(dst, core)
+                g.remote_dma(outs[0][0], ins[0][0], T.sem[sem], T.sem[gone], pid, rid, topo.mask(core, dst))
+                left.append((gone, len(topo.engines(core, dst))))
+                count[sem], ins = len(topo.engines(src, core)), []
+            known[(sem, count[sem])] = dict(seen[q]) if kind != "send" else {}
+            note(hist, q if kind == "call" else "dma", outs, ins, (sem, count[sem]))
+    for sem, val in left:
+        g.wait_ge(T.sem[sem], val)
+    for sem in ("oy", "ok0", "ok1", "op0", "op1", "v", "s", "p", "g"):
+        if seen["y"].get(sem, 0) < count[sem]:
+            g.sync.wait_ge(T.sem[sem], count[sem])

@@ -1,40 +1,64 @@
+import numpy as np
 from concourse.mybir import AluOpType as Op, ActivationFunctionType as AF
 
 RO = 4
 F, B, H, I, U = "float32", "bfloat16", "float16", "int32", "uint16"
 SCRATCH = {}
 for _n, _w, _d in (
-        ("xt", 2064, B), ("nk", 256, I), ("np_", 256, I), ("sg", 4096, B), ("ph_", 256, H), ("kp", 256, F),
-        ("mi", 256, F), ("cl", 16, I), ("v8", 16, I), ("l8", 16, U), ("sel0", 256, H), ("sel1", 256, H), ("pn16", 32, U),
+        ("xt", 2064, B), ("nk", 256, I), ("np_", 256, I), ("yg", 4096, B), ("ph_", 256, H), ("kh", 256, H), ("sn", 256, B),
+        ("mi", 256, F), ("cl", 16, I), ("v8", 16, I), ("l8", 16, U), ("sel0", 384, H), ("sel1", 384, H), ("pn16", 48, U),
         ("nr0", 264, F), ("nr1", 264, F), ("xn", 256, B), ("xr", 256, B), ("eq", 256, B), ("w16", 32, U),
-        ("kk", 16, I), ("ok", 16, I), ("ok16", 16, U), ("sk", 256, B), ("dk", 256, B), ("adk", 256, B), ("c1", 256, B),
-        ("wv", 256, B), ("vv", 256, B), ("pa", 256, F), ("pt", 256, I), ("pn", 256, I), ("yp32", 256, F),
-        ("wt0", 2240, F), ("wt1", 2240, F), ("sc", 288, B), ("ms", 288, F), ("o16", 16, U), ("fr", 256, I), ("fu", 256, I), ("yk32", 256, F),
-        ("jk", 16, B), ("ac", 4, F), ("aa", 1, I), ("ab", 1, I), ("thr", 1, F),
-        ("pi", 2, I), ("li", 2, I), ("lf", 2, F), ("l16", 2, F), ("l15", 2, F), ("ones", 128, B), ("neg", 512, B), ("gm", 128, B), ("idn", 128, B),
-        ("idf", 128, F), ("idk", 128, F), ("gmf", 128, F), ("s15", 128, F), ("s5k", 128, F),
-        ("z1", 143, B), ("zd", 143, B), ("zr", 143, B), ("zn", 143, B), ("zw", 143, B), ("zk", 128, B),
-        ("cj", 128, B), ("rst", 128, F), ("rs", 144, F), ("ex", 2048, B), ("tm", 128, B), ("ij", 128, I), ("iq", 16, I),
-        ("bl", 8, U), ("c16", 8, F), ("i3", 192, I), ("i4", 192, I), ("nil", 64, F),
+        ("yk_", 256, B), ("dk", 256, B), ("adk", 256, B), ("c1", 256, B),
+        ("wv", 256, B), ("vv", 256, B), ("pa", 256, H), ("pt", 256, I), ("pn", 256, I), ("yp32", 256, F),
+        ("wt0", 2176, F), ("wt1", 2176, F), ("fl", 288, B), ("fk", 72, B), ("sc", 288, B), ("ms", 288, F), ("o16", 16, U), ("fr", 256, I), ("fu", 256, I),
+        ("yk32", 256, F), ("jk", 16, B), ("ac", 4, F), ("aa", 1, I), ("ab", 1, I), ("thr", 1, F),
+        ("pi", 2, I), ("li", 2, I), ("lf", 2, F), ("l15", 2, F), ("ones", 128, B), ("neg", 512, B), ("gm", 128, B), ("idn", 128, B),
+        ("idf", 128, F), ("idk", 128, B), ("id1k", 128, B), ("gmf", 128, F), ("s15", 128, B), ("s5k", 128, B), ("qu", 128, B), ("up1", 128, B), ("upk", 128, B),
+        ("z1", 143, B), ("zd", 143, B), ("zr", 143, B), ("zn", 143, B), ("zw", 143, B), ("zk", 128, B), ("zm", 143, B), ("idm", 128, B),
+        ("cj", 128, B), ("rst", 128, F), ("rs", 144, F), ("ex", 2048, B), ("tm", 128, B), ("ij", 128, I), ("iq", 8, I),
+        ("bl", 8, U), ("c16", 4, F), ("i3", 192, I), ("i4", 192, I), ("nil", 64, F),
         ("lutf", 256, B), ("lutk", 256, B), ("lutm", 256, B)):
     SCRATCH[_n] = ("sbuf", [128, _w], _d)
-for _n, _w in (("d3", 256), ("a3", 256), ("ae", 272)):
+for _n, _w in (("d3", 256), ("a3", 256), ("ae", 288)):
     SCRATCH[_n] = ("sbuf", [128, 16, _w], B)
+for _n in ("d2", "a2"):
+    SCRATCH[_n] = ("sbuf", [128, 8, 512], B)
 for _h in range(2):
     SCRATCH["kd%d" % _h] = ("dram", [8, 33, 64], F)
-    for _t in range(RO):
-        for _n in ("k16", "p16") + (("ks", "ps") if _t < RO - 1 else ()):
-            SCRATCH["%s_%d_%d" % (_n, _t, _h)] = ("sbuf", [128, 128], U)
-PSUM = ("e0", "e1", "e2", "c0", "c1_", "m0", "m1", "mc")
+for _t in range(RO):
+    for _n, _w in (("k16_%d_0", 128), ("k16_%d_1", 128), ("p16_%d", 256)) + ((("ks_%d_0", 128), ("ks_%d_1", 128), ("ps_%d", 256)) if _t < RO - 1 else ()):
+        SCRATCH[_n % _t] = ("sbuf", [128, _w], U)
+WIDE = False
+NONE = "y"
+PSUM = ("e0", "e1") + (() if WIDE else ("e2", "e3")) + ("c0", "c1_", "m0", "m1")
 for _n in PSUM:
-    SCRATCH[_n] = ("psum", [128, 512], F)
-SEMAPHORES = (["v", "s", "p", "g", "lx", "lp", "lk", "oy", "ok0", "ok1", "op0", "op1", "kz", "kd0", "kd1", "wd0", "wd1"]
-              + ["%s%d_%d" % (x, t, h) for x in ("ka", "pa", "kl", "pl") for t in range(1, RO) for h in range(2)])
-RELU = (1,)
-BEHIND = {0: 3}
+    SCRATCH[_n] = ("psum", [128, 1024 if WIDE and _n[0] == "e" else 512], F)
+SEMAPHORES = (["v", "s", "p", "g", "lx", "oy", "kz"] + [x + h for x in ("lp", "lk", "ok", "op", "kd", "wd") for h in "01"]
+              + ["%s%s%d_%d" % (y, x, t, h) for x in "kp" for t in range(1, RO) for h in range(4) for y in "al"])
+RELU = (0,)
+BEHIND = {1: 2}
+GATE = False
+LEAD = 4000
+AHEAD = (0, 0, 0, 0)
+MOVES, SEED, PLAN = 9000, 3, []
+SPEEDS = ((1, 0.9, 0.85), (1.4, 0.7, 1.0), (1.5, 0.8, 1.0))
+EB = 3
+FIRST = "pp"
+WHOLE = ("t1",)
+QUART = ()
+HEADS = False
+NEARV = True
+PIECES = {2: ((0, 1), (1, 4)), 3: ((0, 1), (1, 4))}
+PARTS = {}
+SPLIT = True
+LONG = False
+APART = False
+SIGN = (0, 1)
+PICK = 88
+POOL = ("kh", "ph", "ps")
 LOW = -(2.0 ** 24) - 2048
 TOP = 63 * 2.0 ** 17 + 15 * 2.0 ** 13 + 4096
-HOP, CALL, ACT, GATHER, SCATTER, ISSUE, LOCAL, REMOTE, FAR, BYTES, TURNS = 170, 40, 110, 1.56, 3.8, 70, 2000, 850, 3500, 190, 6
+HOP, CALL, ACT, GATHER, SCATTER, ISSUE, LOCAL, REMOTE, FAR, BYTES, MATMUL, COLUMN, ROWS, ROW = 176, 39.6, 76.95, 1.45, 3.5, 242.3, 1300, 588.06, 2800, 152, 9.9, 0.45, 3089.53, 237.18
 
 
 def rank_program(g, core, T, topo):
@@ -54,7 +78,11 @@ def rank_program(g, core, T, topo):
         return (T[name][:, q0:q1, :] if c0 is None else T[name][:, q0:q1, c0:c1], name, w * q0, w * q1, (q1 - q0) * (w if c0 is None else c1 - c0))
 
     def row(name, q):
-        return (T[name][:, q], name, 256 * q, 256 * q + 256, 256)
+        w = SCRATCH[name][1][2]
+        return (T[name][:, q], name, w * q, w * q + w, w)
+
+    def half(name, h, w=128):
+        return a(name, w * h, w * h + w)
 
     def ind(win, off):
         return (win[0].indirect(off[0]), win, off)
@@ -65,18 +93,18 @@ def rank_program(g, core, T, topo):
             r += [x] if isinstance(x[1], str) else [x[1], x[2]]
         return r
 
-    tasks = []
+    tasks, now_ = [], [-1]
 
-    def task(q, kind, call, outs, ins, cost, after=0, more=False):
+    def task(q, kind, call, outs, ins, cost, after=0, more=False, moves=None):
         if not more:
-            tasks.append(dict(q=q, kind=kind, calls=[], after=after))
+            tasks.append(dict(q=q, kind=kind, calls=[], after=after, moves=moves, round=now_[0]))
         tasks[-1]["calls"].append((call, flat(outs), flat(ins), cost))
 
     def vec(fn, out, ins, rate):
         if isinstance(out[1], tuple):
-            task("v", "call", fn, [out[1]], ins + [out[2]], 60 + SCATTER * ins[0][4])
+            task("v", "call", fn, [out[1]], ins + [out[2]], PICK + SCATTER * ins[0][4])
         elif ins and isinstance(ins[0][1], tuple):
-            task("v", "call", fn, [out], ins, 60 + GATHER * out[4])
+            task("v", "call", fn, [out], ins, PICK + GATHER * out[4])
         else:
             task("v", "call", fn, [out], ins, CALL + max(64, rate * out[4]))
 
@@ -110,9 +138,9 @@ def rank_program(g, core, T, topo):
         else:
             task("s", "call", lambda: S.activation(out[0], in_[0], func, accum_out=acc[0], **kw), [out, acc], [in_], cost)
 
-    def mm(out, l, r, start, stop):
-        task("p", "call", lambda: P.matmul(out[0], l[0], r[0], start, stop), [out], [l, r],
-             6 + max(64, r[4]) * (2 if SCRATCH[l[1]][2] == F else 0.5), more=not start)
+    def mm(out, l, r, start, stop, cut=False, holds=None):
+        task("p", "call", lambda: P.matmul(out[0], l[0], r[0], start, stop), [holds or out], [l, r],
+             MATMUL + max(64, r[4]) * (4 if SCRATCH[l[1]][2] == F else 1) * COLUMN, more=not (start or cut))
 
     def iota(out, pattern, base, cm):
         task("g", "call", lambda: g.iota(out[0], pattern, base, cm), [out], [], 160 + 2 * out[4])
@@ -120,26 +148,38 @@ def rank_program(g, core, T, topo):
     def asel(out, in_, pattern, cop, base, cm):
         task("g", "call", lambda: g.affine_select(out[0], in_[0], pattern, cop, 0.0, base, cm), [out], [in_], 200 + 2 * out[4])
 
-    def dmas(q, sem, pairs, outs, ins, size):
-        task(q, "dma", (sem, pairs), outs, ins, ISSUE * len(pairs), LOCAL + size / BYTES)
+    def turn(out, in_, key):
+        if key in POOL:
+            asel(out, in_, [[0, out[4]]], Op.is_equal, 0, 0)
+        else:
+            copy(out, in_)
 
-    def scratch(h, lo, hi):
-        return (None, "kd%d" % h, lo, hi, 0)
+    def dmas(q, sem, pairs, outs, ins, size):
+        task(q, "dma", (sem, pairs), outs, ins, ISSUE * len(pairs), max(LOCAL, LOCAL + size / BYTES - ISSUE * (len(pairs) - 1)),
+             moves=(ISSUE + LOCAL / 2, size / BYTES))
+
+    def scratch(h):
+        return (None, "kd%d" % h, 0, 1, 0)
 
     nxt, prv = T.cores[(rank + 1) % n_ranks], T.cores[(rank - 1) % n_ranks]
 
-    def send(x, t, h, dst, src):
-        task("g", "send", ("%sa%d_%d" % (x, t + 1, h), "%sl%d_%d" % (x, t + 1, h), dst, src),
-             [a("%s16_%d_%d" % (x, t + 1, h))], [a("%ss_%d_%d" % (x, t, h))], REMOTE, FAR)
+    def send(to, names, sem, dst, src):
+        task("g", "send", ("a" + sem, "l" + sem, dst, src), [to], [names], REMOTE, FAR, moves=(REMOTE, ROWS))
 
     table = a("xt", 16, 2064)
 
-    dmas("s", "lk", [(T.nk[:], T.ka[:])], [a("nk")], [], 2 ** 17)
-    dmas("y", "lx", [(T.xt[:, 16:2064], T.x0[:])], [table], [], 2 ** 19)
-    dmas("y", "lp", [(T.np_[:], T.ph[:])], [a("np_")], [], 2 ** 17 + 2 ** 19)
+    if SPLIT:
+        dmas("s", "lp1", [(T.np_[:, 128:256], T.ph[:, 128:256])], [half("np_", 1)], [], 2 ** 16)
+        dmas("y", "lx", [(table[0], T.x0[:])], [table], [], 2 ** 19)
+        dmas("y", "lk0", [(T.nk[:], T.ka[:])], [a("nk")], [], 2 ** 17)
+        dmas("y", "lp0", [(T.np_[:, 0:128], T.ph[:, 0:128])], [half("np_", 0)], [], 2 ** 16)
+    else:
+        dmas("s", "lp0", [(T.np_[:], T.ph[:])], [a("np_")], [], 2 ** 17)
+        dmas("y", "lx", [(table[0], T.x0[:])], [table], [], 2 ** 19)
+        dmas("y", "lk0", [(T.nk[:], T.ka[:])], [a("nk")], [], 2 ** 17)
     for h in (1, 0):
-        copy(a("k16_0_%d" % h), a("nk", 128 * h, 128 * h + 128))
-        copy(a("p16_0_%d" % h), a("np_", 128 * h, 128 * h + 128))
+        copy(half("p16_0", h), half("np_", h))
+        copy(a("k16_0_%d" % h), half("nk", h))
 
     fill(a("ones"), 1.0)
     fill(a("neg"), -1.0)
@@ -148,7 +188,7 @@ def rank_program(g, core, T, topo):
     asel(a("gm"), a("gm"), [[16, 8], [0, 16]], Op.is_ge, 15, -1)
     asel(a("idn"), a("ones"), [[1, 128]], Op.is_equal, 0, -1)
     iota(a("ij"), [[0, 8], [1, 16]], 0, 0)
-    iota(a("iq"), [[1, 16]], 0, 0)
+    iota(a("iq"), [[1, 8]], 0, 0)
     iota(a("i3", 0, 64), [[1, 4], [1, 16]], 129, -1)
     iota(a("i3", 64, 128), [[-1, 4], [1, 16]], 127, -1)
     iota(a("i3", 128, 192), [[0, 4], [1, 16]], 128, -1)
@@ -156,29 +196,39 @@ def rank_program(g, core, T, topo):
         asel(a("ex", 512 * b, 512 * b + 512), a("neg"), [[1, 32], [0, 16]], Op.is_equal, 32 * b, -1)
     fill(a("nil"), 0.0)
     fill(a("z1"), 0.0)
+    fill(a("qu"), 0.25)
+    fill(a("fl"), 0.0)
+    if "fl" in POOL:
+        fill(a("fk"), 0.0)
+        fill(a("fk", 0, 72, 18), 4096.0)
     fill(a("rst"), -1e9)
     fill(a("rst", 0, 128, 16), 1e9)
     fill(a("thr"), TOP)
     fill(a("lutf"), 0.0)
     fill(a("lutk"), -512.0)
-    fill(a("lutm"), 32.0)
+    fill(a("lutm"), 0.0)
     fill(a("lutm", 255, 256), 4096.0)
     fill(a("w16"), 0)
-    fill(a3("ae", 0, 16, 256, 272), 0.0)
+    fill(a3("ae", 0, 16, 0, 16), 0.0)
+    fill(a3("ae", 0, 16, 272, 288), 0.0)
     fill(a("rs"), -0.0625)
     fill(a("rs", 17, 144, 18), 100.0)
     dmas("y", "kz", [(T["kd%d" % h][:, 0, :], T.nil[0:8, :]) for h in range(2)] + [(T["wt%d" % h][0:128:16, 128:1152], T.nil[:]) for h in range(2)],
-         [a("wt0", 128, 1152), a("wt1", 128, 1152), scratch(0, 0, 1), scratch(1, 0, 1)], [a("nil")], 2 ** 16)
+         [a("wt0", 128, 1152), a("wt1", 128, 1152), scratch(0), scratch(1)], [a("nil")], 2 ** 16 + 256 * ROW)
+    asel(a("up1"), a("gm"), [[1, 128]], Op.is_equal, -1, -1)
+    ts(a("upk"), a("up1"), 4096.0, Op.mult)
     ts(a("li"), a("pi"), 15, Op.bitwise_and)
     copy(a("lf"), a("li"))
     ts(a("l15"), a("lf"), 15.0, Op.is_equal)
-    ts(a("l16"), a("lf"), 16.0, Op.mult)
     copy(a("z1", 15, 143, 16), a("gm", 0, 128, 16))
     ts(a("s15"), a("gm"), a("l15", 0, 1), Op.mult)
     copy(a("idf"), a("idn"))
     ts(a("s5k"), a("s15"), 4096.0, Op.mult)
     ts(a("idk"), a("idn"), 4096.0, Op.mult)
-    for z, w in (("zd", 2.0 ** 17), ("zw", -4096.0)) + ((("zr", 2.0 ** 18), ("zn", -(2.0 ** 17))) if RELU else ()):
+    ts(a("id1k"), a("idn"), 1024.0, Op.mult)
+    if APART:
+        asel(a("idm"), a("neg", 0, 128), [[1, 128]], Op.is_equal, 0, -1)
+    for z, w in (("zd", 2.0 ** 17), ("zw", -4096.0)) + ((("zm", -1.0),) if len(SIGN) < 2 else ()) + ((("zr", 2.0 ** 18), ("zn", -(2.0 ** 17))) if RELU else ()):
         ts(a(z), a("z1"), w, Op.mult)
     ts(a("zk"), a("z1", 15, 143), 4096.0, Op.mult)
     vec(lambda: V.memset(T.cj[0:64, :], -15.0 * 2 ** 17), a("cj"), [], 0.5)
@@ -188,125 +238,213 @@ def rank_program(g, core, T, topo):
     for sb in range(2):
         ts(a("lutf", sb, 256, 4), a("i4", 64 * sb, 64 * sb + 64), 0.0, Op.is_equal, 4096.0, Op.mult)
         ts(a("lutk", sb, 256, 4), a("i4", 128, 192), 0.0, Op.is_equal, 4096.0, Op.mult)
-    copy(a("bl"), a("iq", 0, 8))
-    ts(a("c16"), a("iq", 0, 8), 256.0, Op.mult, a("l16", 0, 1), Op.add)
+    copy(a("bl"), a("iq"))
+    ts(a("c16"), a("iq", 0, 4), 16.0, Op.mult, a("lf", 0, 1), Op.add)
     copy(a("gmf"), a("gm"))
     for u in range(2):
-        ts(a("rs", 72 * u + 16, 72 * u + 72, 18), a("c16", 0, 4), 2.0 ** -14, Op.mult)
+        ts(a("rs", 72 * u + 16, 72 * u + 72, 18), a("c16"), 2.0 ** -10, Op.mult, -0.0625, Op.add)
 
-    def half(name, h, w=128):
-        return a(name, w * h, w * h + w)
-
-    def cb(h, lo, hi):
-        return a(("c0", "c1_")[h], lo, hi)
-
-    def lanes(out, z, src, c, w, first, end):
+    def lanes(out, z, src, c, first, end, lo=0, w=16, cut=False, n=4):
         for i in range(16):
-            mm(out, a(z, 15 - i, 143 - i), a3(src, 4 * c, 4 * c + 4, 16 * i, 16 * i + w), first and i == 0, end and i == 15)
+            mm(out, a(z, 15 - i, 143 - i), a3(src, 4 * c, 4 * c + n, lo + 16 * i, lo + 16 * i + w), first and i == 0, end and i == 15, cut and i == 0)
+
+    def wide(out, z, src, c, u, alone):
+        for i in range(16):
+            mm(out, a(z, 15 - i, 143 - i), a3(src, 2 * c, 2 * c + 2, 256 * u + 16 * i, 256 * u + 16 * i + 16), alone and i == 0, alone and i == 15, i == 0)
+
+    def lists(out, src, lo, hi):
+        for i in range(16):
+            mm(out, a("z1", 15 - i, 143 - i), a(src, lo + i, hi, 16), i == 0, i == 15)
 
     def half_round(t, h):
         last = t == RO - 1
-        k16, p16, sel, m, nr, wt = ["%s%d" % (x, h) for x in ("k16_%d_" % t, "p16_%d_" % t, "sel", "m", "nr", "wt")]
-        l8, pk16, n16 = half("l8", h, 8), a("pn16", 16 * h, 16 * h + 8), a("pn16", 16 * h + 8, 16 * h + 16)
-        p_sum = a("mc", 256 + 128 * h, 384 + 128 * h)
+        k16, sel, m, nr, wt = ["%s%d" % (x, h) for x in ("k16_%d_" % t, "sel", "m", "nr", "wt")]
+        p16 = "p16_%d" % t
+        cb = ("c0", "c1_")[h]
+        l8 = half("l8", h, 8)
+        pk16, kk16, n16 = [half("pn16", 3 * h + u, 8) for u in range(3)]
+        pack, factor = (("e3", 128 * h), half("e3", 2 + h)) if EB == 3 else ((m, 128), a(m, 320, 448))
 
+        mm(a(cb, 0, 128), a("ones"), a("cj"), True, False, holds=a(cb))
         for c in (2 * h, 2 * h + 1):
             relu = (c + 2) % 4 in RELU
-            act(a("sg", 1024 * c, 1024 * c + 1024), ind(table, half(k16, c % 2, 64)), AF.Copy)
-            if c in BEHIND:
-                tasks[-1]["calls"][0][2].append(a3("a3", 4 * BEHIND[c], 4 * BEHIND[c] + 4))
+            for lo, hi in PIECES.get(c, ((0, 4),)):
+                act(a("yg", 1024 * c + 256 * lo, 1024 * c + 256 * hi),
+                    ind(table, a(p16, 64 * c + 16 * lo, 64 * c + 16 * hi) if FIRST[h] == "p" else a(k16, 64 * (c % 2) + 16 * lo, 64 * (c % 2) + 16 * hi)), AF.Copy)
+                if c in BEHIND:
+                    tasks[-1]["calls"][0][2].append(a3("a3", 4 * BEHIND[c], 4 * BEHIND[c] + 4))
+            if LONG:
+                for q in (2 * c, 2 * c + 1):
+                    tt(row("d2", q), ind(table, half(k16, q % 4, 32)), half("yg", q, 512), Op.subtract)
+                if relu:
+                    ts(a3("a2", 2 * c, 2 * c + 2), a3("d2", 2 * c, 2 * c + 2), 0.0, Op.max)
+                else:
+                    act(a3("a2", 2 * c, 2 * c + 2), a3("d2", 2 * c, 2 * c + 2), AF.Abs)
+                for u in range(2):
+                    s = 2 * u + c % 2
+                    wide(half(m, 10 + s, 32), "z1", "d2", c, u, True)
+                    if relu:
+                        wide(half(cb, s, 32), "zn", "d2", c, u, False)
+                    wide(half(cb, s, 32), "zr" if relu else "zd", "a2", c, u, False)
+                continue
             for q in range(4 * c, 4 * c + 4):
-                tt(row("d3", q), ind(table, half(p16, q % 8, 16)), half("sg", q, 256), Op.subtract)
+                tt(row("d3", q), ind(table, half(k16, q % 8, 16) if FIRST[h] == "p" else half(p16, q, 16)), half("yg", q, 256), Op.subtract)
+            for lo, hi in PARTS.get(c, ((0, 4),)):
+                if relu:
+                    ts(a3("a3", 4 * c + lo, 4 * c + hi), a3("d3", 4 * c + lo, 4 * c + hi), 0.0, Op.max)
+                else:
+                    act(a3("a3", 4 * c + lo, 4 * c + hi), a3("d3", 4 * c + lo, 4 * c + hi), AF.Abs)
+            if "t%d" % h not in WHOLE and h in SIGN:
+                lanes(half(m, 5 + c % 2, 64), "z1", "d3", c, True, True)
             if relu:
-                ts(a3("a3", 4 * c, 4 * c + 4), a3("d3", 4 * c, 4 * c + 4), 0.0, Op.max)
-            else:
-                act(a3("a3", 4 * c, 4 * c + 4), a3("d3", 4 * c, 4 * c + 4), AF.Abs)
-            o = cb(h, 64 * (c % 2), 64 * (c % 2) + 64)
-            mm(o, a("ones"), a("cj", 0, 64), True, False)
-            if relu:
-                lanes(o, "zn", "d3", c, 16, False, False)
-            lanes(o, "zr" if relu else "zd", "a3", c, 16, False, False)
-            lanes(o, "z1", "d3", c, 16, False, True)
+                lanes(half(cb, c % 2, 64), "zn", "d3", c, False, False, cut=True)
+            if "d%d" % h not in WHOLE:
+                lanes(half(cb, c % 2, 64), "zr" if relu else "zd", "a3", c, False, False, cut=True)
+            if h not in SIGN:
+                lanes(half(cb, c % 2, 64), "zm", "d3", c, False, False, cut=True)
+        if "t%d" % h in WHOLE:
+            lanes(a(m, 320, 448), "z1", "d3", 2 * h, True, True, n=8)
+        if "d%d" % h in WHOLE:
+            lanes(half(cb, 0), "zd", "a3", 2 * h, False, False, cut=True, n=8)
+        if h in SIGN:
+            act(half("sn", h), a(m, 320, 448), AF.Sign, scale=-1.0 if FIRST[h] == "p" else 1.0, bias=0.5)
+            mm(a(cb, 0, 128), a("id1k"), half("sn", h), False, True, cut=True)
+        else:
+            mm(a(cb, 0, 128), a("idn"), a("lutm", 0, 128), False, True, cut=True)
 
-        ts(half("kp", h), a(k16), 32.0, Op.add)
-        for u, (x, y) in enumerate((("s15", "s5k"), ("idf", "idk"))):
-            mm(half("mc", 2 * h + u, 64), a(x), half("kp", 2 * h, 64), True, False)
-            mm(half("mc", 2 * h + u, 64), a(y), half("kp", 2 * h + 1, 64), False, True)
-        act(a(wt, 0, 128), half("mc", h), AF.Copy, bias=-32.0 * 4097)
+        early = len(tasks)
+        turn(half("kh", h), a(k16), "kh")
+        for u, (x, y) in enumerate((("s15", "s5k"), ("idn", "idk"))):
+            o = a(pack[0], pack[1] + 64 * u, pack[1] + 64 * u + 64)
+            mm(o, a(x), half("kh", 2 * h, 64), True, False)
+            mm(o, a(y), half("kh", 2 * h + 1, 64), False, True)
+        act(a(wt, 0, 128), a(pack[0], pack[1], pack[1] + 128), AF.Copy)
         w, k = T[wt], T["kd%d" % h]
-        dmas("y", "kd%d" % h, [(k[:, 1:17, :], w[:, 64:128]), (k[:, 17:33, :], w[:, 0:64])], [scratch(h, 1, 33)], [a(wt, 0, 128)], 2 ** 16)
-        dmas("y", "wd%d" % h, [(w[j:128:16, 128:1152], k[:, 1 + j:17 + j, :]) for j in range(1, 16)] + [(w[:, 2176:2240], k[:, 0:16, :])],
-             [a(wt, 128, 2240)], [scratch(h, 0, 33)], 2 ** 19)
+        dmas("y", "kd%d" % h, [(k[:, 1:17, :], w[:, 64:128]), (k[:, 17:33, :], w[:, 0:64])], [scratch(h)], [a(wt, 0, 128)], 2 ** 16 + 256 * ROW)
+        dmas("y", "wd%d" % h, [(w[j:128:16, 128:1152], k[:, 1 + j:17 + j, :]) for j in range(1, 16)] + ([(w[:, 2112:2176], k[:, 0:16, :])] if NONE == "y" else []),
+             [a(wt, 128, 2176 if NONE == "y" else 1152)], [scratch(h)], 2 ** 19 + 240 * ROW)
+        if NONE != "y":
+            mm(a(m, 448, 512), a("up1"), half("kh", 2 * h, 64), True, False)
+            mm(a(m, 448, 512), a("upk"), half("kh", 2 * h + 1, 64), False, True)
+            if NONE == "s":
+                act(a(wt, 2112, 2176), a(m, 448, 512), AF.Copy)
+            else:
+                copy(a(wt, 2112, 2176), a(m, 448, 512))
 
-        copy(half("ph_", h), a(p16))
-        mm(p_sum, a("idn"), half("ph_", h), True, True)
-        scan(half("mi", h), a("rst"), cb(h, 0, 128), 1e9, Op.max, Op.min)
-        ts(half("cl", h, 8), a("mi", 128 * h + 15, 128 * h + 128, 16), LOW, Op.max, a("thr"), Op.min)
+        for x in tasks[early:]:
+            x["lead"] = LEAD
+
+        turn(half("ph_", h), half(p16, h), "ph")
+        scan(half("mi", h), a("rst"), a(cb, 0, 128), 1e9, Op.max, Op.min)
+        if LONG:
+            for u in range(2):
+                ts(a("cl", 8 * h + u, 8 * h + 8, 2), a("mi", 128 * h + 64 * u + 15, 128 * h + 64 * u + 64, 16), LOW, Op.max, a("thr"), Op.min)
+        else:
+            ts(half("cl", h, 8), a("mi", 128 * h + 15, 128 * h + 128, 16), LOW, Op.max, a("thr"), Op.min)
         ts(half("v8", h, 8), half("cl", h, 8), 11, Op.arith_shift_right, 255, Op.bitwise_and)
         copy(l8, half("v8", h, 8))
-        tt(a(sel, 128, 256), ind(a("lutf"), l8), half("ph_", h), Op.min)
-        tt(a(sel, 0, 128), ind(a("lutk"), l8), half("ph_", h), Op.min)
-        mm(a(m, 0, 64), a("z1", 15, 143), a(sel, 128, 192), True, True)
-        mm(a(m, 64, 128), a("zk"), a(sel, 192, 256), True, True)
+        tt(half(sel, 2), ind(a("lutf"), l8), half("ph_", h), Op.min)
+        tt(half(sel, 0), ind(a("lutk"), l8), half("ph_", h), Op.min)
+        tt(half(sel, 1), ind(a("lutk"), l8), half("kh", h), Op.min)
+        mm(a(m, 0, 64), a("z1", 15, 143), a(sel, 256, 320), True, True)
+        mm(a(m, 64, 128), a("zk"), a(sel, 320, 384), True, True)
         mm(a(m, 128, 256), a("idn"), a("tm"), True, False)
-        mm(a(m, 128, 256), a("gm"), a(sel, 0, 128), False, True)
-        for i in range(16):
-            mm(a(m, 256, 272), a("z1", 15 - i, 143 - i), a(sel, i, 256, 16), i == 0, i == 15)
-        copy(half("pn16", h, 16), a(m, 256, 272))
+        mm(a(m, 128, 256), a("gm"), half(sel, 0), False, True)
+        if HEADS:
+            lists(a(cb, 272, 280), sel, 256, 384)
+            copy(n16, a(cb, 272, 280))
+            lists(a(m, 256, 272), sel, 0, 256)
+            copy(a("pn16", 24 * h, 24 * h + 16), a(m, 256, 272))
+        else:
+            lists(a(m, 256, 280), sel, 0, 384)
+            copy(half("pn16", h, 24), a(m, 256, 280))
         act(a(nr), a(m, 0, 264), AF.Copy)
 
         act(half("xn", h), ind(table, n16), AF.Copy)
-        mm(cb(h, 384, 512), half("xn", h), a("idn"), True, True)
-        act(half("xr", h), cb(h, 384, 512), AF.Copy)
-        for b in range(4 * h, 4 * h + 4):
-            e = a("e%d" % ((8 * t + (b + 4) % 8) % 3))
-            mm(e, a("idn"), half("sg", b, 512), True, False)
-            mm(e, half("xr", h), half("ex", b % 4, 512), False, True)
-            act(a3("ae", 2 * b, 2 * b + 2, 0, 256), e, AF.Abs)
-            if b % 2:
-                lanes(cb(h, 128 + 72 * (b // 2 % 2), 200 + 72 * (b // 2 % 2)), "z1", "ae", b // 2, 18, True, True)
-        act(half("sc", h, 144), cb(h, 128, 272), AF.Sign, bias=-1039.5)
-        act(a("sc", 144 * h + 16, 144 * h + 144, 18), a(nr, 256, 264), AF.Copy, scale=33.0 / 2 ** 17)
-        scan(half("ms", h, 144), half("sc", h, 144), a("rs"), 100.0, Op.min, Op.add)
-        ts(half("o16", h, 8), a("ms", 144 * h + 16, 144 * h + 144, 18), 1024.0, Op.mult, 2176.0, Op.add)
-        tt(half("fr", h), ind(a(wt), half("o16", h, 8)), a(nr, 0, 128), Op.add)
-        ts(half("fu", 2 * h, 64), half("fr", 2 * h, 64), 4095, Op.bitwise_and)
-        ts(half("fu", 2 * h + 1, 64), half("fr", 2 * h + 1, 64), 12, Op.logical_shift_right)
-        if last:
-            copy(half("yk32", h), half("fu", h))
-            dmas("y", "ok%d" % h, [(T.yk[:, 128 * h:128 * h + 128], half("yk32", h)[0])], [], [half("yk32", h)], 2 ** 16)
+        mm(a(cb, 384, 512), half("xn", h), a("idn"), True, True)
+        act(half("xr", h), a(cb, 384, 512), AF.Copy)
+        if "fl" in POOL:
+            turn(a("fl", 144 * h, 144 * h + 144, 18), a(nr, 256, 264), "fl")
         else:
-            copy(a("ks_%d_%d" % (t, h)), half("fu", h))
-            send("k", t, h, nxt, prv)
+            act(a("fl", 144 * h, 144 * h + 144, 18), a(nr, 256, 264), AF.Copy, bias=4096.0)
+        for b in range(4 * h, 4 * h + 4):
+            e = half("e%d" % (b // 2 % 2), b % 2, 512) if WIDE else a("e%d" % ((8 * t + (b + 4) % 8) % EB))
+            mm(e, a("idn"), half("yg", b, 512), True, False)
+            if FIRST[h] == "p":
+                mm(e, a("idn"), row("d2", b) if LONG else a3("d3", 2 * b, 2 * b + 2), False, False)
+            mm(e, half("xr", h), half("ex", b % 4, 512), False, True, cut=True)
+            if not WIDE:
+                act(a3("ae", 2 * b, 2 * b + 2, 16, 272), e, AF.Abs)
+            elif b % 2:
+                act(a3("ae", 2 * b - 2, 2 * b + 2, 16, 272), a(e[1]), AF.Abs)
+            if b % 2 and "e%d" % h not in WHOLE:
+                o = a(cb, 128 + 72 * (b // 2 % 2), 200 + 72 * (b // 2 % 2))
+                mm(o, a("idn"), half("fl", b // 2, 72), True, False)
+                if "fl" in POOL:
+                    mm(o, a("idn"), a("fk"), False, False)
+                lanes(o, "z1", "ae", b // 2, False, True, 15, 18)
+        if "e%d" % h in WHOLE:
+            mm(a(cb, 128, 272), a("idn"), half("fl", h, 144), True, False)
+            lanes(a(cb, 128, 272), "z1", "ae", 2 * h, False, True, 15, 18, n=8)
+        parts = 2 if h in QUART and not last else 1
+        for u in range(parts):
+            n, v = 2 // parts, parts * h + u
+            sums = a(cb, 128 + 72 * u, 128 + 72 * (u + n))
+            if NEARV:
+                ts(half("sc", v, 72 * n), sums, 1040.0, Op.is_lt, -2.0, Op.mult)
+            else:
+                act(half("sc", v, 72 * n), sums, AF.Sign, bias=-1039.5)
+            scan(half("ms", v, 72 * n), half("sc", v, 72 * n), a("rs", 0, 72 * n), 100.0, Op.min, Op.add)
+            ts(half("o16", v, 4 * n), a("ms", 72 * n * v + 16, 72 * n * (v + 1), 18), 1024.0, Op.mult, 2176.0 + 1024 * NEARV, Op.add)
+            tt(half("fr", v, 64 * n), ind(a(wt), half("o16", v, 4 * n)), half(nr, u, 64 * n), Op.add)
+            if u == 0:
+                ts(half("fu", 2 * h, 64), half("fr", 2 * h, 64), 4095, Op.bitwise_and)
+            if u == parts - 1:
+                ts(half("fu", 2 * h + 1, 64), half("fr", 2 * h + 1, 64), 12, Op.logical_shift_right)
+            if last:
+                copy(half("yk32", h), half("fu", h))
+                dmas("y", "ok%d" % h, [(T.yk[:, 128 * h:128 * h + 128], half("yk32", h)[0])], [], [half("yk32", h)], 2 ** 16)
+            else:
+                turn(half("ks_%d_%d" % (t, h), u, 64 * n), half("fu", v, 64 * n), "ks")
+                send(half("k16_%d_%d" % (t + 1, h), u, 64 * n), half("ks_%d_%d" % (t, h), u, 64 * n), "k%d_%d" % (t + 1, 2 * h + u), nxt, prv)
 
-        tt(half("pa", h), ind(a("lutm"), l8), half("kp", h), Op.min)
-        tt(half("pt", h), half("pa", h), p_sum, Op.mult)
+        tt(half("pa", h), ind(a("lutm"), l8), half("kh", h), Op.min)
+        mm(factor, a("ones"), a("qu"), True, False)
+        mm(factor, a("idn"), half("pa", h), False, True)
+        tt(half("pt", h), half("ph_", h), factor, Op.mult)
         ts(half("pn", h), half("pt", h), 5, Op.logical_shift_right, 2047, Op.bitwise_and)
         if last:
             copy(half("yp32", h), half("pn", h))
             dmas("y", "op%d" % h, [(T.yp[:, 128 * h:128 * h + 128], half("yp32", h)[0])], [], [half("yp32", h)], 2 ** 16)
         else:
-            copy(a("ps_%d_%d" % (t, h)), half("pn", h))
-            send("p", t, h, prv, nxt)
+            turn(half("ps_%d" % t, h), half("pn", h), "ps")
+            send(half("p16_%d" % (t + 1), h), half("ps_%d" % t, h), "p%d_%d" % (t + 1, h), prv, nxt)
 
-        ts(half("kk", h, 8), half("cl", h, 8), 13, Op.arith_shift_right, 15, Op.bitwise_and)
-        tt(half("ok", h, 8), half("kk", h, 8), a("c16"), Op.add)
-        copy(half("ok16", h, 8), half("ok", h, 8))
-        act(half("sk", h), ind(half("sg", h, 2048), half("ok16", h, 8)), AF.Copy)
-        tt(half("dk", h), ind(table, pk16), half("sk", h), Op.subtract)
-        act(half("adk", h), half("dk", h), AF.Abs)
+        act(half("yk_", h), ind(table, pk16), AF.Copy)
+        if APART:
+            act(half("dk", h), ind(table, kk16), AF.Copy)
+            mm(a(m, 320, 448), a("idn"), half("dk", h), True, False)
+            mm(a(m, 320, 448), a("idm"), half("yk_", h), False, True)
+            act(half("adk", h), a(m, 320, 448), AF.Abs)
+        else:
+            tt(half("dk", h), ind(table, kk16), half("yk_", h), Op.subtract)
+            act(half("adk", h), half("dk", h), AF.Abs)
         ts(half("c1", h), half("adk", h), 32.0, Op.is_le, 128.0, Op.mult)
         tt(half("wv", h), ind(table, pk16), half("c1", h), Op.subtract)
         ts(half("vv", h), half("wv", h), 0.0, Op.is_lt, 256.0, Op.mult)
         tt(half("eq", h), ind(a(nr, 256, 264), a("bl")), a(nr, 128, 256), Op.is_equal)
-        mm(a(m, 272, 280), a("idf"), a(nr, 256, 264), True, False)
+        mm(a(m, 280, 288), a("idf"), a(nr, 256, 264), True, False)
         for i in range(16):
-            mm(a(m, 272, 280), a("zw", 15 - i, 143 - i), a("eq", 128 * h + i, 128 * h + 128, 16), False, i == 15)
-        ts(a("w16", 16 * h, 16 * h + 16, 2), a(m, 272, 280), 16.0, Op.add, a("lf", 0, 1), Op.max)
+            mm(a(m, 280, 288), a("zw", 15 - i, 143 - i), a("eq", 128 * h + i, 128 * h + 128, 16), False, i == 15)
+        ts(a("w16", 16 * h, 16 * h + 16, 2), a(m, 280, 288), 16.0, Op.add, a("lf", 0, 1), Op.max)
 
     for t in range(RO):
+        now_[0] = t
         for h in (1, 0):
+            start = len(tasks)
             half_round(t, h)
+            for x in tasks[start:]:
+                x["lead"] = x.get("lead", 0) + h * AHEAD[t]
         for q in range(15, -1, -1):
             tt(ind(a("xt"), a("w16", 2 * q, 2 * q + 1)), half("wv", q, 16), half("vv", q, 16), Op.add)
         if t == RO - 1:
@@ -331,17 +469,18 @@ def rank_program(g, core, T, topo):
         for kind, lst in (("w", outs), ("r", ins)):
             for x in lst:
                 e = hist.setdefault(x[1], [])
-                e[:] = [y for y in e if not (y[1] >= x[2] and y[2] <= x[3] and (kind == "w" or y[0] == "r" and y[3] == q != "dma"))]
+                if kind == "w":
+                    e[:] = [y for y in e if not (y[1] >= x[2] and y[2] <= x[3])]
                 e.append((kind, x[2], x[3], q, who))
 
     hist = {}
     for n, x in enumerate(tasks):
         q = x["q"] if x["kind"] == "call" else "dma"
-        x["needs"], x["next"], x["banks"], at = {}, [], set(), 0
+        x["needs"], x["gaps"], x["next"], x["banks"], at = {}, {}, [], set(), 0
         for call, outs, ins, cost in x["calls"]:
             for who, free in clash(hist, q, outs, ins, False):
-                if who != n:
-                    x["needs"][who] = max(x["needs"].get(who, -1e9), (0 if free else HOP) - at)
+                if who != n and (0 if free else HOP) - at > x["needs"].get(who, -1e9):
+                    x["needs"][who], x["gaps"][who] = (0 if free else HOP) - at, (0 if free else HOP, at)
             note(hist, q, outs, ins, n)
             x["banks"].update(y[1] for y in outs + ins if y[1] in PSUM)
             at += cost
@@ -353,15 +492,15 @@ def rank_program(g, core, T, topo):
 
     def in_order(needs, nexts, key):
         order, open_ = [], [len(x) for x in needs]
-        ready = [n for n, k in enumerate(open_) if not k]
+        ready = [(key(n), n) for n, k in enumerate(open_) if not k]
         while ready:
-            n = min(ready, key=key)
-            ready.remove(n)
-            order.append(n)
-            for w in nexts[n]:
+            x = min(ready)
+            ready.remove(x)
+            order.append(x[1])
+            for w in nexts[x[1]]:
                 open_[w] -= 1
                 if not open_[w]:
-                    ready.append(w)
+                    ready.append((key(w), w))
         return order
 
     def place(needs, nexts, key, first):
@@ -369,14 +508,18 @@ def rank_program(g, core, T, topo):
         for n in in_order(needs, nexts, key):
             x = tasks[n]
             at = max([first[n]] + [end[w] + d for w, d in needs[n].items()])
-            held = sorted(busy.get(x["q"], []) + [(lo - HOP, hi + HOP) for b in x["banks"] for lo, hi, q in busy.get(b, []) if q != x["q"]])
-            for lo, hi in held:
+            held = busy.get(x["q"], []) + [(lo - HOP, hi + HOP) for b in x["banks"] for lo, hi, q in busy.get(b, []) if q != x["q"]]
+            if x["moves"]:
+                held += [(lo - sum(x["moves"]) + x["cost"], hi - x["moves"][0]) for lo, hi in busy.get("engines", [])]
+            for lo, hi in sorted(held):
                 if hi > at:
                     if lo >= at + x["cost"]:
                         break
                     at = hi
             end[n] = at + x["cost"]
             busy.setdefault(x["q"], []).append((at, end[n]))
+            if x["moves"]:
+                busy.setdefault("engines", []).append((at + x["moves"][0], at + sum(x["moves"])))
             for b in x["banks"]:
                 busy.setdefault(b, []).append((at, end[n], x["q"]))
         return end
@@ -384,8 +527,71 @@ def rank_program(g, core, T, topo):
     way = [0] * len(tasks)
     for n in range(len(tasks) - 1, -1, -1):
         way[n] = tasks[n]["cost"] + max([tasks[n]["after"]] + [way[w] + d for w, d in behind[n].items()])
-    ends = place(before, behind, lambda n: -way[n], [0] * len(tasks))
+    ends = place(before, behind, lambda n: -way[n] - tasks[n].get("lead", 0), [0] * len(tasks))
     order = in_order(before, behind, lambda n: ends[n] - tasks[n]["cost"])
+
+    def length(order, slow, far, pe):
+        end, free, bank, engines, gone, last = [0] * len(tasks), dict.fromkeys(Q, 0), {}, 0, 0, 0
+        for n in order:
+            q, cost, after, needs, banks, moves, gate = brief[n]
+            at = free[q]
+            for w, d, e in needs:
+                at = max(at, end[w] + d * far - e * slow * pe)
+            for b in banks:
+                if b in bank and bank[b][0] != q:
+                    at = max(at, bank[b][1] + HOP * far)
+            if moves:
+                at = max(at, gone if gate else 0)
+                free[q] = at + cost * far
+                at = max(at, engines - moves[0] * far)
+                engines = at + sum(moves) * far
+                gone = engines + 2 * HOP * far if q == "g" else gone
+                end[n] = at + cost * far
+            else:
+                end[n] = free[q] = at + cost * slow * (pe if q == "p" else 1)
+            for b in banks:
+                bank[b] = (q, end[n])
+            last = max(last, end[n] + after * far)
+        return last
+
+    if MOVES and not PLAN:
+        brief = [(x["q"], x["cost"], x["after"], [(w, tasks[w]["after"] + d, e) for w, (d, e) in x["gaps"].items()], tuple(x["banks"]), x["moves"],
+                  GATE and x["kind"] == "dma" and x["calls"][0][0][0][0] == "w") for x in tasks]
+        start = [ends[n] - x["cost"] for n, x in enumerate(tasks)]
+        step, seen_, table_ = [], {}, {}
+        for n, x in enumerate(tasks):
+            o = (x["calls"][0][1] + x["calls"][0][2])[0]
+            name = (x["q"], o[1][0] if o[1] in PSUM[:EB] else o[1][:2] + o[1][5:].strip("0123")[:0] + o[1][-2:] * (o[1][0] == "k") if "_" in o[1][2:-1] else o[1],
+                    o[2], x["round"] < 0)
+            seen_[name, x["round"]] = seen_.get((name, x["round"]), 0) + 1
+            step.append(name + (seen_[name, x["round"]],))
+        first = [min(start[n] for n, x in enumerate(tasks) if x["round"] == t and step[n][1] == "yg") for t in range(RO)]
+        period = first[2] - first[1]
+        for t in (3, 0, 2, 1, -1):
+            table_.update({step[n]: start[n] - first[max(t, 0)] for n, x in enumerate(tasks) if x["round"] == t})
+        names, one = sorted(table_), [step[n] for n, x in enumerate(tasks) if x["round"] == 1]
+
+        def tried():
+            key = [table_[step[n]] + period * max(x["round"], 0) for n, x in enumerate(tasks)]
+            o = in_order(before, behind, lambda n: key[n])
+            return sum(length(o, *x) / sum(x[:2]) for x in SPEEDS), o
+
+        best = now = tried()
+        rng = np.random.default_rng(SEED)
+        for n in range(MOVES):
+            at, many = int(rng.integers(len(one))), int(rng.integers(2, 12))
+            moved = [names[int(rng.integers(len(names)))]] if rng.random() < 0.6 else set(one[at:at + many])
+            by = rng.normal() * (150, 500, 1500)[int(rng.integers(3))]
+            for x in moved:
+                table_[x] += by
+            new = tried()
+            if new[0] <= now[0] + 15 * (1 - n / MOVES) * rng.exponential():
+                now, best = new, min(best, new)
+            else:
+                for x in moved:
+                    table_[x] -= by
+        PLAN.extend(best[1])
+    order = PLAN or order
 
     hist, seen, known, count, left = {}, {q: {} for q in Q}, {}, {}, []
 
@@ -410,6 +616,8 @@ def rank_program(g, core, T, topo):
                 call().then_inc(T.sem[q], 1)
             elif kind == "dma":
                 sem = call[0]
+                if GATE and sem[0] == "w":
+                    waits(q, [(x, False) for x in left])
                 for out, in_ in call[1]:
                     Q[q].dma_start(out, in_).then_inc(T.sem[sem], 16)
                     count[sem] = count.get(sem, 0) + 16

@@ -6,59 +6,59 @@ F, B, H, I, U = "float32", "bfloat16", "float16", "int32", "uint16"
 SCRATCH = {}
 for _n, _w, _d in (
         ("xt", 2064, B), ("nk", 256, I), ("np_", 256, I), ("yg", 4096, B), ("ph_", 256, H), ("kh", 256, H), ("sn", 256, B),
-        ("mi", 256, F), ("cl", 16, I), ("v8", 16, I), ("l8", 16, U), ("sel0", 384, H), ("sel1", 384, H), ("pn16", 48, U),
-        ("nr0", 264, F), ("nr1", 264, F), ("xn", 256, B), ("xr", 256, B), ("eq", 256, B), ("w16", 32, U),
+        ("mi", 256, F), ("cl", 16, I), ("v8", 16, I), ("l8", 16, U), ("sel", 768, H),
+        ("nr", 528, F), ("xn", 256, B), ("xr", 256, B), ("eq", 256, B), ("mw", 256, F), ("w16", 32, U),
         ("yk_", 256, B), ("dk", 256, B), ("adk", 256, B), ("c1", 256, B),
         ("wv", 256, B), ("vv", 256, B), ("pa", 256, H), ("pt", 256, I), ("pn", 256, I), ("yp32", 256, F),
-        ("wt0", 2176, F), ("wt1", 2176, F), ("fl", 288, B), ("fk", 72, B), ("sc", 288, B), ("ms", 288, F), ("o16", 16, U), ("fr", 256, I), ("fu", 256, I),
+        ("wt0", 1216, F), ("wt1", 1216, F), ("fl", 288, B), ("ms", 288, F), ("o16", 16, U), ("fr", 256, I), ("fu", 256, I),
         ("yk32", 256, F), ("jk", 16, B), ("ac", 4, F), ("aa", 1, I), ("ab", 1, I), ("thr", 1, F),
         ("pi", 2, I), ("li", 2, I), ("lf", 2, F), ("l15", 2, F), ("ones", 128, B), ("neg", 512, B), ("gm", 128, B), ("idn", 128, B),
-        ("idf", 128, F), ("idk", 128, B), ("id1k", 128, B), ("gmf", 128, F), ("s15", 128, B), ("s5k", 128, B), ("qu", 128, B), ("up1", 128, B), ("upk", 128, B),
-        ("z1", 143, B), ("zd", 143, B), ("zr", 143, B), ("zn", 143, B), ("zw", 143, B), ("zk", 128, B), ("zm", 143, B), ("idm", 128, B),
-        ("cj", 128, B), ("rst", 128, F), ("rs", 144, F), ("ex", 2048, B), ("tm", 128, B), ("ij", 128, I), ("iq", 8, I),
-        ("bl", 8, U), ("c16", 4, F), ("i3", 192, I), ("i4", 192, I), ("nil", 64, F),
-        ("lutf", 256, B), ("lutk", 256, B), ("lutm", 256, B)):
+        ("idf", 128, F), ("idk", 128, B), ("gmf", 128, F), ("s15", 128, B), ("s5k", 128, B), ("i64", 128, B), ("qu", 128, B),
+        ("z1", 143, B), ("zd", 143, B), ("zb", 143, B), ("r0", 128, B),
+        ("cj", 128, B), ("rst", 128, F), ("ri", 144, I), ("rp", 144, F), ("ex", 2048, B), ("tm", 128, B), ("ij", 128, I), ("iq", 16, I),
+        ("bl", 16, U), ("i3", 192, I), ("i4", 192, I), ("nil", 64, F),
+        ("lutf", 256, B), ("lutk", 256, B), ("lutq", 256, B)):
     SCRATCH[_n] = ("sbuf", [128, _w], _d)
 for _n, _w in (("d3", 256), ("a3", 256), ("ae", 288)):
     SCRATCH[_n] = ("sbuf", [128, 16, _w], B)
-for _n in ("d2", "a2"):
-    SCRATCH[_n] = ("sbuf", [128, 8, 512], B)
+SCRATCH["pn16"] = ("sbuf", [128, 3, 16], U)
 for _h in range(2):
     SCRATCH["kd%d" % _h] = ("dram", [8, 33, 64], F)
 for _t in range(RO):
-    for _n, _w in (("k16_%d_0", 128), ("k16_%d_1", 128), ("p16_%d", 256)) + ((("ks_%d_0", 128), ("ks_%d_1", 128), ("ps_%d", 256)) if _t < RO - 1 else ()):
-        SCRATCH[_n % _t] = ("sbuf", [128, _w], U)
-WIDE = False
-NONE = "y"
-PSUM = ("e0", "e1") + (() if WIDE else ("e2", "e3")) + ("c0", "c1_", "m0", "m1")
+    for _n in ("k16_%d", "p16_%d") + (("ks_%d", "ps_%d") if _t < RO - 1 else ()):
+        SCRATCH[_n % _t] = ("sbuf", [128, 256], U)
+PSUM = ("e0", "e1", "e2", "e3", "c0", "c1_", "m0", "m1")
 for _n in PSUM:
-    SCRATCH[_n] = ("psum", [128, 1024 if WIDE and _n[0] == "e" else 512], F)
-SEMAPHORES = (["v", "s", "p", "g", "lx", "oy", "kz"] + [x + h for x in ("lp", "lk", "ok", "op", "kd", "wd") for h in "01"]
+    SCRATCH[_n] = ("psum", [128, 512], F)
+SEMAPHORES = (["v", "s", "p", "g", "lx", "oy", "kz"] + [x + h for x in ("lp", "lk", "kd", "wd") for h in "01"] + [x + h for x in ("ok", "op") for h in "0123"]
               + ["%s%s%d_%d" % (y, x, t, h) for x in "kp" for t in range(1, RO) for h in range(4) for y in "al"])
-RELU = (0,)
+NEARS = ((2, 4), (0, 2))
+PHAGES = ((2, 4), (0, 2))
+WRITES = ((2, 4), (0, 2))
+EQUAL = ((2, 4), (0, 2))
+RELU = (2,)
+WHOLE = (1,)
 BEHIND = {1: 2}
-GATE = False
-LEAD = 4000
-AHEAD = (0, 0, 0, 0)
-MOVES, SEED, PLAN = 9000, 3, []
-SPEEDS = ((1, 0.9, 0.85), (1.4, 0.7, 1.0), (1.5, 0.8, 1.0))
-EB = 3
-FIRST = "pp"
-WHOLE = ("t1",)
-QUART = ()
-HEADS = False
-NEARV = True
 PIECES = {2: ((0, 1), (1, 4)), 3: ((0, 1), (1, 4))}
-PARTS = {}
-SPLIT = True
-LONG = False
-APART = False
-SIGN = (0, 1)
-PICK = 88
-POOL = ("kh", "ph", "ps")
-LOW = -(2.0 ** 24) - 2048
-TOP = 63 * 2.0 ** 17 + 15 * 2.0 ** 13 + 4096
-HOP, CALL, ACT, GATHER, SCATTER, ISSUE, LOCAL, REMOTE, FAR, BYTES, MATMUL, COLUMN, ROWS, ROW = 176, 39.6, 76.95, 1.45, 3.5, 242.3, 1300, 588.06, 2800, 152, 9.9, 0.45, 3089.53, 237.18
+PARTS = {1: ((0, 2), (2, 4))}
+POOL = ("kh", "ph", "ps", "thr", "yp", "k0", "p0")
+AGAIN = True
+SPARE = ("idf", "gmf", "s5k", "idk", "zd", "zb", "i64", "ae", "rst", "lutf", "lutk")
+SIDE = ()
+FIRST = "pp"
+ONV = ()
+SUMS = ()
+AHEAD = {}
+LEAD = 4000
+EB = 3
+AIM, REACH, HEAT, WARM = 0.8, 8, 90, 600
+STEPS, MOVES, SEED, PLAN = 8000, 14000, 8, []
+APART, MILD, CLASS = 2000, 150, (0, 1, 1, 2)
+SPEEDS = ((1.05, 0.95, 0.85, 1.0, 1.0, 0.95), (1.25, 0.8, 1.1, 1.3, 0.95, 1.2), (1.4, 1.3, 1.0, 0.9, 1.0, 0.7), (1.55, 0.8, 1.1, 1.1, 0.92, 0.8),
+          (1.05, 1.5, 0.9, 0.8, 1.0, 1.3), (1.3, 0.7, 1.1, 0.75, 1.0, 0.6))
+LOW = -192 * 2.0 ** 19 + 8192
+HOP, CALL, PICK, ACT, GATHER, SCATTER, ISSUE, LOCAL, REMOTE, FAR, BYTES, MATMUL, COLUMN, ROWS, ROW = 176, 40, 88, 77, 1.45, 3.5, 242, 1300, 588, 2800, 152, 10, 0.45, 2000, 150
+INFO = {}
 
 
 def rank_program(g, core, T, topo):
@@ -73,6 +73,9 @@ def rank_program(g, core, T, topo):
         hi = SCRATCH[name][1][1] if hi is None else hi
         return (T[name][:, lo:hi] if step is None else T[name][:, lo:hi:step], name, lo, hi, len(range(lo, hi, step or 1)))
 
+    def back(name, lo, hi):
+        return (T[name][:, hi - 1:(lo - 1 if lo else None):-1], name, lo, hi, hi - lo)
+
     def a3(name, q0, q1, c0=None, c1=None):
         w = SCRATCH[name][1][2]
         return (T[name][:, q0:q1, :] if c0 is None else T[name][:, q0:q1, c0:c1], name, w * q0, w * q1, (q1 - q0) * (w if c0 is None else c1 - c0))
@@ -84,6 +87,12 @@ def rank_program(g, core, T, topo):
     def half(name, h, w=128):
         return a(name, w * h, w * h + w)
 
+    def part(name, c0, c1, w=64):
+        return a(name, w * c0, w * c1)
+
+    def names16(u, c0, c1):
+        return (T.pn16[:, u, 4 * c0:4 * c1], "pn16", 4 * c0, 4 * c1, 4 * (c1 - c0))
+
     def ind(win, off):
         return (win[0].indirect(off[0]), win, off)
 
@@ -93,18 +102,18 @@ def rank_program(g, core, T, topo):
             r += [x] if isinstance(x[1], str) else [x[1], x[2]]
         return r
 
-    tasks, now_ = [], [-1]
+    tasks, now_ = [], ["start", 0]
 
-    def task(q, kind, call, outs, ins, cost, after=0, more=False, moves=None):
+    def task(q, kind, call, outs, ins, cost, after=0, more=False, moves=None, picks=0):
         if not more:
-            tasks.append(dict(q=q, kind=kind, calls=[], after=after, moves=moves, round=now_[0]))
-        tasks[-1]["calls"].append((call, flat(outs), flat(ins), cost))
+            tasks.append(dict(q=q, kind=kind, calls=[], after=after, moves=moves, stage=now_[0], round=now_[1], lead=AHEAD.get(now_[0], 0), picks=picks))
+        tasks[-1]["calls"].append((call, flat(outs), flat(ins), cost + picks))
 
     def vec(fn, out, ins, rate):
         if isinstance(out[1], tuple):
-            task("v", "call", fn, [out[1]], ins + [out[2]], PICK + SCATTER * ins[0][4])
+            task("v", "call", fn, [out[1]], ins + [out[2]], PICK, picks=SCATTER * ins[0][4])
         elif ins and isinstance(ins[0][1], tuple):
-            task("v", "call", fn, [out], ins, PICK + GATHER * out[4])
+            task("v", "call", fn, [out], ins, PICK, picks=GATHER * out[4])
         else:
             task("v", "call", fn, [out], ins, CALL + max(64, rate * out[4]))
 
@@ -129,12 +138,15 @@ def rank_program(g, core, T, topo):
         vec(lambda: V.tensor_tensor_scan(out[0], d0[0], d1[0], first, op0, op1), out, [d0, d1], 1)
 
     def fill(out, val):
-        vec(lambda: V.memset(out[0], val), out, [], narrow(out))
+        if out[1] in SPARE:
+            act(out, a("neg", 0, out[4]), AF.Copy, scale=-val)
+        else:
+            vec(lambda: V.memset(out[0], val), out, [], narrow(out))
 
     def act(out, in_, func, acc=None, **kw):
-        cost = 80 + GATHER * out[4] if isinstance(in_[1], tuple) else ACT + out[4]
+        cost, picks = (80, GATHER * out[4]) if isinstance(in_[1], tuple) else (ACT + out[4], 0)
         if acc is None:
-            task("s", "call", lambda: S.activation(out[0], in_[0], func, **kw), [out], [in_], cost)
+            task("s", "call", lambda: S.activation(out[0], in_[0], func, **kw), [out], [in_], cost, picks=picks)
         else:
             task("s", "call", lambda: S.activation(out[0], in_[0], func, accum_out=acc[0], **kw), [out, acc], [in_], cost)
 
@@ -154,6 +166,12 @@ def rank_program(g, core, T, topo):
         else:
             copy(out, in_)
 
+    def fetch(out, in_, key, scale=1.0):
+        if key in ONV:
+            ts(out, in_, scale, Op.mult)
+        else:
+            act(out, in_, AF.Copy, scale=scale)
+
     def dmas(q, sem, pairs, outs, ins, size):
         task(q, "dma", (sem, pairs), outs, ins, ISSUE * len(pairs), max(LOCAL, LOCAL + size / BYTES - ISSUE * (len(pairs) - 1)),
              moves=(ISSUE + LOCAL / 2, size / BYTES))
@@ -168,18 +186,13 @@ def rank_program(g, core, T, topo):
 
     table = a("xt", 16, 2064)
 
-    if SPLIT:
-        dmas("s", "lp1", [(T.np_[:, 128:256], T.ph[:, 128:256])], [half("np_", 1)], [], 2 ** 16)
-        dmas("y", "lx", [(table[0], T.x0[:])], [table], [], 2 ** 19)
-        dmas("y", "lk0", [(T.nk[:], T.ka[:])], [a("nk")], [], 2 ** 17)
-        dmas("y", "lp0", [(T.np_[:, 0:128], T.ph[:, 0:128])], [half("np_", 0)], [], 2 ** 16)
-    else:
-        dmas("s", "lp0", [(T.np_[:], T.ph[:])], [a("np_")], [], 2 ** 17)
-        dmas("y", "lx", [(table[0], T.x0[:])], [table], [], 2 ** 19)
-        dmas("y", "lk0", [(T.nk[:], T.ka[:])], [a("nk")], [], 2 ** 17)
+    dmas("s", "lp1", [(T.np_[:, 128:256], T.ph[:, 128:256])], [half("np_", 1)], [], 2 ** 16)
+    dmas("y", "lx", [(table[0], T.x0[:])], [table], [], 2 ** 19)
+    dmas("y", "lk0", [(T.nk[:], T.ka[:])], [a("nk")], [], 2 ** 17)
+    dmas("y", "lp0", [(T.np_[:, 0:128], T.ph[:, 0:128])], [half("np_", 0)], [], 2 ** 16)
     for h in (1, 0):
-        copy(half("p16_0", h), half("np_", h))
-        copy(a("k16_0_%d" % h), half("nk", h))
+        turn(half("p16_0", h), half("np_", h), "p%d" % h)
+        turn(half("k16_0", h), half("nk", h), "k%d" % h)
 
     fill(a("ones"), 1.0)
     fill(a("neg"), -1.0)
@@ -188,263 +201,218 @@ def rank_program(g, core, T, topo):
     asel(a("gm"), a("gm"), [[16, 8], [0, 16]], Op.is_ge, 15, -1)
     asel(a("idn"), a("ones"), [[1, 128]], Op.is_equal, 0, -1)
     iota(a("ij"), [[0, 8], [1, 16]], 0, 0)
-    iota(a("iq"), [[1, 8]], 0, 0)
+    iota(a("iq"), [[520, 2], [1, 8]], 0, 0)
     iota(a("i3", 0, 64), [[1, 4], [1, 16]], 129, -1)
     iota(a("i3", 64, 128), [[-1, 4], [1, 16]], 127, -1)
     iota(a("i3", 128, 192), [[0, 4], [1, 16]], 128, -1)
+    iota(a("ri"), [[0, 2], [16, 4], [64, 18]], 64 - 2048, 0)
     for b in range(4):
         asel(a("ex", 512 * b, 512 * b + 512), a("neg"), [[1, 32], [0, 16]], Op.is_equal, 32 * b, -1)
     fill(a("nil"), 0.0)
     fill(a("z1"), 0.0)
     fill(a("qu"), 0.25)
-    fill(a("fl"), 0.0)
-    if "fl" in POOL:
-        fill(a("fk"), 0.0)
-        fill(a("fk", 0, 72, 18), 4096.0)
-    fill(a("rst"), -1e9)
-    fill(a("rst", 0, 128, 16), 1e9)
-    fill(a("thr"), TOP)
+    fill(a("fl"), -1040.0 * 4096)
+    fill(a("fl", 17, 288, 18), -2.0 ** 26)
+    fill(a("rst"), -4e9)
+    fill(a("rst", 0, 128, 16), 4e9)
+    fill(a("thr"), 0.0)
     fill(a("lutf"), 0.0)
     fill(a("lutk"), -512.0)
-    fill(a("lutm"), 0.0)
-    fill(a("lutm", 255, 256), 4096.0)
+    fill(a("lutq"), 0.0)
+    fill(a("lutq", 1, 2), -1.0)
     fill(a("w16"), 0)
+    fill(a("xt", 0, 16), 0.0)
+    fill(a("r0"), 1.0)
+    fill(a("r0", 0, 128, 16), 0.0)
     fill(a3("ae", 0, 16, 0, 16), 0.0)
     fill(a3("ae", 0, 16, 272, 288), 0.0)
-    fill(a("rs"), -0.0625)
-    fill(a("rs", 17, 144, 18), 100.0)
     dmas("y", "kz", [(T["kd%d" % h][:, 0, :], T.nil[0:8, :]) for h in range(2)] + [(T["wt%d" % h][0:128:16, 128:1152], T.nil[:]) for h in range(2)],
          [a("wt0", 128, 1152), a("wt1", 128, 1152), scratch(0), scratch(1)], [a("nil")], 2 ** 16 + 256 * ROW)
-    asel(a("up1"), a("gm"), [[1, 128]], Op.is_equal, -1, -1)
-    ts(a("upk"), a("up1"), 4096.0, Op.mult)
     ts(a("li"), a("pi"), 15, Op.bitwise_and)
     copy(a("lf"), a("li"))
     ts(a("l15"), a("lf"), 15.0, Op.is_equal)
     copy(a("z1", 15, 143, 16), a("gm", 0, 128, 16))
     ts(a("s15"), a("gm"), a("l15", 0, 1), Op.mult)
-    copy(a("idf"), a("idn"))
-    ts(a("s5k"), a("s15"), 4096.0, Op.mult)
-    ts(a("idk"), a("idn"), 4096.0, Op.mult)
-    ts(a("id1k"), a("idn"), 1024.0, Op.mult)
-    if APART:
-        asel(a("idm"), a("neg", 0, 128), [[1, 128]], Op.is_equal, 0, -1)
-    for z, w in (("zd", 2.0 ** 17), ("zw", -4096.0)) + ((("zm", -1.0),) if len(SIGN) < 2 else ()) + ((("zr", 2.0 ** 18), ("zn", -(2.0 ** 17))) if RELU else ()):
-        ts(a(z), a("z1"), w, Op.mult)
-    ts(a("zk"), a("z1", 15, 143), 4096.0, Op.mult)
-    vec(lambda: V.memset(T.cj[0:64, :], -15.0 * 2 ** 17), a("cj"), [], 0.5)
-    vec(lambda: V.tensor_scalar(T.cj[64:128, :], T.ij[64:128, :], 128.0, 32.0, Op.mult, Op.add), a("cj"), [a("ij")], 1)
-    ts(a("i4"), a("i3"), 15, Op.bitwise_and)
-    ts(a("tm"), a("ij"), a("lf", 0, 1), Op.is_le, 16384.0, Op.mult)
-    for sb in range(2):
-        ts(a("lutf", sb, 256, 4), a("i4", 64 * sb, 64 * sb + 64), 0.0, Op.is_equal, 4096.0, Op.mult)
-        ts(a("lutk", sb, 256, 4), a("i4", 128, 192), 0.0, Op.is_equal, 4096.0, Op.mult)
-    copy(a("bl"), a("iq"))
-    ts(a("c16"), a("iq", 0, 4), 16.0, Op.mult, a("lf", 0, 1), Op.add)
-    copy(a("gmf"), a("gm"))
-    for u in range(2):
-        ts(a("rs", 72 * u + 16, 72 * u + 72, 18), a("c16"), 2.0 ** -10, Op.mult, -0.0625, Op.add)
-
-    def lanes(out, z, src, c, first, end, lo=0, w=16, cut=False, n=4):
-        for i in range(16):
-            mm(out, a(z, 15 - i, 143 - i), a3(src, 4 * c, 4 * c + n, lo + 16 * i, lo + 16 * i + w), first and i == 0, end and i == 15, cut and i == 0)
-
-    def wide(out, z, src, c, u, alone):
-        for i in range(16):
-            mm(out, a(z, 15 - i, 143 - i), a3(src, 2 * c, 2 * c + 2, 256 * u + 16 * i, 256 * u + 16 * i + 16), alone and i == 0, alone and i == 15, i == 0)
-
-    def lists(out, src, lo, hi):
-        for i in range(16):
-            mm(out, a("z1", 15 - i, 143 - i), a(src, lo + i, hi, 16), i == 0, i == 15)
-
-    def half_round(t, h):
-        last = t == RO - 1
-        k16, sel, m, nr, wt = ["%s%d" % (x, h) for x in ("k16_%d_" % t, "sel", "m", "nr", "wt")]
-        p16 = "p16_%d" % t
-        cb = ("c0", "c1_")[h]
-        l8 = half("l8", h, 8)
-        pk16, kk16, n16 = [half("pn16", 3 * h + u, 8) for u in range(3)]
-        pack, factor = (("e3", 128 * h), half("e3", 2 + h)) if EB == 3 else ((m, 128), a(m, 320, 448))
-
-        mm(a(cb, 0, 128), a("ones"), a("cj"), True, False, holds=a(cb))
-        for c in (2 * h, 2 * h + 1):
-            relu = (c + 2) % 4 in RELU
-            for lo, hi in PIECES.get(c, ((0, 4),)):
-                act(a("yg", 1024 * c + 256 * lo, 1024 * c + 256 * hi),
-                    ind(table, a(p16, 64 * c + 16 * lo, 64 * c + 16 * hi) if FIRST[h] == "p" else a(k16, 64 * (c % 2) + 16 * lo, 64 * (c % 2) + 16 * hi)), AF.Copy)
-                if c in BEHIND:
-                    tasks[-1]["calls"][0][2].append(a3("a3", 4 * BEHIND[c], 4 * BEHIND[c] + 4))
-            if LONG:
-                for q in (2 * c, 2 * c + 1):
-                    tt(row("d2", q), ind(table, half(k16, q % 4, 32)), half("yg", q, 512), Op.subtract)
-                if relu:
-                    ts(a3("a2", 2 * c, 2 * c + 2), a3("d2", 2 * c, 2 * c + 2), 0.0, Op.max)
-                else:
-                    act(a3("a2", 2 * c, 2 * c + 2), a3("d2", 2 * c, 2 * c + 2), AF.Abs)
-                for u in range(2):
-                    s = 2 * u + c % 2
-                    wide(half(m, 10 + s, 32), "z1", "d2", c, u, True)
-                    if relu:
-                        wide(half(cb, s, 32), "zn", "d2", c, u, False)
-                    wide(half(cb, s, 32), "zr" if relu else "zd", "a2", c, u, False)
-                continue
-            for q in range(4 * c, 4 * c + 4):
-                tt(row("d3", q), ind(table, half(k16, q % 8, 16) if FIRST[h] == "p" else half(p16, q, 16)), half("yg", q, 256), Op.subtract)
-            for lo, hi in PARTS.get(c, ((0, 4),)):
-                if relu:
-                    ts(a3("a3", 4 * c + lo, 4 * c + hi), a3("d3", 4 * c + lo, 4 * c + hi), 0.0, Op.max)
-                else:
-                    act(a3("a3", 4 * c + lo, 4 * c + hi), a3("d3", 4 * c + lo, 4 * c + hi), AF.Abs)
-            if "t%d" % h not in WHOLE and h in SIGN:
-                lanes(half(m, 5 + c % 2, 64), "z1", "d3", c, True, True)
-            if relu:
-                lanes(half(cb, c % 2, 64), "zn", "d3", c, False, False, cut=True)
-            if "d%d" % h not in WHOLE:
-                lanes(half(cb, c % 2, 64), "zr" if relu else "zd", "a3", c, False, False, cut=True)
-            if h not in SIGN:
-                lanes(half(cb, c % 2, 64), "zm", "d3", c, False, False, cut=True)
-        if "t%d" % h in WHOLE:
-            lanes(a(m, 320, 448), "z1", "d3", 2 * h, True, True, n=8)
-        if "d%d" % h in WHOLE:
-            lanes(half(cb, 0), "zd", "a3", 2 * h, False, False, cut=True, n=8)
-        if h in SIGN:
-            act(half("sn", h), a(m, 320, 448), AF.Sign, scale=-1.0 if FIRST[h] == "p" else 1.0, bias=0.5)
-            mm(a(cb, 0, 128), a("id1k"), half("sn", h), False, True, cut=True)
+    for z, x, w in (("i64", "idn", -64.0),) * (len(SIDE) > 0) + (("idf", "idn", -1.0), ("gmf", "gm", 1.0), ("s5k", "s15", 4096.0), ("idk", "idn", 4096.0), ("zd", "z1", 2.0 ** 19), ("zb", "z1", 4096.0)):
+        if z in SPARE:
+            act(a(z), a(x), AF.Copy, scale=w)
         else:
-            mm(a(cb, 0, 128), a("idn"), a("lutm", 0, 128), False, True, cut=True)
+            ts(a(z), a(x), w, Op.mult)
+    vec(lambda: V.memset(T.cj[0:64, :], -16.0 * 2 ** 19), a("cj"), [], 0.5)
+    vec(lambda: V.tensor_scalar(T.cj[64:128, :], T.ij[64:128, :], 512.0, 320.0, Op.mult, Op.add), a("cj"), [a("ij")], 1)
+    ts(a("i4"), a("i3"), 15, Op.bitwise_and)
+    ts(a("tm"), a("ij"), a("lf", 0, 1), Op.is_ge, 16384.0, Op.mult)
+    for sb in range(2):
+        ts(a("lutf", 2 + sb, 256, 4), a("i4", 64 * sb, 64 * sb + 64), 0.0, Op.is_equal, 4096.0, Op.mult)
+        ts(a("lutk", 2 + sb, 256, 4), a("i4", 128, 192), 0.0, Op.is_equal, 4096.0, Op.mult)
+        ts(a("lutq", 2 + sb, 256, 4), a("i4", 128, 192), 0.0, Op.is_equal)
+    copy(a("bl"), a("iq"))
+    ts(a("rp"), a("ri"), a("lf", 0, 1), Op.add)
 
-        early = len(tasks)
-        turn(half("kh", h), a(k16), "kh")
+    def lanes(out, z, src, c, first, end, lo=0, w=16, cut=False, n=1):
+        for i in range(16):
+            mm(out, a(z, 15 - i, 143 - i), a3(src, 4 * c, 4 * (c + n), lo + 16 * i, lo + 16 * i + w), first and i == 0, end and i == 15, cut and i == 0)
+
+    def shifted(t, h):
+        early, wt = len(tasks), "wt%d" % h
+        turn(half("kh", h), half("k16_%d" % t, h), "kh")
         for u, (x, y) in enumerate((("s15", "s5k"), ("idn", "idk"))):
-            o = a(pack[0], pack[1] + 64 * u, pack[1] + 64 * u + 64)
+            o = half("e3", 2 * h + u, 64) if EB == 3 else half(PSUM[6 + h], 5 + u, 64)
             mm(o, a(x), half("kh", 2 * h, 64), True, False)
             mm(o, a(y), half("kh", 2 * h + 1, 64), False, True)
-        act(a(wt, 0, 128), a(pack[0], pack[1], pack[1] + 128), AF.Copy)
+        fetch(a(wt, 0, 128), half("e3", h) if EB == 3 else a(PSUM[6 + h], 320, 448), wt)
         w, k = T[wt], T["kd%d" % h]
         dmas("y", "kd%d" % h, [(k[:, 1:17, :], w[:, 64:128]), (k[:, 17:33, :], w[:, 0:64])], [scratch(h)], [a(wt, 0, 128)], 2 ** 16 + 256 * ROW)
-        dmas("y", "wd%d" % h, [(w[j:128:16, 128:1152], k[:, 1 + j:17 + j, :]) for j in range(1, 16)] + ([(w[:, 2112:2176], k[:, 0:16, :])] if NONE == "y" else []),
-             [a(wt, 128, 2176 if NONE == "y" else 1152)], [scratch(h)], 2 ** 19 + 240 * ROW)
-        if NONE != "y":
-            mm(a(m, 448, 512), a("up1"), half("kh", 2 * h, 64), True, False)
-            mm(a(m, 448, 512), a("upk"), half("kh", 2 * h + 1, 64), False, True)
-            if NONE == "s":
-                act(a(wt, 2112, 2176), a(m, 448, 512), AF.Copy)
-            else:
-                copy(a(wt, 2112, 2176), a(m, 448, 512))
-
+        dmas("y", "wd%d" % h, [(w[j:128:16, 128:1152], k[:, 1 + j:17 + j, :]) for j in range(1, 16)] + [(w[:, 1152:1216], k[:, 0:16, :])],
+             [a(wt, 128, 1216)], [scratch(h)], 2 ** 19 + 240 * ROW)
         for x in tasks[early:]:
             x["lead"] = LEAD
 
+    def half_round(t, h):
+        last = t == RO - 1
+        c0, c1 = 2 * h, 2 * h + 2
+        k16, p16, cb, m = "k16_%d" % t, "p16_%d" % t, PSUM[4 + h], PSUM[6 + h]
+        same, packed, lists = (a(m, 0, 128), 128, a(m, 256, 280)) if h else (a(m, 152, 280), 24, a(m, 0, 24))
+        sk, sa, sf = [half("sel", 3 * h + (u if h else 2 - u)) for u in range(3)]
+        l8, code, names = half("l8", h, 8), a(cb, 0, 128), a("nr", 520 * h, 520 * h + 8)
+
+        mine, other = (p16, k16) if FIRST[h] == "p" else (k16, p16)
+
+        now_[0] = "codes%d" % h
+        mm(code, a("ones"), a("cj"), True, False, holds=a(cb))
+        for c in range(c0, c1):
+            o = half(cb, c - c0, 64)
+            for lo, hi in PIECES.get(c, ((0, 4),)):
+                act(a("yg", 1024 * c + 256 * lo, 1024 * c + 256 * hi), ind(table, a(mine, 64 * c + 16 * lo, 64 * c + 16 * hi)), AF.Copy)
+                if c in BEHIND:
+                    tasks[-1]["calls"][0][2].append(a3("a3", 4 * BEHIND[c], 4 * BEHIND[c] + 4))
+            for q in range(4 * c, 4 * c + 4):
+                tt(row("d3", q), ind(table, half(other, q, 16)), half("yg", q, 256), Op.subtract)
+            for lo, hi in PARTS.get(c, ((0, 4),)):
+                if c in RELU:
+                    ts(a3("a3", 4 * c + lo, 4 * c + hi), a3("d3", 4 * c + lo, 4 * c + hi), 0.0, Op.min, -2.0, Op.mult)
+                else:
+                    act(a3("a3", 4 * c + lo, 4 * c + hi), a3("d3", 4 * c + lo, 4 * c + hi), AF.Abs)
+            if h not in WHOLE:
+                lanes(a(m, same[2] + 64 * (c - c0), same[2] + 64 * (c - c0 + 1)), "z1", "d3", c, True, True)
+            if c in RELU:
+                lanes(o, "zd", "d3", c, False, False, cut=True)
+            lanes(o, "zd", "a3", c, False, False, cut=True)
+        if h in WHOLE:
+            lanes(same, "z1", "d3", c0, True, True, n=2)
+        act(half("sn", h), same, AF.Sign, scale=-1.0 if FIRST[h] == "p" else 1.0, bias=0.5)
+        mm(code, a("idk"), half("sn", h), False, True, cut=True)
+        shifted(t, h)
+
+        now_[0] = "least%d" % h
         turn(half("ph_", h), half(p16, h), "ph")
-        scan(half("mi", h), a("rst"), a(cb, 0, 128), 1e9, Op.max, Op.min)
-        if LONG:
-            for u in range(2):
-                ts(a("cl", 8 * h + u, 8 * h + 8, 2), a("mi", 128 * h + 64 * u + 15, 128 * h + 64 * u + 64, 16), LOW, Op.max, a("thr"), Op.min)
-        else:
-            ts(half("cl", h, 8), a("mi", 128 * h + 15, 128 * h + 128, 16), LOW, Op.max, a("thr"), Op.min)
-        ts(half("v8", h, 8), half("cl", h, 8), 11, Op.arith_shift_right, 255, Op.bitwise_and)
-        copy(l8, half("v8", h, 8))
-        tt(half(sel, 2), ind(a("lutf"), l8), half("ph_", h), Op.min)
-        tt(half(sel, 0), ind(a("lutk"), l8), half("ph_", h), Op.min)
-        tt(half(sel, 1), ind(a("lutk"), l8), half("kh", h), Op.min)
-        mm(a(m, 0, 64), a("z1", 15, 143), a(sel, 256, 320), True, True)
-        mm(a(m, 64, 128), a("zk"), a(sel, 320, 384), True, True)
-        mm(a(m, 128, 256), a("idn"), a("tm"), True, False)
-        mm(a(m, 128, 256), a("gm"), half(sel, 0), False, True)
-        if HEADS:
-            lists(a(cb, 272, 280), sel, 256, 384)
-            copy(n16, a(cb, 272, 280))
-            lists(a(m, 256, 272), sel, 0, 256)
-            copy(a("pn16", 24 * h, 24 * h + 16), a(m, 256, 272))
-        else:
-            lists(a(m, 256, 280), sel, 0, 384)
-            copy(half("pn16", h, 24), a(m, 256, 280))
-        act(a(nr), a(m, 0, 264), AF.Copy)
-
-        act(half("xn", h), ind(table, n16), AF.Copy)
-        mm(a(cb, 384, 512), half("xn", h), a("idn"), True, True)
-        act(half("xr", h), a(cb, 384, 512), AF.Copy)
-        if "fl" in POOL:
-            turn(a("fl", 144 * h, 144 * h + 144, 18), a(nr, 256, 264), "fl")
-        else:
-            act(a("fl", 144 * h, 144 * h + 144, 18), a(nr, 256, 264), AF.Copy, bias=4096.0)
-        for b in range(4 * h, 4 * h + 4):
-            e = half("e%d" % (b // 2 % 2), b % 2, 512) if WIDE else a("e%d" % ((8 * t + (b + 4) % 8) % EB))
-            mm(e, a("idn"), half("yg", b, 512), True, False)
-            if FIRST[h] == "p":
-                mm(e, a("idn"), row("d2", b) if LONG else a3("d3", 2 * b, 2 * b + 2), False, False)
-            mm(e, half("xr", h), half("ex", b % 4, 512), False, True, cut=True)
-            if not WIDE:
-                act(a3("ae", 2 * b, 2 * b + 2, 16, 272), e, AF.Abs)
-            elif b % 2:
-                act(a3("ae", 2 * b - 2, 2 * b + 2, 16, 272), a(e[1]), AF.Abs)
-            if b % 2 and "e%d" % h not in WHOLE:
-                o = a(cb, 128 + 72 * (b // 2 % 2), 200 + 72 * (b // 2 % 2))
-                mm(o, a("idn"), half("fl", b // 2, 72), True, False)
-                if "fl" in POOL:
-                    mm(o, a("idn"), a("fk"), False, False)
-                lanes(o, "z1", "ae", b // 2, False, True, 15, 18)
-        if "e%d" % h in WHOLE:
-            mm(a(cb, 128, 272), a("idn"), half("fl", h, 144), True, False)
-            lanes(a(cb, 128, 272), "z1", "ae", 2 * h, False, True, 15, 18, n=8)
-        parts = 2 if h in QUART and not last else 1
-        for u in range(parts):
-            n, v = 2 // parts, parts * h + u
-            sums = a(cb, 128 + 72 * u, 128 + 72 * (u + n))
-            if NEARV:
-                ts(half("sc", v, 72 * n), sums, 1040.0, Op.is_lt, -2.0, Op.mult)
-            else:
-                act(half("sc", v, 72 * n), sums, AF.Sign, bias=-1039.5)
-            scan(half("ms", v, 72 * n), half("sc", v, 72 * n), a("rs", 0, 72 * n), 100.0, Op.min, Op.add)
-            ts(half("o16", v, 4 * n), a("ms", 72 * n * v + 16, 72 * n * (v + 1), 18), 1024.0, Op.mult, 2176.0 + 1024 * NEARV, Op.add)
-            tt(half("fr", v, 64 * n), ind(a(wt), half("o16", v, 4 * n)), half(nr, u, 64 * n), Op.add)
-            if u == 0:
-                ts(half("fu", 2 * h, 64), half("fr", 2 * h, 64), 4095, Op.bitwise_and)
-            if u == parts - 1:
-                ts(half("fu", 2 * h + 1, 64), half("fr", 2 * h + 1, 64), 12, Op.logical_shift_right)
-            if last:
-                copy(half("yk32", h), half("fu", h))
-                dmas("y", "ok%d" % h, [(T.yk[:, 128 * h:128 * h + 128], half("yk32", h)[0])], [], [half("yk32", h)], 2 ** 16)
-            else:
-                turn(half("ks_%d_%d" % (t, h), u, 64 * n), half("fu", v, 64 * n), "ks")
-                send(half("k16_%d_%d" % (t + 1, h), u, 64 * n), half("ks_%d_%d" % (t, h), u, 64 * n), "k%d_%d" % (t + 1, 2 * h + u), nxt, prv)
-
-        tt(half("pa", h), ind(a("lutm"), l8), half("kh", h), Op.min)
-        mm(factor, a("ones"), a("qu"), True, False)
-        mm(factor, a("idn"), half("pa", h), False, True)
-        tt(half("pt", h), half("ph_", h), factor, Op.mult)
-        ts(half("pn", h), half("pt", h), 5, Op.logical_shift_right, 2047, Op.bitwise_and)
-        if last:
-            copy(half("yp32", h), half("pn", h))
-            dmas("y", "op%d" % h, [(T.yp[:, 128 * h:128 * h + 128], half("yp32", h)[0])], [], [half("yp32", h)], 2 ** 16)
-        else:
-            turn(half("ps_%d" % t, h), half("pn", h), "ps")
-            send(half("p16_%d" % (t + 1), h), half("ps_%d" % t, h), "p%d_%d" % (t + 1, h), prv, nxt)
-
-        act(half("yk_", h), ind(table, pk16), AF.Copy)
-        if APART:
-            act(half("dk", h), ind(table, kk16), AF.Copy)
-            mm(a(m, 320, 448), a("idn"), half("dk", h), True, False)
-            mm(a(m, 320, 448), a("idm"), half("yk_", h), False, True)
-            act(half("adk", h), a(m, 320, 448), AF.Abs)
-        else:
-            tt(half("dk", h), ind(table, kk16), half("yk_", h), Op.subtract)
-            act(half("adk", h), half("dk", h), AF.Abs)
-        ts(half("c1", h), half("adk", h), 32.0, Op.is_le, 128.0, Op.mult)
-        tt(half("wv", h), ind(table, pk16), half("c1", h), Op.subtract)
-        ts(half("vv", h), half("wv", h), 0.0, Op.is_lt, 256.0, Op.mult)
-        tt(half("eq", h), ind(a(nr, 256, 264), a("bl")), a(nr, 128, 256), Op.is_equal)
-        mm(a(m, 280, 288), a("idf"), a(nr, 256, 264), True, False)
+        scan(half("mi", h), a("rst"), code, 4e9, Op.max, Op.min)
+        ts(half("cl", h, 8), a("mi", 128 * h + 15, 128 * h + 128, 16), LOW, Op.max, a("thr"), Op.min)
+        ts(half("v8", h, 8), half("cl", h, 8), 13, Op.arith_shift_right, 255, Op.bitwise_and)
+        turn(l8, half("v8", h, 8), "l8%d" % h)
+        tt(sf, ind(a("lutf"), l8), half("ph_", h), Op.min)
+        tt(sk, ind(a("lutk"), l8), half("ph_", h), Op.min)
+        tt(sa, ind(a("lutq"), l8), half("kh", h), Op.mult)
+        for u, z in enumerate(("z1", "zb")):
+            mm(a(m, packed + 64 * u, packed + 64 * u + 64), a(z, 15, 143), a("sel", sf[2] + 64 * u, sf[2] + 64 * u + 64), True, True)
+        mm(same, a("idn"), a("tm"), True, False)
+        mm(same, a("gm"), sk, False, True)
         for i in range(16):
-            mm(a(m, 280, 288), a("zw", 15 - i, 143 - i), a("eq", 128 * h + i, 128 * h + 128, 16), False, i == 15)
-        ts(a("w16", 16 * h, 16 * h + 16, 2), a(m, 280, 288), 16.0, Op.add, a("lf", 0, 1), Op.max)
+            mm(lists, a("z1", 15 - i, 143 - i), a("sel", 384 * h + i, 384 * h + 384, 16), i == 0, i == 15)
+        copy((T.pn16[:, :, 8:16] if h else T.pn16[:, ::-1, 0:8], "pn16", 8 * h, 8 * h + 8, 24), lists)
+        fetch(half("nr", h, 264), a(m, 16 - 16 * h, 280 - 16 * h), "nr%d" % h)
 
+        now_[0] = "near%d" % h
+        act(half("xn", h), ind(table, names16(2, c0, c1)), AF.Copy)
+        mm(code, half("xn", h), a("idn"), True, True)
+        fetch(half("xr", h), code, "xr%d" % h)
+        fetch(a("fl", 144 * h, 144 * h + 144, 18), names, "fl%d" % h, 8192.0)
+        for c in range(c1 - 1, c0 - 1, -1):
+            for b in (2 * c, 2 * c + 1):
+                e = a("e%d" % (turns[0] % EB))
+                turns[0] += 1
+                mm(e, a("idn"), half("yg", b, 512), True, False)
+                if FIRST[h] == "p":
+                    mm(e, a("idn"), a3("d3", 2 * b, 2 * b + 2), False, False)
+                mm(e, half("xr", h), half("ex", b % 4, 512), False, True, cut=True)
+                act(a3("ae", 2 * b, 2 * b + 2, 16, 272), e, AF.Abs)
+            if h not in SUMS:
+                o = a(cb, 256 + 72 * (c - c0), 328 + 72 * (c - c0))
+                mm(o, a("idn"), half("fl", c, 72), True, False)
+                lanes(o, "zb", "ae", c, False, True, 15, 18)
+        if h in SUMS:
+            mm(a(cb, 256, 400), a("idn"), half("fl", h, 144), True, False)
+            lanes(a(cb, 256, 400), "zb", "ae", c0, False, True, 15, 18, n=2)
+        for lo, hi in NEARS:
+            if lo // 2 != h:
+                continue
+            scan(back("ms", 72 * lo, 72 * hi), back(cb, 256 + 72 * (lo - c0), 256 + 72 * (hi - c0)), back("rp", 0, 72 * (hi - lo)), -4096.0, Op.min, Op.max)
+            ts(part("o16", lo, hi, 4), a("ms", 72 * lo, 72 * hi, 18), 2048.0, Op.add)
+            tt(part("fr", lo, hi), ind(a("wt%d" % h), part("o16", lo, hi, 4)), a("nr", 8 + 256 * h + 64 * lo, 8 + 256 * h + 64 * hi), Op.add)
+            for c in range(hi - 1, lo - 1, -1):
+                if c % 2 == 0:
+                    ts(half("fu", c, 64), half("fr", c, 64), 4095, Op.bitwise_and)
+                    if not last:
+                        turn(half("ks_%d" % t, c, 64), half("fu", c, 64), "ks")
+                elif last:
+                    ts(half("fu", c, 64), half("fr", c, 64), 12, Op.logical_shift_right)
+                else:
+                    ts(half("ks_%d" % t, c, 64), half("fr", c, 64), 2.0 ** -12, Op.mult)
+            if last:
+                copy(part("yk32", lo, hi), part("fu", lo, hi))
+                dmas("y", "ok%d" % lo, [(T.yk[:, 64 * lo:64 * hi], T.yk32[:, 64 * lo:64 * hi])], [], [part("yk32", lo, hi)], 2 ** 15 * (hi - lo))
+            else:
+                send(part("k16_%d" % (t + 1), lo, hi), part("ks_%d" % t, lo, hi), "k%d_%d" % (t + 1, lo), nxt, prv)
+
+        now_[0] = "phages%d" % h
+        ts(half("pa", h), sa, -1.0, Op.mult, 0.0, Op.max)
+        for lo, hi in PHAGES:
+            if lo == c0:
+                factor = a("e3", 256 + 64 * lo, 256 + 64 * hi) if EB == 3 else a(m, 320, 448)
+                mm(factor, a("ones"), a("qu", 0, 64 * (hi - lo)), True, False)
+                mm(factor, a("idn"), part("pa", lo, hi), False, True)
+                tt(part("pt", lo, hi), part("ph_", lo, hi), factor, Op.mult)
+                ts(part("pn", lo, hi), part("pt", lo, hi), 5, Op.logical_shift_right, 2047, Op.bitwise_and)
+                if last:
+                    turn(part("yp32", lo, hi), part("pn", lo, hi), "yp")
+                    dmas("y", "op%d" % lo, [(T.yp[:, 64 * lo:64 * hi], T.yp32[:, 64 * lo:64 * hi])], [], [part("yp32", lo, hi)], 2 ** 15 * (hi - lo))
+                else:
+                    turn(part("ps_%d" % t, lo, hi), part("pn", lo, hi), "ps")
+                    send(part("p16_%d" % (t + 1), lo, hi), part("ps_%d" % t, lo, hi), "p%d_%d" % (t + 1, lo), prv, nxt)
+
+        now_[0] = "writes%d" % h
+        for lo, hi in WRITES:
+            if lo == c0:
+                yk, c1_, wv = part("yk_", lo, hi), part("c1", lo, hi), part("wv", lo, hi)
+                less = 64.0 * (h in SIDE)
+                act(yk, ind(table, names16(0, lo, hi)), AF.Copy, bias=-less)
+                tt(part("dk", lo, hi), ind(table, names16(1, lo, hi)), yk, Op.subtract)
+                act(part("adk", lo, hi), part("dk", lo, hi), AF.Abs, bias=-less)
+                if less:
+                    act(c1_, part("adk", lo, hi), AF.Sign, scale=-1.0, bias=32.5)
+                    mm(same, a("idn"), yk, True, False)
+                    mm(same, a("i64"), c1_, False, True)
+                    act(wv, same, AF.Copy)
+                else:
+                    ts(c1_, part("adk", lo, hi), 32.0, Op.is_le, -128.0, Op.mult)
+                    tt(wv, ind(table, names16(0, lo, hi)), c1_, Op.add)
+                ts(part("vv", lo, hi), wv, 0.0, Op.is_lt, 256.0, Op.mult)
+        for lo, hi in EQUAL:
+            if lo == c0:
+                whole = hi - lo > 2
+                tt(part("eq", lo, hi), ind(a("nr") if whole else names, a("bl", 0, 4 * (hi - lo))), a("nr", 136 + 64 * lo, 136 + 64 * hi), Op.is_equal)
+                o = half("e3", h) if EB == 3 else same
+                mm(o, a("idk"), part("eq", lo, hi), True, False)
+                mm(a(o[1], o[2] + 15, o[3], 16), a("idf"), names, False, True)
+                scan(part("mw", lo, hi), a("r0", 0, 64 * (hi - lo)), o, 0.0, Op.mult, Op.subtract)
+                ts(a("w16", 8 * lo, 8 * hi, 2), a("mw", 64 * lo + 15, 64 * hi, 16), 16.0, Op.add, a("lf", 0, 1), Op.max)
+
+    turns = [0]
     for t in range(RO):
-        now_[0] = t
+        now_[1] = t
         for h in (1, 0):
-            start = len(tasks)
             half_round(t, h)
-            for x in tasks[start:]:
-                x["lead"] = x.get("lead", 0) + h * AHEAD[t]
+        now_[0] = "table"
         for q in range(15, -1, -1):
             tt(ind(a("xt"), a("w16", 2 * q, 2 * q + 1)), half("wv", q, 16), half("vv", q, 16), Op.add)
         if t == RO - 1:
@@ -452,10 +420,10 @@ def rank_program(g, core, T, topo):
         else:
             act(a("jk"), a("mi", 15, 256, 16), AF.Sign, acc=a("ac", t, t + 1), scale=-1.0, bias=LOW)
             for u in range(t + 1):
-                mm(a("m1", 288, 289), a("gmf"), a("ac", u, u + 1), u == 0, u == t)
-            ts(a("aa"), a("m1", 288, 289), 0.5, Op.mult, 128.0 * (t + 1), Op.add)
-            ts(a("ab"), a("aa"), 15, Op.bitwise_and)
-            ts(a("thr"), a("ab"), 2.0 ** 19, Op.mult, TOP, Op.add)
+                mm(a("m0", 300, 301), a("gmf"), a("ac", u, u + 1), u == 0, u == t)
+            ts(a("aa"), a("m0", 300, 301), 2.0 ** 20, Op.mult, 2.0 ** 28 * (t + 1), Op.add)
+            ts(a("ab"), a("aa"), 15 << 21, Op.bitwise_and)
+            turn(a("thr"), a("ab"), "thr")
 
     def clash(hist, q, outs, ins, banks):
         for kind, lst in (("w", outs), ("r", ins)):
@@ -473,125 +441,198 @@ def rank_program(g, core, T, topo):
                     e[:] = [y for y in e if not (y[1] >= x[2] and y[2] <= x[3])]
                 e.append((kind, x[2], x[3], q, who))
 
-    hist = {}
-    for n, x in enumerate(tasks):
-        q = x["q"] if x["kind"] == "call" else "dma"
-        x["needs"], x["gaps"], x["next"], x["banks"], at = {}, {}, [], set(), 0
-        for call, outs, ins, cost in x["calls"]:
-            for who, free in clash(hist, q, outs, ins, False):
-                if who != n and (0 if free else HOP) - at > x["needs"].get(who, -1e9):
-                    x["needs"][who], x["gaps"][who] = (0 if free else HOP) - at, (0 if free else HOP, at)
-            note(hist, q, outs, ins, n)
-            x["banks"].update(y[1] for y in outs + ins if y[1] in PSUM)
-            at += cost
-        x["cost"] = at
-        for who in x["needs"]:
-            tasks[who]["next"].append(n)
-    before = [{w: d + tasks[w]["after"] for w, d in x["needs"].items()} for x in tasks]
-    behind = [{w: before[w][n] for w in x["next"]} for n, x in enumerate(tasks)]
-
-    def in_order(needs, nexts, key):
-        order, open_ = [], [len(x) for x in needs]
-        ready = [(key(n), n) for n, k in enumerate(open_) if not k]
-        while ready:
-            x = min(ready)
-            ready.remove(x)
-            order.append(x[1])
-            for w in nexts[x[1]]:
-                open_[w] -= 1
-                if not open_[w]:
-                    ready.append((key(w), w))
-        return order
-
-    def place(needs, nexts, key, first):
-        end, busy = {}, {}
-        for n in in_order(needs, nexts, key):
-            x = tasks[n]
-            at = max([first[n]] + [end[w] + d for w, d in needs[n].items()])
-            held = busy.get(x["q"], []) + [(lo - HOP, hi + HOP) for b in x["banks"] for lo, hi, q in busy.get(b, []) if q != x["q"]]
-            if x["moves"]:
-                held += [(lo - sum(x["moves"]) + x["cost"], hi - x["moves"][0]) for lo, hi in busy.get("engines", [])]
-            for lo, hi in sorted(held):
-                if hi > at:
-                    if lo >= at + x["cost"]:
-                        break
-                    at = hi
-            end[n] = at + x["cost"]
-            busy.setdefault(x["q"], []).append((at, end[n]))
-            if x["moves"]:
-                busy.setdefault("engines", []).append((at + x["moves"][0], at + sum(x["moves"])))
-            for b in x["banks"]:
-                busy.setdefault(b, []).append((at, end[n], x["q"]))
-        return end
-
-    way = [0] * len(tasks)
-    for n in range(len(tasks) - 1, -1, -1):
-        way[n] = tasks[n]["cost"] + max([tasks[n]["after"]] + [way[w] + d for w, d in behind[n].items()])
-    ends = place(before, behind, lambda n: -way[n] - tasks[n].get("lead", 0), [0] * len(tasks))
-    order = in_order(before, behind, lambda n: ends[n] - tasks[n]["cost"])
-
-    def length(order, slow, far, pe):
-        end, free, bank, engines, gone, last = [0] * len(tasks), dict.fromkeys(Q, 0), {}, 0, 0, 0
-        for n in order:
-            q, cost, after, needs, banks, moves, gate = brief[n]
-            at = free[q]
-            for w, d, e in needs:
-                at = max(at, end[w] + d * far - e * slow * pe)
-            for b in banks:
-                if b in bank and bank[b][0] != q:
-                    at = max(at, bank[b][1] + HOP * far)
-            if moves:
-                at = max(at, gone if gate else 0)
-                free[q] = at + cost * far
-                at = max(at, engines - moves[0] * far)
-                engines = at + sum(moves) * far
-                gone = engines + 2 * HOP * far if q == "g" else gone
-                end[n] = at + cost * far
-            else:
-                end[n] = free[q] = at + cost * slow * (pe if q == "p" else 1)
-            for b in banks:
-                bank[b] = (q, end[n])
-            last = max(last, end[n] + after * far)
-        return last
-
-    if MOVES and not PLAN:
-        brief = [(x["q"], x["cost"], x["after"], [(w, tasks[w]["after"] + d, e) for w, (d, e) in x["gaps"].items()], tuple(x["banks"]), x["moves"],
-                  GATE and x["kind"] == "dma" and x["calls"][0][0][0][0] == "w") for x in tasks]
-        start = [ends[n] - x["cost"] for n, x in enumerate(tasks)]
-        step, seen_, table_ = [], {}, {}
+    def planned():
+        hist = {}
         for n, x in enumerate(tasks):
+            q = x["q"] if x["kind"] == "call" else "dma"
+            x["needs"], x["gaps"], x["banks"], at = {}, {}, set(), 0
+            for call, outs, ins, cost in x["calls"]:
+                for who, free in clash(hist, q, outs, ins, False):
+                    if who != n and (0 if free else HOP) - at > x["needs"].get(who, -1e9):
+                        x["needs"][who], x["gaps"][who] = (0 if free else HOP) - at, (0 if free else HOP, at)
+                note(hist, q, outs, ins, n)
+                x["banks"].update(y[1] for y in outs + ins if y[1] in PSUM)
+                at += cost
+            x["cost"] = at
+        before = [{w: d + tasks[w]["after"] for w, d in x["needs"].items()} for x in tasks]
+        nexts = [[] for x in tasks]
+        for n, x in enumerate(before):
+            for w in x:
+                nexts[w].append(n)
+
+        def in_order(key):
+            key = list(key)
+            for n in range(len(key) - 1, -1, -1):
+                for w in before[n]:
+                    if key[w] > key[n]:
+                        key[w] = key[n]
+            return [n for k, n in sorted(zip(key, range(len(key))))]
+
+        def place(key):
+            end, busy = {}, {}
+            for n in in_order(key):
+                x = tasks[n]
+                at = max([0] + [end[w] + d for w, d in before[n].items()])
+                held = busy.get(x["q"], []) + [(lo - HOP, hi + HOP) for b in x["banks"] for lo, hi, q in busy.get(b, []) if q != x["q"]]
+                if x["moves"]:
+                    held += [(lo - sum(x["moves"]) + x["cost"], hi - x["moves"][0]) for lo, hi in busy.get("engines", [])]
+                for lo, hi in sorted(held):
+                    if hi > at:
+                        if lo >= at + x["cost"]:
+                            break
+                        at = hi
+                end[n] = at + x["cost"]
+                busy.setdefault(x["q"], []).append((at, end[n]))
+                if x["moves"]:
+                    busy.setdefault("engines", []).append((at + x["moves"][0], at + sum(x["moves"])))
+                for b in x["banks"]:
+                    busy.setdefault(b, []).append((at, end[n], x["q"]))
+            return end
+
+        way = [0] * len(tasks)
+        for n in range(len(tasks) - 1, -1, -1):
+            way[n] = tasks[n]["cost"] + max([tasks[n]["after"]] + [way[w] + before[w][n] for w in nexts[n]])
+        ends = place([-way[n] - x["lead"] for n, x in enumerate(tasks)])
+        start = [ends[n] - x["cost"] for n, x in enumerate(tasks)]
+
+        briefs = [[(x["q"], (x["cost"] + (pick - 1) * x["picks"]) * (far if x["moves"] else slow * {"p": pe, "s": sc}.get(x["q"], 1)), x["after"] * far,
+                    [(w, tasks[w]["after"] * far + d * hop - e * slow * pe) for w, (d, e) in x["gaps"].items()], tuple(sorted(x["banks"])),
+                    x["moves"] and (x["moves"][0] * far, sum(x["moves"]) * far)) for x in tasks] for slow, far, pe, pick, sc, hop in SPEEDS]
+
+        def length(order, brief, hop, why=None):
+            end, free, bank, engines, last = [0] * len(tasks), dict.fromkeys(Q, (0, -1)), dict.fromkeys(PSUM, ("p", 0, -1)), (0, -1), (0, -1)
+            for n in order:
+                q, cost, after, needs, banks, moves = brief[n]
+                at, who = free[q]
+                for w, d in needs:
+                    if end[w] + d > at:
+                        at, who = end[w] + d, w
+                for b in banks:
+                    if bank[b][0] != q and bank[b][1] > at:
+                        at, who = bank[b][1:]
+                free[q] = (at + cost, n)
+                if moves:
+                    if engines[0] - moves[0] > at:
+                        at, who = engines[0] - moves[0], engines[1]
+                    engines = (at + moves[1], n)
+                end[n] = at = at + cost
+                for b in banks:
+                    bank[b] = (q, at + hop, n)
+                if at + after > last[0]:
+                    last = (at + after, n)
+                if why:
+                    why[n] = who
+            if why:
+                why[-1] = last[1]
+            return last[0]
+
+        def total(order):
+            return sum(length(order, b, HOP * x[5]) / sum(x[:2]) for b, x in zip(briefs, SPEEDS))
+
+        def blocks(order):
+            found = []
+            for b, x in zip(briefs, SPEEDS):
+                why = [-1] * (len(tasks) + 1)
+                length(order, b, HOP * x[5], why)
+                n = why[-1]
+                while why[n] >= 0:
+                    if why[n] not in before[n]:
+                        found.append((why[n], n))
+                    n = why[n]
+            return found
+
+        rng = np.random.default_rng(SEED)
+
+        step, seen_, table_ = [], {}, {}
+        for x in tasks:
             o = (x["calls"][0][1] + x["calls"][0][2])[0]
-            name = (x["q"], o[1][0] if o[1] in PSUM[:EB] else o[1][:2] + o[1][5:].strip("0123")[:0] + o[1][-2:] * (o[1][0] == "k") if "_" in o[1][2:-1] else o[1],
-                    o[2], x["round"] < 0)
+            name = (x["stage"], x["q"], "e" if o[1] in PSUM[:EB] else o[1].rstrip("0123") if "_" in o[1][2:-1] else o[1], o[2])
             seen_[name, x["round"]] = seen_.get((name, x["round"]), 0) + 1
             step.append(name + (seen_[name, x["round"]],))
-        first = [min(start[n] for n, x in enumerate(tasks) if x["round"] == t and step[n][1] == "yg") for t in range(RO)]
-        period = first[2] - first[1]
-        for t in (3, 0, 2, 1, -1):
-            table_.update({step[n]: start[n] - first[max(t, 0)] for n, x in enumerate(tasks) if x["round"] == t})
-        names, one = sorted(table_), [step[n] for n, x in enumerate(tasks) if x["round"] == 1]
-
-        def tried():
-            key = [table_[step[n]] + period * max(x["round"], 0) for n, x in enumerate(tasks)]
-            o = in_order(before, behind, lambda n: key[n])
-            return sum(length(o, *x) / sum(x[:2]) for x in SPEEDS), o
-
-        best = now = tried()
-        rng = np.random.default_rng(SEED)
-        for n in range(MOVES):
-            at, many = int(rng.integers(len(one))), int(rng.integers(2, 12))
-            moved = [names[int(rng.integers(len(names)))]] if rng.random() < 0.6 else set(one[at:at + many])
-            by = rng.normal() * (150, 500, 1500)[int(rng.integers(3))]
-            for x in moved:
-                table_[x] += by
-            new = tried()
-            if new[0] <= now[0] + 15 * (1 - n / MOVES) * rng.exponential():
-                now, best = new, min(best, new)
+        first = [min(start[n] for n, x in enumerate(tasks) if x["round"] == t and step[n][2] == "yg") for t in range(RO)]
+        for t in (3, 0, 2, 1):
+            table_.update({step[n]: start[n] - first[t] * (x["stage"] != "start") for n, x in enumerate(tasks) if x["round"] == t})
+        names = sorted(table_)
+        where = np.array([names.index(x) for x in step])
+        times = np.array([table_[x] for x in names])
+        shift = np.array([first[0] * (x["stage"] != "start") + (first[2] - first[1]) * x["round"] for x in tasks])
+        order = in_order((times[where] + shift).tolist())
+        best = now = (total(order), order, times)
+        INFO["first"] = now[0]
+        pairs = blocks(order)
+        for n in range(STEPS):
+            if n == STEPS - APART:
+                own = np.array([where[k] + len(names) * CLASS[x["round"]] for k, x in enumerate(tasks)])
+                now, times, where = best[:2], np.tile(best[2], 3), own
+            new = times.copy()
+            if rng.random() < AIM:
+                u, v = pairs[int(rng.integers(len(pairs)))]
+                key = new[where] + shift
+                if rng.random() < 0.5:
+                    new[where[v]] = min(key[u], key[v]) - 1 - rng.exponential() * 30 - shift[v]
+                else:
+                    at, todo = max(key[u], key[v]) + 1 + rng.exponential() * 30, [u]
+                    while todo:
+                        w = todo.pop()
+                        if key[w] < at:
+                            key[w], new[where[w]] = at, at - shift[w]
+                            todo += nexts[w]
             else:
-                for x in moved:
-                    table_[x] -= by
-        PLAN.extend(best[1])
-    order = PLAN or order
+                at = int(rng.integers(len(tasks)))
+                new[np.unique(where[at:at + (1 if rng.random() < 0.6 else int(rng.integers(2, 12)))])] += rng.normal() * (150, 500, 1500)[int(rng.integers(3))]
+            order = in_order((new[where] + shift).tolist())
+            cost = total(order)
+            if cost <= now[0] + (WARM * (1 - n / (STEPS - APART)) if n < STEPS - APART else MILD * (STEPS - n) / APART) * rng.exponential():
+                if cost != now[0]:
+                    pairs = blocks(order)
+                now, times = (cost, order), new
+                if cost < best[0]:
+                    best = (cost, order, new)
+        INFO["steps"] = best[0]
+
+        now = best = best[:2]
+        pairs = blocks(now[1])
+        for n in range(MOVES):
+            order = now[1]
+            if rng.random() < AIM:
+                u, v = pairs[int(rng.integers(len(pairs)))]
+                lo, hi = sorted((order.index(u), order.index(v)))
+            else:
+                lo = int(rng.integers(len(order) - 1))
+                hi = min(len(order) - 1, lo + 1 + int(rng.exponential() * REACH))
+            run = order[lo:hi + 1]
+            if rng.random() < 0.5:
+                moved = {run[-1]}
+                for w in run[-2::-1]:
+                    if any(x in moved for x in nexts[w]):
+                        moved.add(w)
+                run = [w for w in run if w in moved] + [w for w in run if w not in moved]
+            else:
+                moved = {run[0]}
+                for w in run[1:]:
+                    if any(x in moved for x in before[w]):
+                        moved.add(w)
+                run = [w for w in run if w not in moved] + [w for w in run if w in moved]
+            order = order[:lo] + run + order[hi + 1:]
+            new = (total(order), order)
+            if new[0] <= now[0] + HEAT * (1 - n / MOVES) * rng.exponential():
+                if new[0] != now[0]:
+                    pairs = blocks(order)
+                now, best = new, min(best, new)
+        INFO["total"] = best[0]
+        INFO["best"] = [int(length(best[1], b, HOP * x[5]) * 0.83) for b, x in zip(briefs, SPEEDS)]
+        why = [-1] * (len(tasks) + 1)
+        length(best[1], briefs[-1], HOP * SPEEDS[-1][1], why)
+        n, INFO["path"] = why[-1], []
+        INFO["busy"] = {q: int(sum(b[1] for b in briefs[-1] if b[0] == q) * 0.83) for q in Q}
+        while n >= 0:
+            o = (tasks[n]["calls"][0][1] + tasks[n]["calls"][0][2])[0]
+            INFO["path"].append("%s%s%s:%d %d" % ("" if why[n] in before[n] else "*", tasks[n]["q"].upper(), o[1], o[2], briefs[-1][n][1] * 0.83))
+            n = why[n]
+        return best[1]
+
+    if not PLAN:
+        PLAN.extend(planned())
 
     hist, seen, known, count, left = {}, {q: {} for q in Q}, {}, {}, []
 
@@ -607,7 +648,7 @@ def rank_program(g, core, T, topo):
                 for s2, v2 in known.get((sem, val), {}).items():
                     seen[q][s2] = max(seen[q].get(s2, 0), v2)
 
-    for n in order:
+    for n in PLAN:
         q, kind = tasks[n]["q"], tasks[n]["kind"]
         for call, outs, ins, cost in tasks[n]["calls"]:
             waits(q, clash(hist, q if kind == "call" else "dma", outs, ins, True))
@@ -616,8 +657,6 @@ def rank_program(g, core, T, topo):
                 call().then_inc(T.sem[q], 1)
             elif kind == "dma":
                 sem = call[0]
-                if GATE and sem[0] == "w":
-                    waits(q, [(x, False) for x in left])
                 for out, in_ in call[1]:
                     Q[q].dma_start(out, in_).then_inc(T.sem[sem], 16)
                     count[sem] = count.get(sem, 0) + 16
@@ -631,6 +670,7 @@ def rank_program(g, core, T, topo):
             note(hist, q if kind == "call" else "dma", outs, ins, (sem, count[sem]))
     for sem, val in left:
         g.wait_ge(T.sem[sem], val)
-    for sem in ("oy", "ok0", "ok1", "op0", "op1", "v", "s", "p", "g"):
-        if seen["y"].get(sem, 0) < count[sem]:
-            g.sync.wait_ge(T.sem[sem], count[sem])
+    for sem in count:
+        if sem[0] == "o" or len(sem) == 1:
+            if seen["y"].get(sem, 0) < count[sem]:
+                g.sync.wait_ge(T.sem[sem], count[sem])

@@ -5,23 +5,23 @@ RO = 4
 F, B, H, I, U = "float32", "bfloat16", "float16", "int32", "uint16"
 SCRATCH = {}
 for _n, _w, _d in (
-        ("xt", 2064, B), ("nk", 256, I), ("np_", 256, I), ("yg", 4096, B), ("ph_", 256, H), ("kh", 256, H), ("sn", 256, B),
-        ("mi", 256, F), ("cl", 16, I), ("v8", 16, I), ("l8", 16, U), ("sel", 768, H),
-        ("nr", 528, F), ("xn", 256, B), ("xr", 256, B), ("eq", 256, B), ("mw", 256, F), ("w16", 32, U),
-        ("yk_", 256, B), ("dk", 256, B), ("adk", 256, B), ("c1", 256, B),
-        ("wv", 256, B), ("vv", 256, B), ("pa", 256, H), ("pt", 256, I), ("pn", 256, I), ("yp32", 256, F),
+        ("xt", 2080, B), ("nk", 256, I), ("np_", 256, I), ("yg", 4096, B), ("ph_", 256, H), ("kh", 256, H), ("sn", 256, B),
+        ("mi", 256, I), ("cl", 16, I), ("v8", 16, I), ("l8", 16, U), ("sel", 768, H),
+        ("nr", 792, F), ("xn", 256, B), ("xr", 256, B), ("eq", 512, B), ("mw", 512, U), ("nm", 512, U), ("w16", 32, U),
+        ("yk_", 256, F), ("dk", 256, B), ("c1", 256, B),
+        ("pn16", 48, U), ("ys", 512, B), ("sg", 256, B), ("idm", 128, B), ("i128", 128, B), ("vv", 256, B), ("pa", 256, H), ("pt", 256, I), ("pn", 256, I), ("yp32", 256, F),
         ("wt0", 1216, F), ("wt1", 1216, F), ("fl", 288, B), ("ms", 288, F), ("o16", 16, U), ("fr", 256, I), ("fu", 256, I),
-        ("yk32", 256, F), ("jk", 16, B), ("ac", 4, F), ("aa", 1, I), ("ab", 1, I), ("thr", 1, F),
+        ("yk32", 256, F), ("jk", 24, B), ("ac", 4, F), ("aa", 8, I), ("ab", 8, I), ("big", 8, F),
         ("pi", 2, I), ("li", 2, I), ("lf", 2, F), ("l15", 2, F), ("ones", 128, B), ("neg", 512, B), ("gm", 128, B), ("idn", 128, B),
-        ("idf", 128, F), ("idk", 128, B), ("gmf", 128, F), ("s15", 128, B), ("s5k", 128, B), ("i64", 128, B), ("qu", 128, B),
-        ("z1", 143, B), ("zd", 143, B), ("zb", 143, B), ("r0", 128, B),
-        ("cj", 128, B), ("rst", 128, F), ("ri", 144, I), ("rp", 144, F), ("ex", 2048, B), ("tm", 128, B), ("ij", 128, I), ("iq", 16, I),
-        ("bl", 16, U), ("i3", 192, I), ("i4", 192, I), ("nil", 64, F),
+        ("idk", 128, B), ("gmf", 128, F), ("s15", 128, B), ("s5k", 128, B), ("qu", 128, B),
+        ("z1", 143, B), ("zd", 143, B), ("zb", 143, B), ("it", 256, I), ("iu", 16, I),
+        ("cj", 128, B), ("rst", 128, F), ("ri", 144, I), ("rp", 144, F), ("ex", 2048, B), ("ij", 128, I), ("iq", 32, I),
+        ("bl", 32, U), ("i3", 192, I), ("i4", 192, I), ("nil", 64, F),
         ("lutf", 256, B), ("lutk", 256, B), ("lutq", 256, B)):
     SCRATCH[_n] = ("sbuf", [128, _w], _d)
 for _n, _w in (("d3", 256), ("a3", 256), ("ae", 288)):
     SCRATCH[_n] = ("sbuf", [128, 16, _w], B)
-SCRATCH["pn16"] = ("sbuf", [128, 3, 16], U)
+SCRATCH["tm"] = ("sbuf", [128, 24, 32], B)
 for _h in range(2):
     SCRATCH["kd%d" % _h] = ("dram", [8, 33, 64], F)
 for _t in range(RO):
@@ -41,22 +41,35 @@ WHOLE = (1,)
 BEHIND = {1: 2}
 PIECES = {2: ((0, 1), (1, 4)), 3: ((0, 1), (1, 4))}
 PARTS = {1: ((0, 2), (2, 4))}
+CUTS = {2: ((0, 1), (1, 4)), 3: ((0, 2), (2, 4)), 1: ((0, 2), (2, 4))}
 POOL = ("kh", "ph", "ps", "thr", "yp", "k0", "p0")
 AGAIN = True
-SPARE = ("idf", "gmf", "s5k", "idk", "zd", "zb", "i64", "ae", "rst", "lutf", "lutk")
+WIDE = (16, 16)
+SPARE = ("nm", "gmf", "s5k", "idk", "zd", "zb", "idm", "i128", "ae", "rst", "lutf", "lutk")
 SIDE = ()
-FIRST = "pp"
+FIRST = "kp"
 ONV = ()
 SUMS = ()
 AHEAD = {}
 LEAD = 4000
 EB = 3
 AIM, REACH, HEAT, WARM = 0.8, 8, 90, 600
-STEPS, MOVES, SEED, PLAN = 8000, 14000, 8, []
-APART, MILD, CLASS = 2000, 150, (0, 1, 1, 2)
+STEPS, MOVES, SEED, PLAN = 12000, 16000, 8, []
+APART, MILD, CLASS = 3000, 150, (0, 1, 1, 2)
+FREE = ()
+SHOW = 0
+MARK, SLACK = 32, 150
+DIRECT = False
+ONS = ()
+HAND = {}
+TRIES, AIM2, WARM2, BASE, SOME = 0, 0.6, 1500, 6, (0, 1, 2, 3, 4, 5)
+PACKS, MIXES, NOISE, SHARE, LOOSE = 0, (0, 1, 2, 3, 4, 5), (0, 100, 300), 0.2, 1000
+FLIP = ()
 SPEEDS = ((1.05, 0.95, 0.85, 1.0, 1.0, 0.95), (1.25, 0.8, 1.1, 1.3, 0.95, 1.2), (1.4, 1.3, 1.0, 0.9, 1.0, 0.7), (1.55, 0.8, 1.1, 1.1, 0.92, 0.8),
-          (1.05, 1.5, 0.9, 0.8, 1.0, 1.3), (1.3, 0.7, 1.1, 0.75, 1.0, 0.6))
-LOW = -192 * 2.0 ** 19 + 8192
+          (1.05, 1.5, 0.9, 0.8, 1.0, 1.3), (1.3, 0.7, 1.1, 0.75, 1.0, 0.6), (1.2, 1.1, 1.0, 1.0, 1.0, 1.0))
+TOP = 192 * 2.0 ** 17 + 2048
+ROUND = 1.5 * 2.0 ** 29
+MID = 12288.0
 HOP, CALL, PICK, ACT, GATHER, SCATTER, ISSUE, LOCAL, REMOTE, FAR, BYTES, MATMUL, COLUMN, ROWS, ROW = 176, 40, 88, 77, 1.45, 3.5, 242, 1300, 588, 2800, 152, 10, 0.45, 2000, 150
 INFO = {}
 
@@ -90,8 +103,8 @@ def rank_program(g, core, T, topo):
     def part(name, c0, c1, w=64):
         return a(name, w * c0, w * c1)
 
-    def names16(u, c0, c1):
-        return (T.pn16[:, u, 4 * c0:4 * c1], "pn16", 4 * c0, 4 * c1, 4 * (c1 - c0))
+    def names16(u, h):
+        return half("pn16", 3 * h + (2 - u if h else u), 8)
 
     def ind(win, off):
         return (win[0].indirect(off[0]), win, off)
@@ -135,7 +148,7 @@ def rank_program(g, core, T, topo):
             vec(lambda: V.tensor_scalar(out[0], x[0], c[0], c[1], op0, op1), out, ins, narrow(out, x))
 
     def scan(out, d0, d1, first, op0, op1):
-        vec(lambda: V.tensor_tensor_scan(out[0], d0[0], d1[0], first, op0, op1), out, [d0, d1], 1)
+        vec(lambda: V.tensor_tensor_scan(out[0], d0[0], d1[0], first, op0, op1), out, [d0, d1], narrow(out, d0, d1))
 
     def fill(out, val):
         if out[1] in SPARE:
@@ -145,8 +158,10 @@ def rank_program(g, core, T, topo):
 
     def act(out, in_, func, acc=None, **kw):
         cost, picks = (80, GATHER * out[4]) if isinstance(in_[1], tuple) else (ACT + out[4], 0)
+        cols = [x for x in kw.values() if isinstance(x, tuple)]
+        kw = {k: x[0] if isinstance(x, tuple) else x for k, x in kw.items()}
         if acc is None:
-            task("s", "call", lambda: S.activation(out[0], in_[0], func, **kw), [out], [in_], cost, picks=picks)
+            task("s", "call", lambda: S.activation(out[0], in_[0], func, **kw), [out], [in_] + cols, cost, picks=picks)
         else:
             task("s", "call", lambda: S.activation(out[0], in_[0], func, accum_out=acc[0], **kw), [out, acc], [in_], cost)
 
@@ -163,6 +178,8 @@ def rank_program(g, core, T, topo):
     def turn(out, in_, key):
         if key in POOL:
             asel(out, in_, [[0, out[4]]], Op.is_equal, 0, 0)
+        elif key in ONS:
+            act(out, in_, AF.Copy)
         else:
             copy(out, in_)
 
@@ -184,7 +201,7 @@ def rank_program(g, core, T, topo):
     def send(to, names, sem, dst, src):
         task("g", "send", ("a" + sem, "l" + sem, dst, src), [to], [names], REMOTE, FAR, moves=(REMOTE, ROWS))
 
-    table = a("xt", 16, 2064)
+    table = a("xt", 32, 2080)
 
     dmas("s", "lp1", [(T.np_[:, 128:256], T.ph[:, 128:256])], [half("np_", 1)], [], 2 ** 16)
     dmas("y", "lx", [(table[0], T.x0[:])], [table], [], 2 ** 19)
@@ -201,7 +218,6 @@ def rank_program(g, core, T, topo):
     asel(a("gm"), a("gm"), [[16, 8], [0, 16]], Op.is_ge, 15, -1)
     asel(a("idn"), a("ones"), [[1, 128]], Op.is_equal, 0, -1)
     iota(a("ij"), [[0, 8], [1, 16]], 0, 0)
-    iota(a("iq"), [[520, 2], [1, 8]], 0, 0)
     iota(a("i3", 0, 64), [[1, 4], [1, 16]], 129, -1)
     iota(a("i3", 64, 128), [[-1, 4], [1, 16]], 127, -1)
     iota(a("i3", 128, 192), [[0, 4], [1, 16]], 128, -1)
@@ -214,39 +230,56 @@ def rank_program(g, core, T, topo):
     fill(a("fl"), -1040.0 * 4096)
     fill(a("fl", 17, 288, 18), -2.0 ** 26)
     fill(a("rst"), -4e9)
-    fill(a("rst", 0, 128, 16), 4e9)
-    fill(a("thr"), 0.0)
+    fill(a("rst", 0, 128, 16), TOP)
+    fill(a("big"), 2.0 ** 18)
     fill(a("lutf"), 0.0)
     fill(a("lutk"), -512.0)
+    fill(a("lutk", 0, 1), -768.0)
     fill(a("lutq"), 0.0)
-    fill(a("lutq", 1, 2), -1.0)
+    fill(a("lutq", 0, 1), -1.0)
     fill(a("w16"), 0)
-    fill(a("xt", 0, 16), 0.0)
-    fill(a("r0"), 1.0)
-    fill(a("r0", 0, 128, 16), 0.0)
+    fill(a("nr", 392, 400), 1.0)
+    fill(a("xt", 0, 32), 0.0)
     fill(a3("ae", 0, 16, 0, 16), 0.0)
     fill(a3("ae", 0, 16, 272, 288), 0.0)
     dmas("y", "kz", [(T["kd%d" % h][:, 0, :], T.nil[0:8, :]) for h in range(2)] + [(T["wt%d" % h][0:128:16, 128:1152], T.nil[:]) for h in range(2)],
          [a("wt0", 128, 1152), a("wt1", 128, 1152), scratch(0), scratch(1)], [a("nil")], 2 ** 16 + 256 * ROW)
     ts(a("li"), a("pi"), 15, Op.bitwise_and)
     copy(a("lf"), a("li"))
-    ts(a("l15"), a("lf"), 15.0, Op.is_equal)
+    ts(a("l15", 0, 1), a("lf", 0, 1), 15.0, Op.is_equal)
     copy(a("z1", 15, 143, 16), a("gm", 0, 128, 16))
     ts(a("s15"), a("gm"), a("l15", 0, 1), Op.mult)
-    for z, x, w in (("i64", "idn", -64.0),) * (len(SIDE) > 0) + (("idf", "idn", -1.0), ("gmf", "gm", 1.0), ("s5k", "s15", 4096.0), ("idk", "idn", 4096.0), ("zd", "z1", 2.0 ** 19), ("zb", "z1", 4096.0)):
+    for z, x, w in (("gmf", "gm", 1.0), ("s5k", "s15", 4096.0), ("idk", "idn", 4096.0), ("zd", "z1", 2.0 ** 17), ("zb", "z1", 4096.0),
+                    ("idm", "idn", -1.0), ("i128", "idn", 128.0)):
         if z in SPARE:
             act(a(z), a(x), AF.Copy, scale=w)
         else:
             ts(a(z), a(x), w, Op.mult)
-    vec(lambda: V.memset(T.cj[0:64, :], -16.0 * 2 ** 19), a("cj"), [], 0.5)
-    vec(lambda: V.tensor_scalar(T.cj[64:128, :], T.ij[64:128, :], 512.0, 320.0, Op.mult, Op.add), a("cj"), [a("ij")], 1)
+    vec(lambda: V.memset(T.cj[0:64, :], -13.0 * 2 ** 17), a("cj"), [], 0.5)
+    vec(lambda: V.tensor_scalar(T.cj[64:128, :], T.ij[64:128, :], 128.0, 96.0, Op.mult, Op.add), a("cj"), [a("ij")], 1)
     ts(a("i4"), a("i3"), 15, Op.bitwise_and)
-    ts(a("tm"), a("ij"), a("lf", 0, 1), Op.is_ge, 16384.0, Op.mult)
+    for wide in sorted(set(WIDE)):
+        iota(a("it", 0, 8 * wide), [[0, 8], [1, wide]], 16 - wide, 0)
+        ts(a3("tm", wide - 16, wide - 16 + wide // 4), a("it", 0, 8 * wide), a("lf", 0, 1), Op.is_ge, 16384.0, Op.mult)
+        if wide > 16:
+            fill((T.tm[:, 16:24:2, 0:16], "tm", 512, 768, 64), 16384.0)
+            ts(a("lf", 1, 2), a("lf", 0, 1), 16.0, Op.add)
+            ts(a("l15", 1, 2), a("lf", 0, 1), -1.0, Op.mult, 16.0, Op.add)
+    for h in range(2):
+        wide = WIDE[h]
+        x0, x1, n = 256 * h, 256 * h + 8 * wide, wide // 16
+        fill(a("nm", x0, x1), 0.0)
+        if wide > 16:
+            ts(a("nm", x0, x1, 64), a("big", 0, 4), 0.0, Op.mult, a("lf", 1, 2), Op.add)
+        iota(a("iq", 16 * h, 16 * h + 8 * n), [[1, 8], [0, n]], 8 * h, 0)
+        iota(a("iu", 8 * h, 8 * h + 8), [[-1, 8]], 8 - 16 * h, 0)
+        ts(a("iu", 8 * h, 8 * h + 8), a("iu", 8 * h, 8 * h + 8), a("l15", 0, 1), Op.mult)
+        tt(a("iq", 16 * h + n - 1, 16 * h + 8 * n, n), a("iq", 16 * h + n - 1, 16 * h + 8 * n, n), a("iu", 8 * h, 8 * h + 8), Op.add)
+        copy(a("bl", 16 * h, 16 * h + 8 * n), a("iq", 16 * h, 16 * h + 8 * n))
     for sb in range(2):
         ts(a("lutf", 2 + sb, 256, 4), a("i4", 64 * sb, 64 * sb + 64), 0.0, Op.is_equal, 4096.0, Op.mult)
         ts(a("lutk", 2 + sb, 256, 4), a("i4", 128, 192), 0.0, Op.is_equal, 4096.0, Op.mult)
         ts(a("lutq", 2 + sb, 256, 4), a("i4", 128, 192), 0.0, Op.is_equal)
-    copy(a("bl"), a("iq"))
     ts(a("rp"), a("ri"), a("lf", 0, 1), Op.add)
 
     def lanes(out, z, src, c, first, end, lo=0, w=16, cut=False, n=1):
@@ -272,9 +305,12 @@ def rank_program(g, core, T, topo):
         last = t == RO - 1
         c0, c1 = 2 * h, 2 * h + 2
         k16, p16, cb, m = "k16_%d" % t, "p16_%d" % t, PSUM[4 + h], PSUM[6 + h]
-        same, packed, lists = (a(m, 0, 128), 128, a(m, 256, 280)) if h else (a(m, 152, 280), 24, a(m, 0, 24))
-        sk, sa, sf = [half("sel", 3 * h + (u if h else 2 - u)) for u in range(3)]
-        l8, code, names = half("l8", h, 8), a(cb, 0, 128), a("nr", 520 * h, 520 * h + 8)
+        wide = WIDE[h]
+        same, packed, lists = (a(m, 152, 152 + 8 * wide), 24, a(m, 0, 24)) if h else (a(m, 256 - 8 * wide, 256), 256, a(m, 384, 408))
+        signed = a(m, same[2], same[2] + 128)
+        sk, sa, sf = [half("sel", 3 * h + (2 - u if h else u)) for u in range(3)]
+        l8, code, names = half("l8", h, 8), a(cb, 0, 128), half("nr", 48 + 2 * h, 8)
+        at, rows, news = (400, 536, 408) if h else (256 - 8 * wide, 256 - 8 * wide, 256)
 
         mine, other = (p16, k16) if FIRST[h] == "p" else (k16, p16)
 
@@ -299,31 +335,41 @@ def rank_program(g, core, T, topo):
                 lanes(o, "zd", "d3", c, False, False, cut=True)
             lanes(o, "zd", "a3", c, False, False, cut=True)
         if h in WHOLE:
-            lanes(same, "z1", "d3", c0, True, True, n=2)
-        act(half("sn", h), same, AF.Sign, scale=-1.0 if FIRST[h] == "p" else 1.0, bias=0.5)
-        mm(code, a("idk"), half("sn", h), False, True, cut=True)
+            lanes(signed, "z1", "d3", c0, True, True, n=2)
+        act(half("sn", h), signed, AF.Sign, scale=-1.0 if FIRST[h] == "p" else 1.0, bias=0.5)
+        mm(code, a("i128"), half("sn", h), False, True, cut=True)
         shifted(t, h)
 
         now_[0] = "least%d" % h
         turn(half("ph_", h), half(p16, h), "ph")
-        scan(half("mi", h), a("rst"), code, 4e9, Op.max, Op.min)
-        ts(half("cl", h, 8), a("mi", 128 * h + 15, 128 * h + 128, 16), LOW, Op.max, a("thr"), Op.min)
-        ts(half("v8", h, 8), half("cl", h, 8), 13, Op.arith_shift_right, 255, Op.bitwise_and)
+        least = a("mi", 128 * h + 15, 128 * h + 128, 16)
+        scan(half("mi", h), a("rst"), code, 0.0, Op.max, Op.min)
+        if SCRATCH["mi"][2] == F:
+            copy(half("cl", h, 8), least)
+            least = half("cl", h, 8)
+        ts(half("v8", h, 8), least, (255 << 11) - 2 ** 31, Op.bitwise_and, 11, Op.arith_shift_right)
         turn(l8, half("v8", h, 8), "l8%d" % h)
         tt(sf, ind(a("lutf"), l8), half("ph_", h), Op.min)
         tt(sk, ind(a("lutk"), l8), half("ph_", h), Op.min)
         tt(sa, ind(a("lutq"), l8), half("kh", h), Op.mult)
         for u, z in enumerate(("z1", "zb")):
             mm(a(m, packed + 64 * u, packed + 64 * u + 64), a(z, 15, 143), a("sel", sf[2] + 64 * u, sf[2] + 64 * u + 64), True, True)
-        mm(same, a("idn"), a("tm"), True, False)
-        mm(same, a("gm"), sk, False, True)
+        mm(same, a("idn"), a3("tm", wide - 16, wide - 16 + wide // 4), True, False)
+        if wide == 16:
+            mm(same, a("gm"), sk, False, True)
+        for q in range(8 * (wide > 16)):
+            mm(a(m, same[2] + 32 * q + 16 - 16 * (q % 2), same[2] + 32 * q + 32), a("gm"), a("sel", sk[2] + 32 * (q // 2), sk[2] + 16 * q + 16), False, q == 7)
+        mm(a(m, same[2] + wide - 1, same[3], wide), a("idn"), a("ones", 0, 8), True, True)
         for i in range(16):
             mm(lists, a("z1", 15 - i, 143 - i), a("sel", 384 * h + i, 384 * h + 384, 16), i == 0, i == 15)
-        copy((T.pn16[:, :, 8:16] if h else T.pn16[:, ::-1, 0:8], "pn16", 8 * h, 8 * h + 8, 24), lists)
-        fetch(half("nr", h, 264), a(m, 16 - 16 * h, 280 - 16 * h), "nr%d" % h)
+        if "pn" in ONS:
+            act(half("pn16", h, 24), lists, AF.Copy)
+        else:
+            copy(half("pn16", h, 24), lists)
+        fetch(a("nr", at, at + 136 + 8 * wide), a(m, 16, 152 + 8 * wide) if h else a(m, at, 392), "nr%d" % h)
 
         now_[0] = "near%d" % h
-        act(half("xn", h), ind(table, names16(2, c0, c1)), AF.Copy)
+        act(half("xn", h), ind(table, names16(2, h)), AF.Copy)
         mm(code, half("xn", h), a("idn"), True, True)
         fetch(half("xr", h), code, "xr%d" % h)
         fetch(a("fl", 144 * h, 144 * h + 144, 18), names, "fl%d" % h, 8192.0)
@@ -347,25 +393,33 @@ def rank_program(g, core, T, topo):
             if lo // 2 != h:
                 continue
             scan(back("ms", 72 * lo, 72 * hi), back(cb, 256 + 72 * (lo - c0), 256 + 72 * (hi - c0)), back("rp", 0, 72 * (hi - lo)), -4096.0, Op.min, Op.max)
-            ts(part("o16", lo, hi, 4), a("ms", 72 * lo, 72 * hi, 18), 2048.0, Op.add)
-            tt(part("fr", lo, hi), ind(a("wt%d" % h), part("o16", lo, hi, 4)), a("nr", 8 + 256 * h + 64 * lo, 8 + 256 * h + 64 * hi), Op.add)
+            if "o16" in ONS:
+                act(part("o16", lo, hi, 4), a("ms", 72 * lo, 72 * hi, 18), AF.Copy, bias=2048.0)
+            else:
+                ts(part("o16", lo, hi, 4), a("ms", 72 * lo, 72 * hi, 18), 2048.0, Op.add)
+            tt(part("fr", lo, hi), ind(a("wt%d" % h), part("o16", lo, hi, 4)), a("nr", news + 64 * (lo - c0), news + 64 * (hi - c0)), Op.add)
             for c in range(hi - 1, lo - 1, -1):
+                to = half("yk32" if last else "ks_%d" % t, c, 64)
                 if c % 2 == 0:
                     ts(half("fu", c, 64), half("fr", c, 64), 4095, Op.bitwise_and)
-                    if not last:
-                        turn(half("ks_%d" % t, c, 64), half("fu", c, 64), "ks")
+                    turn(to, half("fu", c, 64), "ks")
                 elif last:
                     ts(half("fu", c, 64), half("fr", c, 64), 12, Op.logical_shift_right)
+                    turn(to, half("fu", c, 64), "ks")
+                elif "hi" in ONS:
+                    act(to, half("fr", c, 64), AF.Copy, scale=2.0 ** -12)
                 else:
-                    ts(half("ks_%d" % t, c, 64), half("fr", c, 64), 2.0 ** -12, Op.mult)
+                    ts(to, half("fr", c, 64), 2.0 ** -12, Op.mult)
             if last:
-                copy(part("yk32", lo, hi), part("fu", lo, hi))
                 dmas("y", "ok%d" % lo, [(T.yk[:, 64 * lo:64 * hi], T.yk32[:, 64 * lo:64 * hi])], [], [part("yk32", lo, hi)], 2 ** 15 * (hi - lo))
             else:
                 send(part("k16_%d" % (t + 1), lo, hi), part("ks_%d" % t, lo, hi), "k%d_%d" % (t + 1, lo), nxt, prv)
 
         now_[0] = "phages%d" % h
-        ts(half("pa", h), sa, -1.0, Op.mult, 0.0, Op.max)
+        if "pa" in ONS:
+            act(half("pa", h), sa, AF.Relu, scale=-1.0)
+        else:
+            ts(half("pa", h), sa, -1.0, Op.mult, 0.0, Op.max)
         for lo, hi in PHAGES:
             if lo == c0:
                 factor = a("e3", 256 + 64 * lo, 256 + 64 * hi) if EB == 3 else a(m, 320, 448)
@@ -383,29 +437,33 @@ def rank_program(g, core, T, topo):
         now_[0] = "writes%d" % h
         for lo, hi in WRITES:
             if lo == c0:
-                yk, c1_, wv = part("yk_", lo, hi), part("c1", lo, hi), part("wv", lo, hi)
-                less = 64.0 * (h in SIDE)
-                act(yk, ind(table, names16(0, lo, hi)), AF.Copy, bias=-less)
-                tt(part("dk", lo, hi), ind(table, names16(1, lo, hi)), yk, Op.subtract)
-                act(part("adk", lo, hi), part("dk", lo, hi), AF.Abs, bias=-less)
-                if less:
-                    act(c1_, part("adk", lo, hi), AF.Sign, scale=-1.0, bias=32.5)
-                    mm(same, a("idn"), yk, True, False)
-                    mm(same, a("i64"), c1_, False, True)
-                    act(wv, same, AF.Copy)
+                yk, c1_, wv = part("yk_", lo, hi), part("c1", lo, hi), half("ys", 3 * h)
+                if h in FLIP:
+                    dk, turned = a(m, 304, 432), a(cb, 128, 256)
+                    act(half("ys", h, 256), ind(table, half("pn16", 2 * h, 16)), AF.Copy)
+                    act(half("sg", h), wv, AF.Sign, scale=-1.0, bias=127.5)
+                    mm(dk, a("idn"), half("ys", 1 + h), True, False)
+                    mm(dk, a("idm"), wv, False, True)
+                    mm(turned, a("i128"), half("sg", h), True, True)
+                    ts(c1_, dk, ROUND, Op.add, ROUND, Op.is_equal)
+                    tt(half("vv", h), c1_, turned, Op.mult)
                 else:
-                    ts(c1_, part("adk", lo, hi), 32.0, Op.is_le, -128.0, Op.mult)
-                    tt(wv, ind(table, names16(0, lo, hi)), c1_, Op.add)
-                ts(part("vv", lo, hi), wv, 0.0, Op.is_lt, 256.0, Op.mult)
+                    act(yk, ind(table, names16(0, h)), AF.Copy, bias=-MID)
+                    tt(part("dk", lo, hi), ind(table, names16(1, h)), yk, Op.subtract)
+                    ts(c1_, part("dk", lo, hi), MID, Op.is_equal, -128.0, Op.mult)
+                    tt(wv, ind(table, names16(0, h)), c1_, Op.add)
+                    ts(part("vv", lo, hi), wv, 0.0, Op.is_lt, 256.0, Op.mult)
         for lo, hi in EQUAL:
             if lo == c0:
-                whole = hi - lo > 2
-                tt(part("eq", lo, hi), ind(a("nr") if whole else names, a("bl", 0, 4 * (hi - lo))), a("nr", 136 + 64 * lo, 136 + 64 * hi), Op.is_equal)
-                o = half("e3", h) if EB == 3 else same
-                mm(o, a("idk"), part("eq", lo, hi), True, False)
-                mm(a(o[1], o[2] + 15, o[3], 16), a("idf"), names, False, True)
-                scan(part("mw", lo, hi), a("r0", 0, 64 * (hi - lo)), o, 0.0, Op.mult, Op.subtract)
-                ts(a("w16", 8 * lo, 8 * hi, 2), a("mw", 64 * lo + 15, 64 * hi, 16), 16.0, Op.add, a("lf", 0, 1), Op.max)
+                x0, x1 = 256 * h, 256 * h + 8 * wide
+                if wide == 16:
+                    act(a("nm", x0 + 14, x1, 16), names, AF.Relu, bias=32.0)
+                else:
+                    act(a("nm", x0 + 62, x1, 64), a("nr", names[2] + 1, names[3], 2), AF.Relu, bias=32.0)
+                    act(a("nm", x0 + 30, x1, 64), a("nr", names[2], names[3], 2), AF.Relu, bias=a("l15", 1, 2))
+                tt(a("eq", x0, x1), ind(a("nr", 384 + 8 * h, 400 + 8 * h), a("bl", 16 * h, 16 * h + wide // 2)), a("nr", rows, rows + 8 * wide), Op.not_equal)
+                scan(back("mw", x0, x1), back("nm", x0, x1), back("eq", x0, x1), 0.0, Op.add, Op.mult)
+                ts(a("w16", 16 * h, 16 * h + 256 // wide, 32 // wide), a("mw", x0, x1, wide), a("lf", 0, 1), Op.max)
 
     turns = [0]
     for t in range(RO):
@@ -413,17 +471,20 @@ def rank_program(g, core, T, topo):
         for h in (1, 0):
             half_round(t, h)
         now_[0] = "table"
-        for q in range(15, -1, -1):
-            tt(ind(a("xt"), a("w16", 2 * q, 2 * q + 1)), half("wv", q, 16), half("vv", q, 16), Op.add)
+        for h in (1, 0):
+            wide = WIDE[h]
+            for b in range(128 // wide - 1, -1, -1):
+                tt(ind(a("xt"), a("w16", 16 * h + 2 * b, 16 * h + 2 * b + wide // 16)), a("ys", 384 * h + wide * b, 384 * h + wide * b + wide),
+                   a("vv", 128 * h + wide * b, 128 * h + wide * b + wide), Op.add)
         if t == RO - 1:
             dmas("y", "oy", [(T.yx[:], table[0])], [], [table], 2 ** 19)
         else:
-            act(a("jk"), a("mi", 15, 256, 16), AF.Sign, acc=a("ac", t, t + 1), scale=-1.0, bias=LOW)
+            act(a("jk"), a("nr", 384, 408), AF.Sign, acc=a("ac", t, t + 1), scale=-1.0, bias=-10240.0)
             for u in range(t + 1):
-                mm(a("m0", 300, 301), a("gmf"), a("ac", u, u + 1), u == 0, u == t)
-            ts(a("aa"), a("m0", 300, 301), 2.0 ** 20, Op.mult, 2.0 ** 28 * (t + 1), Op.add)
-            ts(a("ab"), a("aa"), 15 << 21, Op.bitwise_and)
-            turn(a("thr"), a("ab"), "thr")
+                mm(a("m0", 500, 501), a("gmf"), a("ac", u, u + 1), u == 0, u == t)
+            ts(a("aa"), a("big"), a("m0", 500, 501), Op.mult, 384 * 2.0 ** 18 * (t + 1), Op.add)
+            ts(a("ab"), a("aa"), 15 << 19, Op.bitwise_and)
+            ts(a("rst", 0, 128, 16), a("ab"), TOP, Op.add)
 
     def clash(hist, q, outs, ins, banks):
         for kind, lst in (("w", outs), ("r", ins)):
@@ -431,7 +492,7 @@ def rank_program(g, core, T, topo):
                 for k2, lo, hi, q2, who in hist.get(x[1], ()):
                     same = q2 == q and q != "dma"
                     if banks and x[1] in PSUM and not same or not (k2 == kind == "r" or hi <= x[2] or lo >= x[3]):
-                        yield who, same and q == "p"
+                        yield who, same and (q == "p" or k2 + kind in FREE)
 
     def note(hist, q, outs, ins, who):
         for kind, lst in (("w", outs), ("r", ins)):
@@ -495,51 +556,74 @@ def rank_program(g, core, T, topo):
         ends = place([-way[n] - x["lead"] for n, x in enumerate(tasks)])
         start = [ends[n] - x["cost"] for n, x in enumerate(tasks)]
 
-        briefs = [[(x["q"], (x["cost"] + (pick - 1) * x["picks"]) * (far if x["moves"] else slow * {"p": pe, "s": sc}.get(x["q"], 1)), x["after"] * far,
-                    [(w, tasks[w]["after"] * far + d * hop - e * slow * pe) for w, (d, e) in x["gaps"].items()], tuple(sorted(x["banks"])),
-                    x["moves"] and (x["moves"][0] * far, sum(x["moves"]) * far)) for x in tasks] for slow, far, pe, pick, sc, hop in SPEEDS]
+        def direct(n, w):
+            return not any(w in before[u] and before[u][w] >= 0 and d >= 0 and before[u][w] + tasks[u]["cost"] + d >= before[n][w] for u, d in before[n].items())
 
-        def length(order, brief, hop, why=None):
-            end, free, bank, engines, last = [0] * len(tasks), dict.fromkeys(Q, (0, -1)), dict.fromkeys(PSUM, ("p", 0, -1)), (0, -1), (0, -1)
-            for n in order:
-                q, cost, after, needs, banks, moves = brief[n]
-                at, who = free[q]
-                for w, d in needs:
-                    if end[w] + d > at:
-                        at, who = end[w] + d, w
-                for b in banks:
-                    if bank[b][0] != q and bank[b][1] > at:
-                        at, who = bank[b][1:]
-                free[q] = (at + cost, n)
-                if moves:
-                    if engines[0] - moves[0] > at:
-                        at, who = engines[0] - moves[0], engines[1]
-                    engines = (at + moves[1], n)
-                end[n] = at = at + cost
-                for b in banks:
-                    bank[b] = (q, at + hop, n)
-                if at + after > last[0]:
-                    last = (at + after, n)
-                if why:
+        briefs = [[(x["q"], (x["cost"] + (pick - 1) * x["picks"]) * (far if x["moves"] else slow * {"p": pe, "s": sc}.get(x["q"], 1)),
+                    [(w, tasks[w]["after"] * far + d * hop - e * slow * pe) for w, (d, e) in x["gaps"].items() if direct(n, w)], tuple(sorted(x["banks"])),
+                    x["moves"] and (x["moves"][0] * far, sum(x["moves"]) * far)) for n, x in enumerate(tasks)] for slow, far, pe, pick, sc, hop in SPEEDS]
+        finals = [n for n in range(len(tasks)) if not nexts[n]]
+
+        def length(order, mix, old=None, same=0):
+            brief, far, hop = briefs[mix], SPEEDS[mix][1], HOP * SPEEDS[mix][5]
+            if old:
+                marks = old[3][:same // MARK + 1]
+                end, why, free, bank, engines = old[2][:], old[1][:], dict(marks[-1][0]), dict(marks[-1][1]), marks[-1][2]
+                marks = marks[:-1]
+            else:
+                end, why, free, bank, engines = [0] * (len(tasks) + 1), [-1] * (len(tasks) + 1), dict.fromkeys(Q, (0, -1)), dict.fromkeys(PSUM, ("p", 0, -1)), (0, -1)
+                marks = []
+            for k in range(MARK * len(marks), len(order), MARK):
+                marks.append((dict(free), dict(bank), engines))
+                for n in order[k:k + MARK]:
+                    q, cost, needs, banks, moves = brief[n]
+                    at, who = free[q]
+                    for w, d in needs:
+                        d += end[w]
+                        if d > at:
+                            at, who = d, w
+                    if banks:
+                        for b in banks:
+                            o = bank[b]
+                            if o[1] > at and o[0] != q:
+                                at, who = o[1:]
+                        o = (q, at + cost + hop, n)
+                        for b in banks:
+                            bank[b] = o
+                    free[q] = (at + cost, n)
+                    if moves:
+                        if engines[0] - moves[0] > at:
+                            at, who = engines[0] - moves[0], engines[1]
+                        engines = (at + moves[1], n)
+                    end[n] = at + cost
                     why[n] = who
-            if why:
-                why[-1] = last[1]
-            return last[0]
+            last, why[-1] = max((end[n] + tasks[n]["after"] * far, n) for n in finals)
+            return last, why, end, marks
 
-        def total(order):
-            return sum(length(order, b, HOP * x[5]) / sum(x[:2]) for b, x in zip(briefs, SPEEDS))
+        def total(order, mixes=range(6), limit=None, same=0):
+            new, gap = [], 0
+            for k, mix in enumerate(mixes):
+                new.append(length(order, mix, runs[k] if same else None, same))
+                if limit is not None:
+                    gap += (new[k][0] - runs[k][0]) / sum(SPEEDS[mix][:2]) * 6 / len(mixes)
+                    if gap > limit + SLACK * (len(mixes) - 1 - k):
+                        return 1e12
+            tried[:] = new
+            return sum(r[0] / sum(SPEEDS[x][:2]) for r, x in zip(new, mixes)) * 6 / len(mixes)
 
         def blocks(order):
             found = []
-            for b, x in zip(briefs, SPEEDS):
-                why = [-1] * (len(tasks) + 1)
-                length(order, b, HOP * x[5], why)
+            runs[:] = tried
+            for run in runs:
+                why = run[1]
                 n = why[-1]
                 while why[n] >= 0:
                     if why[n] not in before[n]:
                         found.append((why[n], n))
                     n = why[n]
             return found
+
+        runs, tried = [], []
 
         rng = np.random.default_rng(SEED)
 
@@ -556,14 +640,23 @@ def rank_program(g, core, T, topo):
         where = np.array([names.index(x) for x in step])
         times = np.array([table_[x] for x in names])
         shift = np.array([first[0] * (x["stage"] != "start") + (first[2] - first[1]) * x["round"] for x in tasks])
+        if HAND:
+            shift = np.array([first[0] * (x["stage"] != "start") + HAND["period"] * x["round"] for x in tasks])
+            for k, x in enumerate(names):
+                if x[0] != "start":
+                    v = HAND.get("%s%s%d" % x[1:4], 3000)
+                    times[k] = 12 * (v[x[4] - 1] if isinstance(v, list) else v)
         order = in_order((times[where] + shift).tolist())
-        best = now = (total(order), order, times)
+        best = now = (total(order, SOME), order, times)
         INFO["first"] = now[0]
         pairs = blocks(order)
         for n in range(STEPS):
             if n == STEPS - APART:
                 own = np.array([where[k] + len(names) * CLASS[x["round"]] for k, x in enumerate(tasks)])
                 now, times, where = best[:2], np.tile(best[2], 3), own
+                best = now + (times,)
+                total(now[1], SOME)
+                pairs = blocks(now[1])
             new = times.copy()
             if rng.random() < AIM:
                 u, v = pairs[int(rng.integers(len(pairs)))]
@@ -581,16 +674,118 @@ def rank_program(g, core, T, topo):
                 at = int(rng.integers(len(tasks)))
                 new[np.unique(where[at:at + (1 if rng.random() < 0.6 else int(rng.integers(2, 12)))])] += rng.normal() * (150, 500, 1500)[int(rng.integers(3))]
             order = in_order((new[where] + shift).tolist())
-            cost = total(order)
-            if cost <= now[0] + (WARM * (1 - n / (STEPS - APART)) if n < STEPS - APART else MILD * (STEPS - n) / APART) * rng.exponential():
-                if cost != now[0]:
-                    pairs = blocks(order)
+            if order == now[1]:
+                times = new
+                continue
+            limit = (WARM * (1 - n / (STEPS - APART)) if n < STEPS - APART else MILD * (STEPS - n) / APART) * rng.exponential()
+            cost = total(order, SOME, limit)
+            if cost <= now[0] + limit:
+                pairs = blocks(order)
                 now, times = (cost, order), new
                 if cost < best[0]:
                     best = (cost, order, new)
         INFO["steps"] = best[0]
 
+        def pack(key, mix, back_):
+            brief, far, hop = briefs[mix], SPEEDS[mix][1], HOP * SPEEDS[mix][5]
+            order = in_order(key) if not back_ else in_order([-k for k in key])[::-1]
+            busy = {r: ([], [], []) for r in list(Q) + list(PSUM) + ["engines"]}
+            end = [0] * len(tasks)
+            for n in order:
+                q, cost, needs, banks, moves = brief[n]
+                at = tasks[n]["after"] * far if back_ else 0
+                for w, d in (later[mix][n] if back_ else needs):
+                    d += end[w]
+                    if d > at:
+                        at = d
+                held = [(busy[q], 0, cost, None)] + [(busy[b], -hop, cost + hop, q) for b in banks]
+                if moves:
+                    held.append((busy["engines"], cost - moves[1], cost - moves[0], None) if back_ else (busy["engines"], moves[0], moves[1], None))
+                again = True
+                while again:
+                    again = False
+                    for (los, his, qs), lo, hi, mine in held:
+                        k = find(his, at + lo)
+                        while k < len(los) and los[k] < at + hi:
+                            if qs[k] != mine:
+                                at, again = his[k] - lo, True
+                            k += 1
+                for (los, his, qs), lo, hi, mine in held:
+                    if mine:
+                        lo, hi = 0, cost
+                    k = find(his, at + lo)
+                    los.insert(k, at + lo)
+                    his.insert(k, at + hi)
+                    qs.insert(k, q)
+                end[n] = at + cost
+            return end
+
+        def find(xs, x):
+            lo, hi = 0, len(xs)
+            while lo < hi:
+                mid = (lo + hi) // 2
+                if xs[mid] > x + 1e-6:
+                    hi = mid
+                else:
+                    lo = mid + 1
+            return lo
+
+        later = [[[] for x in tasks] for b in briefs]
+        for mix, brief in enumerate(briefs):
+            for n, x in enumerate(brief):
+                for w, d in x[2]:
+                    later[mix][w].append((n, d))
+        def decoded(times):
+            end = pack((times[where] + shift).tolist(), BASE, False)
+            order = in_order([e - x[1] for e, x in zip(end, briefs[BASE])])
+            return (total(order, SOME), order, times)
+
+        if TRIES:
+            now = best = decoded(best[2])
+            pairs = blocks(now[1])
+        for n in range(TRIES):
+            if n == TRIES - TRIES // 4:
+                own = np.array([where[k] + len(names) * CLASS[x["round"]] for k, x in enumerate(tasks)])
+                where = own
+                now = best = best[:2] + (np.tile(best[2], 3),)
+            new = now[2].copy()
+            if rng.random() < AIM2:
+                u, v = pairs[int(rng.integers(len(pairs)))]
+                key = new[where] + shift
+                if rng.random() < 0.5:
+                    new[where[v]] = min(key[u], key[v]) - 1 - rng.exponential() * 100 - shift[v]
+                else:
+                    at, todo = max(key[u], key[v]) + 1 + rng.exponential() * 100, [u]
+                    while todo:
+                        w = todo.pop()
+                        if key[w] < at:
+                            key[w], new[where[w]] = at, at - shift[w]
+                            todo += nexts[w]
+            else:
+                at = int(rng.integers(len(tasks)))
+                new[np.unique(where[at:at + (1 if rng.random() < 0.5 else int(rng.integers(2, 20)))])] += rng.normal() * (200, 700, 2000)[int(rng.integers(3))]
+            new = decoded(new)
+            if new[0] <= now[0] + WARM2 * (1 - n / TRIES) * rng.exponential():
+                pairs, now = blocks(new[1]) or pairs, new
+                if new[0] < best[0]:
+                    best = new
+        best = (total(best[1]), best[1])
+        INFO["tries"] = best[0]
         now = best = best[:2]
+        for n in range(PACKS):
+            mix = MIXES[int(rng.integers(len(MIXES)))]
+            end = length(now[1], mix)[2]
+            noise = rng.normal(size=len(tasks)) * NOISE[int(rng.integers(len(NOISE)))] * (rng.random(len(tasks)) < SHARE)
+            end = pack([-end[k] + noise[k] for k in range(len(tasks))], mix, True)
+            end = pack([-e for e in end], mix, False)
+            order = in_order([e - x[1] for e, x in zip(end, briefs[mix])])
+            new = (total(order), order)
+            if new[0] <= now[0] + LOOSE * (1 - n / PACKS) * rng.exponential():
+                now, best = new, min(best, new)
+        INFO["packs"] = best[0]
+
+        now = best = best[:2]
+        total(now[1])
         pairs = blocks(now[1])
         for n in range(MOVES):
             order = now[1]
@@ -614,21 +809,18 @@ def rank_program(g, core, T, topo):
                         moved.add(w)
                 run = [w for w in run if w not in moved] + [w for w in run if w in moved]
             order = order[:lo] + run + order[hi + 1:]
-            new = (total(order), order)
-            if new[0] <= now[0] + HEAT * (1 - n / MOVES) * rng.exponential():
-                if new[0] != now[0]:
-                    pairs = blocks(order)
+            if order == now[1]:
+                continue
+            limit = HEAT * (1 - n / MOVES) * rng.exponential()
+            new = (total(order, range(6), limit, lo), order)
+            if new[0] <= now[0] + limit:
+                pairs = blocks(order)
                 now, best = new, min(best, new)
         INFO["total"] = best[0]
-        INFO["best"] = [int(length(best[1], b, HOP * x[5]) * 0.83) for b, x in zip(briefs, SPEEDS)]
-        why = [-1] * (len(tasks) + 1)
-        length(best[1], briefs[-1], HOP * SPEEDS[-1][1], why)
-        n, INFO["path"] = why[-1], []
-        INFO["busy"] = {q: int(sum(b[1] for b in briefs[-1] if b[0] == q) * 0.83) for q in Q}
-        while n >= 0:
-            o = (tasks[n]["calls"][0][1] + tasks[n]["calls"][0][2])[0]
-            INFO["path"].append("%s%s%s:%d %d" % ("" if why[n] in before[n] else "*", tasks[n]["q"].upper(), o[1], o[2], briefs[-1][n][1] * 0.83))
-            n = why[n]
+        INFO["best"] = [int(length(best[1], mix)[0] * 0.83) for mix in range(len(SPEEDS))]
+        end = length(best[1], SHOW)[2]
+        INFO["line"] = [(int((end[n] - briefs[SHOW][n][1]) * 0.83), int(briefs[SHOW][n][1] * 0.83), tasks[n]["q"], step[n][2], step[n][3], tasks[n]["round"]) for n in best[1]]
+        INFO["all"] = [{q: int(sum(b[1] for b in br if b[0] == q) * 0.83) for q in Q} for br in briefs]
         return best[1]
 
     if not PLAN:

@@ -5,23 +5,20 @@ RO = 4
 F, B, H, I, U = "float32", "bfloat16", "float16", "int32", "uint16"
 SCRATCH = {}
 for _n, _w, _d in (
-        ("xt", 2080, B), ("nk", 256, I), ("np_", 256, I), ("yg", 4096, B), ("ph_", 256, H), ("kh", 256, H), ("sn", 256, B),
-        ("mi", 256, I), ("cl", 16, I), ("v8", 16, I), ("l8", 16, U), ("sel", 768, H),
-        ("nr", 792, F), ("xn", 256, B), ("xr", 256, B), ("eq", 512, B), ("mw", 512, U), ("nm", 512, U), ("w16", 32, U),
-        ("yk_", 256, F), ("dk", 256, B), ("c1", 256, B),
-        ("pn16", 48, U), ("ys", 512, B), ("sg", 256, B), ("idm", 128, B), ("i128", 128, B), ("vv", 256, B), ("pa", 256, H), ("pt", 256, I), ("pn", 256, I), ("yp32", 256, F),
-        ("wt0", 1216, F), ("wt1", 1216, F), ("fl", 288, B), ("ms", 288, F), ("o16", 16, U), ("fr", 256, I), ("fu", 256, I),
-        ("yk32", 256, F), ("jk", 24, B), ("ac", 4, F), ("aa", 8, I), ("ab", 8, I), ("big", 8, F),
+        ("xt_0", 2080, B), ("xt_1", 2080, B), ("nk", 256, I), ("np_", 256, I), ("yg", 4096, B), ("ph_", 256, H), ("kh", 256, H),
+        ("sn", 256, B), ("sg", 256, H), ("mi", 256, I), ("v8", 16, I), ("l8", 16, U), ("sel", 768, H), ("pn16", 48, U), ("nr", 816, F),
+        ("xn", 256, B), ("xr", 256, B), ("fl", 288, B), ("ms", 288, F), ("o16", 16, U), ("wt0", 1216, F), ("wt1", 1216, F),
+        ("fr", 256, I), ("fu", 256, I), ("yk32", 256, F), ("pa", 256, H), ("pt", 256, I), ("pn", 256, I), ("yp32", 256, F),
+        ("cy", 512, B), ("dk", 256, B), ("ys", 512, B), ("vv", 256, B), ("eq", 512, B), ("nm", 512, U), ("mw", 512, U),
+        ("w16", 16, U), ("jk", 16, B), ("ac", 4, F), ("aa", 8, I), ("ab", 8, I),
         ("pi", 2, I), ("li", 2, I), ("lf", 2, F), ("l15", 2, F), ("ones", 128, B), ("neg", 512, B), ("gm", 128, B), ("idn", 128, B),
-        ("idk", 128, B), ("gmf", 128, F), ("s15", 128, B), ("s5k", 128, B), ("qu", 128, B),
-        ("z1", 143, B), ("zd", 143, B), ("zb", 143, B), ("it", 256, I), ("iu", 16, I),
-        ("cj", 128, B), ("rst", 128, F), ("ri", 144, I), ("rp", 144, F), ("ex", 2048, B), ("ij", 128, I), ("iq", 32, I),
-        ("bl", 32, U), ("i3", 192, I), ("i4", 192, I), ("nil", 64, F),
-        ("lutf", 256, B), ("lutk", 256, B), ("lutq", 256, B)):
+        ("idk", 128, B), ("idd", 128, B), ("i128", 128, B), ("n128", 128, B), ("gmf", 128, F), ("s15", 128, B), ("s5k", 128, B),
+        ("qu", 128, B), ("z1", 143, B), ("zd", 143, B), ("zb", 143, B), ("cj", 128, B), ("rst", 128, F), ("ri", 144, I), ("rp", 144, F),
+        ("ex", 2048, B), ("tm", 256, B), ("lane", 128, B), ("ij", 128, I), ("i3", 192, I), ("i4", 192, I), ("nil", 64, F), ("sc", 256, B),
+        ("iq", 16, I), ("iu", 8, I), ("bl", 16, U), ("lutf", 256, B), ("lutk", 256, B), ("lutq", 256, B)):
     SCRATCH[_n] = ("sbuf", [128, _w], _d)
 for _n, _w in (("d3", 256), ("a3", 256), ("ae", 288)):
     SCRATCH[_n] = ("sbuf", [128, 16, _w], B)
-SCRATCH["tm"] = ("sbuf", [128, 24, 32], B)
 for _h in range(2):
     SCRATCH["kd%d" % _h] = ("dram", [8, 33, 64], F)
 for _t in range(RO):
@@ -30,48 +27,60 @@ for _t in range(RO):
 PSUM = ("e0", "e1", "e2", "e3", "c0", "c1_", "m0", "m1")
 for _n in PSUM:
     SCRATCH[_n] = ("psum", [128, 512], F)
-SEMAPHORES = (["v", "s", "p", "g", "lx", "oy", "kz"] + [x + h for x in ("lp", "lk", "kd", "wd") for h in "01"] + [x + h for x in ("ok", "op") for h in "0123"]
-              + ["%s%s%d_%d" % (y, x, t, h) for x in "kp" for t in range(1, RO) for h in range(4) for y in "al"])
-NEARS = ((2, 4), (0, 2))
-PHAGES = ((2, 4), (0, 2))
-WRITES = ((2, 4), (0, 2))
-EQUAL = ((2, 4), (0, 2))
-RELU = (2,)
-WHOLE = (1,)
-BEHIND = {1: 2}
+SEMAPHORES = (["v", "s", "p", "g", "lx", "oy", "kz"] + [x + h for x in ("lp", "lk", "kd", "wd", "ok", "op") for h in "01"]
+              + ["%s%s%d" % (y, x, t) for x in ("k0_", "k1_", "p_") for t in range(1, RO) for y in "al"])
+FIRST = "pkpk"
+RELU = 2
 PIECES = {2: ((0, 1), (1, 4)), 3: ((0, 1), (1, 4))}
 PARTS = {1: ((0, 2), (2, 4))}
-CUTS = {2: ((0, 1), (1, 4)), 3: ((0, 2), (2, 4)), 1: ((0, 2), (2, 4))}
-POOL = ("kh", "ph", "ps", "thr", "yp", "k0", "p0")
-AGAIN = True
-WIDE = (16, 16)
-SPARE = ("nm", "gmf", "s5k", "idk", "zd", "zb", "idm", "i128", "ae", "rst", "lutf", "lutk")
-SIDE = ()
-FIRST = "kp"
-ONV = ()
-SUMS = ()
-AHEAD = {}
-LEAD = 4000
-EB = 3
-AIM, REACH, HEAT, WARM = 0.8, 8, 90, 600
-STEPS, MOVES, SEED, PLAN = 12000, 16000, 8, []
-APART, MILD, CLASS = 3000, 150, (0, 1, 1, 2)
-FREE = ()
-SHOW = 0
-MARK, SLACK = 32, 150
-DIRECT = False
-ONS = ()
-HAND = {}
-TRIES, AIM2, WARM2, BASE, SOME = 0, 0.6, 1500, 6, (0, 1, 2, 3, 4, 5)
-PACKS, MIXES, NOISE, SHARE, LOOSE = 0, (0, 1, 2, 3, 4, 5), (0, 100, 300), 0.2, 1000
-FLIP = ()
-SPEEDS = ((1.05, 0.95, 0.85, 1.0, 1.0, 0.95), (1.25, 0.8, 1.1, 1.3, 0.95, 1.2), (1.4, 1.3, 1.0, 0.9, 1.0, 0.7), (1.55, 0.8, 1.1, 1.1, 0.92, 0.8),
-          (1.05, 1.5, 0.9, 0.8, 1.0, 1.3), (1.3, 0.7, 1.1, 0.75, 1.0, 0.6), (1.2, 1.1, 1.0, 1.0, 1.0, 1.0))
+COPY = 4
+SPARE = ("nm", "ae", "rst", "lutf", "lutk")
+AIM, REACH, HEAT, WARM, MILD, LOOSE = 0.8, 8, 40, 250, 100, 1500
+STEPS, APART, MOVES, SEED, CLASS = 8000, 2500, 3500, 3, (0, 1, 1, 2)
+MARK, SLACK, AFTER, ANEW = 32, 400, 128, 1000
+TIMES = """first=661 period=2517 c0:gkh0.1=419 c0:pc00.1=-47 c0:pc00.2=858 c0:pc00.3=1186 c0:pc064.1=1052 c0:pe3256.1=460 c0:pe3320.1=456
+c0:pm0152.1=858 c0:pm0216.1=1057 c0:sa30.1=1145 c0:sa31024.1=875 c0:sa31536.1=897 c0:ssn0.1=1006 c0:swt00.1=1047 c0:syg0.1=176
+c0:syg1024.1=286 c0:vd30.1=720 c0:vd31024.1=898 c0:vd31280.1=862 c0:vd31536.1=863 c0:vd31792.1=1063 c0:vd3256.1=533 c0:vd3512.1=536
+c0:vd3768.1=542 c0:ykd00.1=740 c0:ywt0128.1=1186 c1:gkh128.1=287 c1:pc1_0.1=-171 c1:pc1_0.2=729 c1:pc1_0.3=836 c1:pc1_0.4=810
+c1:pc1_64.1=855 c1:pe3384.1=487 c1:pe3448.1=225 c1:pm1152.1=454 c1:pm1216.1=485 c1:sa33072.1=730 c1:ssg128.1=773 c1:ssn128.1=785
+c1:swt10.1=271 c1:syg2048.1=136 c1:syg2304.1=175 c1:syg3072.1=176 c1:syg3328.1=169 c1:va32048.1=483 c1:vd32048.1=206 c1:vd32304.1=203
+c1:vd32560.1=9 c1:vd32816.1=12 c1:vd33072.1=232 c1:vd33328.1=227 c1:vd33584.1=222 c1:vd33840.1=209 c1:ykd10.1=382 c1:ywt1128.1=934
+l0:gph_0.1=419 l0:pm00.1=1447 l0:pm0152.1=1322 l0:pm024.1=1315 l0:snr8.1=1794 l0:vl80.1=1356 l0:vmi0.1=1229 l0:vpn160.1=1529
+l0:vsel0.1=1351 l0:vsel128.1=1325 l0:vsel256.1=1320 l0:vv80.1=1098 l1:gph_128.1=1034 l1:pm10.1=1098 l1:pm1152.1=1303 l1:pm124.1=1305
+l1:snr416.1=1340 l1:vl88.1=1067 l1:vmi128.1=883 l1:vpn1624.1=1171 l1:vsel384.1=949 l1:vsel512.1=957 l1:vsel640.1=954 l1:vv88.1=910
+n0:gfl0.1=1951 n0:gk16_0.1=2519 n0:pc00.1=1770 n0:pc0256.1=2211 n0:pc0328.1=2187 n0:pe0.1=1726 n0:pe0.2=1936 n0:pe0.3=1753
+n0:pe0.4=1800 n0:pe0.5=1973 n0:pe0.6=1984 n0:pe0.7=2091 n0:pe0.8=1992 n0:sae0.1=2039 n0:sae1152.1=1799 n0:sae1728.1=2038
+n0:sae576.1=2219 n0:sxn0.1=1665 n0:sxr0.1=1848 n0:vfr0.1=2328 n0:vfu0.1=2330 n0:vfu64.1=2329 n0:vks_0.1=2556 n0:vks_64.1=2549
+n0:vms0.1=2247 n0:vo160.1=2309 n0:vyk320.1=2443 n0:vyk3264.1=2342 n0:yyk320.1=2607 n1:gfl144.1=1485 n1:gk16_128.1=2135
+n1:gyk32128.1=2087 n1:gyk32192.1=2149 n1:pc1_0.1=1307 n1:pc1_256.1=1752 n1:pc1_328.1=1794 n1:pe0.1=446 n1:pe0.2=1325 n1:pe0.3=56
+n1:pe0.4=1440 n1:pe0.5=231 n1:pe0.6=1452 n1:pe0.7=1534 n1:pe0.8=1728 n1:sae2304.1=1453 n1:sae2880.1=1533 n1:sae3456.1=1600
+n1:sae4032.1=1728 n1:sxn128.1=1271 n1:sxr128.1=1380 n1:vfr128.1=2028 n1:vfu128.1=2077 n1:vfu192.1=2071 n1:vks_128.1=2189
+n1:vks_192.1=2080 n1:vms144.1=1906 n1:vo168.1=1975 n1:yyk32128.1=2080 p0:gp16_0.1=1832 p0:gps_0.1=1827 p0:gyp320.1=1835
+p0:pc0128.1=1535 p0:vpa0.1=1536 p0:vpn0.1=1627 p0:vpt0.1=1596 p0:yyp320.1=1835 p1:gps_128.1=1485 p1:gyp32128.1=1440
+p1:pc1_128.1=1134 p1:vpa128.1=1087 p1:vpn128.1=1374 p1:vpt128.1=1358 p1:yyp32128.1=1440 st:gex0.1=1171 st:gex1024.1=193
+st:gex1536.1=2013 st:gex512.1=1934 st:ggm0.1=-46 st:ggm0.2=136 st:gi30.1=276 st:gi3128.1=182 st:gi364.1=277 st:gidn0.1=-42
+st:gij0.1=-46 st:giq0.1=949 st:giu0.1=-47 st:gk16_0.1=1150 st:glane0.1=1753 st:gp16_0.1=949 st:gpi0.1=-146 st:gri0.1=2426
+st:gtm0.1=1052 st:gtm0.2=1499 st:sae0.1=96 st:sae0.2=347 st:sgmf0.1=1826 st:si1280.1=316 st:sidd0.1=431 st:sidk0.1=430
+st:slutf0.1=88 st:slutk0.1=146 st:slutk0.2=937 st:sn1280.1=292 st:snm0.1=225 st:snm256.1=1804 st:snp_128.1=32 st:srst0.1=243
+st:srst0.2=1433 st:ss5k0.1=432 st:szb0.1=1839 st:szd0.1=836 st:vaa0.1=179 st:vbl0.1=2026 st:vcj0.1=137 st:vcj0.2=413 st:vfl0.1=133
+st:vfl17.1=298 st:vi40.1=414 st:viq1.1=2020 st:viu0.1=887 st:vk16_128.1=601 st:vl150.1=182 st:vlf0.1=281 st:vlf1.1=1145 st:vli0.1=71
+st:vlutf2.1=420 st:vlutf3.1=602 st:vlutk2.1=611 st:vlutk3.1=718 st:vlutq0.1=184 st:vlutq0.2=190 st:vlutq2.1=629 st:vlutq3.1=719
+st:vneg0.1=-12 st:vnil0.1=8 st:vnm0.1=2032 st:vnr0.1=1671 st:vones0.1=1 st:vp16_128.1=263 st:vqu0.1=914 st:vrp0.1=2464
+st:vs150.1=313 st:vsc0.1=183 st:vsc1.1=185 st:vtm0.1=192 st:vtm31.1=1577 st:vxt_0.1=250 st:vxt_0.2=357 st:vz10.1=264 st:vz115.1=207
+st:ynk0.1=385 st:ynk128.1=350 st:ynp_0.1=383 st:ywt0128.1=422 st:yxt_32.1=39 te:gxt_1056.1=-164 te:gxt_1568.1=734 te:gxt_32.1=1272
+te:gxt_544.1=1090 te:pm0500.1=2297 te:sjk0.1=2236 te:srst0.1=3296 te:vaa0.1=2324 te:vab0.1=2328 te:vxt_0.1=1618 te:vxt_0.2=1635
+te:vxt_0.3=1802 te:vxt_0.4=1839 te:vxt_0.5=2058 te:vxt_0.6=2374 te:vxt_0.7=2562 te:vxt_0.8=2137 te:yxt_32.1=2097 w0:gnm30.1=1604
+w0:scy1.1=1606 w0:vcy0.1=1801 w0:vdk0.1=1632 w0:veq0.1=1878 w0:vmw0.1=1927 w0:vvv0.1=1977 w0:vw160.1=1999 w0:vys0.1=1803
+w1:gnm286.1=1350 w1:scy257.1=1272 w1:vcy256.1=1525 w1:vdk128.1=1363 w1:veq256.1=1527 w1:vmw256.1=1550 w1:vvv128.1=1587
+w1:vw168.1=1584 w1:vys256.1=1581"""
+PLAN, INFO = [], {}
+SPEEDS = ((1.03, 0.95, 0.87, 1.0, 1.1, 1.2), (1.3, 0.8, 0.87, 1.3, 0.7, 1.2), (1.45, 1.1, 0.87, 1.0, 1.2, 0.9),
+          (1.2, 1.0, 1.45, 1.1, 0.8, 1.0), (1.05, 1.3, 1.35, 0.85, 1.3, 1.4), (1.4, 0.8, 1.25, 1.0, 1.0, 0.8),
+          (1.05, 1.4, 0.87, 0.8, 1.5, 1.4), (1.5, 0.8, 0.87, 1.25, 1.5, 0.8), (1.5, 0.9, 0.87, 0.9, 1.0, 1.0))
 TOP = 192 * 2.0 ** 17 + 2048
+HUGE = 2.0 ** 40
 ROUND = 1.5 * 2.0 ** 29
-MID = 12288.0
 HOP, CALL, PICK, ACT, GATHER, SCATTER, ISSUE, LOCAL, REMOTE, FAR, BYTES, MATMUL, COLUMN, ROWS, ROW = 176, 40, 88, 77, 1.45, 3.5, 242, 1300, 588, 2800, 152, 10, 0.45, 2000, 150
-INFO = {}
 
 
 def rank_program(g, core, T, topo):
@@ -100,11 +109,11 @@ def rank_program(g, core, T, topo):
     def half(name, h, w=128):
         return a(name, w * h, w * h + w)
 
-    def part(name, c0, c1, w=64):
-        return a(name, w * c0, w * c1)
+    def top(name):
+        return (T[name][0:16, :],) + a(name)[1:]
 
     def names16(u, h):
-        return half("pn16", 3 * h + (2 - u if h else u), 8)
+        return half("pn16", 3 * h + 2 - u, 8)
 
     def ind(win, off):
         return (win[0].indirect(off[0]), win, off)
@@ -119,7 +128,7 @@ def rank_program(g, core, T, topo):
 
     def task(q, kind, call, outs, ins, cost, after=0, more=False, moves=None, picks=0):
         if not more:
-            tasks.append(dict(q=q, kind=kind, calls=[], after=after, moves=moves, stage=now_[0], round=now_[1], lead=AHEAD.get(now_[0], 0), picks=picks))
+            tasks.append(dict(q=q, kind=kind, calls=[], after=after, moves=moves, stage=now_[0], round=now_[1], picks=picks))
         tasks[-1]["calls"].append((call, flat(outs), flat(ins), cost + picks))
 
     def vec(fn, out, ins, rate):
@@ -156,38 +165,25 @@ def rank_program(g, core, T, topo):
         else:
             vec(lambda: V.memset(out[0], val), out, [], narrow(out))
 
-    def act(out, in_, func, acc=None, **kw):
+    def act(out, in_, func=AF.Copy, acc=None, **kw):
         cost, picks = (80, GATHER * out[4]) if isinstance(in_[1], tuple) else (ACT + out[4], 0)
-        cols = [x for x in kw.values() if isinstance(x, tuple)]
-        kw = {k: x[0] if isinstance(x, tuple) else x for k, x in kw.items()}
         if acc is None:
-            task("s", "call", lambda: S.activation(out[0], in_[0], func, **kw), [out], [in_] + cols, cost, picks=picks)
+            task("s", "call", lambda: S.activation(out[0], in_[0], func, **kw), [out], [in_], cost, picks=picks)
         else:
             task("s", "call", lambda: S.activation(out[0], in_[0], func, accum_out=acc[0], **kw), [out, acc], [in_], cost)
 
-    def mm(out, l, r, start, stop, cut=False, holds=None):
+    def mm(out, l, r, start, stop, cut=False, holds=None, join=False):
         task("p", "call", lambda: P.matmul(out[0], l[0], r[0], start, stop), [holds or out], [l, r],
-             MATMUL + max(64, r[4]) * (4 if SCRATCH[l[1]][2] == F else 1) * COLUMN, more=not (start or cut))
+             MATMUL + max(64, r[4]) * (4 if SCRATCH[l[1]][2] == F else 1) * COLUMN, more=join or not (start or cut))
 
     def iota(out, pattern, base, cm):
         task("g", "call", lambda: g.iota(out[0], pattern, base, cm), [out], [], 160 + 2 * out[4])
 
-    def asel(out, in_, pattern, cop, base, cm):
-        task("g", "call", lambda: g.affine_select(out[0], in_[0], pattern, cop, 0.0, base, cm), [out], [in_], 200 + 2 * out[4])
+    def asel(out, in_, pattern, cop, base, cm, other=0.0):
+        task("g", "call", lambda: g.affine_select(out[0], in_[0], pattern, cop, other, base, cm), [out], [in_], 200 + 2 * out[4])
 
-    def turn(out, in_, key):
-        if key in POOL:
-            asel(out, in_, [[0, out[4]]], Op.is_equal, 0, 0)
-        elif key in ONS:
-            act(out, in_, AF.Copy)
-        else:
-            copy(out, in_)
-
-    def fetch(out, in_, key, scale=1.0):
-        if key in ONV:
-            ts(out, in_, scale, Op.mult)
-        else:
-            act(out, in_, AF.Copy, scale=scale)
+    def pool(out, in_):
+        asel(out, in_, [[0, out[4]]], Op.is_equal, 0, 0)
 
     def dmas(q, sem, pairs, outs, ins, size):
         task(q, "dma", (sem, pairs), outs, ins, ISSUE * len(pairs), max(LOCAL, LOCAL + size / BYTES - ISSUE * (len(pairs) - 1)),
@@ -201,15 +197,17 @@ def rank_program(g, core, T, topo):
     def send(to, names, sem, dst, src):
         task("g", "send", ("a" + sem, "l" + sem, dst, src), [to], [names], REMOTE, FAR, moves=(REMOTE, ROWS))
 
-    table = a("xt", 32, 2080)
+    def xt(t, lo=32, hi=2080):
+        return a("xt_%d" % (t % 2), lo, hi)
 
     dmas("s", "lp1", [(T.np_[:, 128:256], T.ph[:, 128:256])], [half("np_", 1)], [], 2 ** 16)
-    dmas("y", "lx", [(table[0], T.x0[:])], [table], [], 2 ** 19)
-    dmas("y", "lk0", [(T.nk[:], T.ka[:])], [a("nk")], [], 2 ** 17)
-    dmas("y", "lp0", [(T.np_[:, 0:128], T.ph[:, 0:128])], [half("np_", 0)], [], 2 ** 16)
-    for h in (1, 0):
-        turn(half("p16_0", h), half("np_", h), "p%d" % h)
-        turn(half("k16_0", h), half("nk", h), "k%d" % h)
+    dmas("y", "lx", [(xt(0)[0], T.x0[:])], [xt(0)], [], 2 ** 19)
+    dmas("y", "lk1", [(T.nk[:, 128:256], T.ka[:, 128:256])], [half("nk", 1)], [], 2 ** 16 + 128 * ROW)
+    dmas("y", "lp0", [(T.np_[:, 0:128], T.ph[:, 0:128])], [half("np_", 0)], [], 2 ** 16 + 128 * ROW)
+    dmas("y", "lk0", [(T.nk[:, 0:128], T.ka[:, 0:128])], [half("nk", 0)], [], 2 ** 16 + 128 * ROW)
+    for h, turn in ((1, copy), (0, pool)):
+        turn(half("p16_0", h), half("np_", h))
+        turn(half("k16_0", h), half("nk", h))
 
     fill(a("ones"), 1.0)
     fill(a("neg"), -1.0)
@@ -224,24 +222,10 @@ def rank_program(g, core, T, topo):
     iota(a("ri"), [[0, 2], [16, 4], [64, 18]], 64 - 2048, 0)
     for b in range(4):
         asel(a("ex", 512 * b, 512 * b + 512), a("neg"), [[1, 32], [0, 16]], Op.is_equal, 32 * b, -1)
-    fill(a("nil"), 0.0)
-    fill(a("z1"), 0.0)
-    fill(a("qu"), 0.25)
-    fill(a("fl"), -1040.0 * 4096)
-    fill(a("fl", 17, 288, 18), -2.0 ** 26)
-    fill(a("rst"), -4e9)
-    fill(a("rst", 0, 128, 16), TOP)
-    fill(a("big"), 2.0 ** 18)
-    fill(a("lutf"), 0.0)
-    fill(a("lutk"), -512.0)
-    fill(a("lutk", 0, 1), -768.0)
-    fill(a("lutq"), 0.0)
-    fill(a("lutq", 0, 1), -1.0)
-    fill(a("w16"), 0)
-    fill(a("nr", 392, 400), 1.0)
-    fill(a("xt", 0, 32), 0.0)
-    fill(a3("ae", 0, 16, 0, 16), 0.0)
-    fill(a3("ae", 0, 16, 272, 288), 0.0)
+    for x, val in ((a("nil"), 0.0), (a("z1"), 0.0), (a("qu"), 0.25), (a("fl"), -1040.0), (a("fl", 17, 288, 18), -2.0 ** 14), (a("rst"), -4e9),
+                   (a("rst", 0, 128, 16), TOP), (a("aa"), 0), (a("lutf"), 0.0), (a("lutk"), -512.0), (a("lutk", 0, 1), -768.0), (a("lutq"), 0.0),
+                   (a("lutq", 0, 1), -1.0), (xt(0, 0, 32), 0.0), (xt(1, 0, 32), 0.0), (a3("ae", 0, 16, 0, 16), 0.0), (a3("ae", 0, 16, 272, 288), 0.0)):
+        fill(x, val)
     dmas("y", "kz", [(T["kd%d" % h][:, 0, :], T.nil[0:8, :]) for h in range(2)] + [(T["wt%d" % h][0:128:16, 128:1152], T.nil[:]) for h in range(2)],
          [a("wt0", 128, 1152), a("wt1", 128, 1152), scratch(0), scratch(1)], [a("nil")], 2 ** 16 + 256 * ROW)
     ts(a("li"), a("pi"), 15, Op.bitwise_and)
@@ -249,221 +233,156 @@ def rank_program(g, core, T, topo):
     ts(a("l15", 0, 1), a("lf", 0, 1), 15.0, Op.is_equal)
     copy(a("z1", 15, 143, 16), a("gm", 0, 128, 16))
     ts(a("s15"), a("gm"), a("l15", 0, 1), Op.mult)
-    for z, x, w in (("gmf", "gm", 1.0), ("s5k", "s15", 4096.0), ("idk", "idn", 4096.0), ("zd", "z1", 2.0 ** 17), ("zb", "z1", 4096.0),
-                    ("idm", "idn", -1.0), ("i128", "idn", 128.0)):
-        if z in SPARE:
-            act(a(z), a(x), AF.Copy, scale=w)
-        else:
-            ts(a(z), a(x), w, Op.mult)
+    for z, x, w in (("gmf", "gm", 2.0 ** 18), ("s5k", "s15", 4096.0), ("idk", "idn", 4096.0), ("zd", "z1", 2.0 ** 17), ("zb", "z1", 4096.0),
+                    ("n128", "idn", -128.0), ("i128", "idn", 128.0), ("idd", "idn", 2.0 ** 17)):
+        act(a(z), a(x), scale=w)
     vec(lambda: V.memset(T.cj[0:64, :], -13.0 * 2 ** 17), a("cj"), [], 0.5)
     vec(lambda: V.tensor_scalar(T.cj[64:128, :], T.ij[64:128, :], 128.0, 96.0, Op.mult, Op.add), a("cj"), [a("ij")], 1)
     ts(a("i4"), a("i3"), 15, Op.bitwise_and)
-    for wide in sorted(set(WIDE)):
-        iota(a("it", 0, 8 * wide), [[0, 8], [1, wide]], 16 - wide, 0)
-        ts(a3("tm", wide - 16, wide - 16 + wide // 4), a("it", 0, 8 * wide), a("lf", 0, 1), Op.is_ge, 16384.0, Op.mult)
-        if wide > 16:
-            fill((T.tm[:, 16:24:2, 0:16], "tm", 512, 768, 64), 16384.0)
-            ts(a("lf", 1, 2), a("lf", 0, 1), 16.0, Op.add)
-            ts(a("l15", 1, 2), a("lf", 0, 1), -1.0, Op.mult, 16.0, Op.add)
-    for h in range(2):
-        wide = WIDE[h]
-        x0, x1, n = 256 * h, 256 * h + 8 * wide, wide // 16
-        fill(a("nm", x0, x1), 0.0)
-        if wide > 16:
-            ts(a("nm", x0, x1, 64), a("big", 0, 4), 0.0, Op.mult, a("lf", 1, 2), Op.add)
-        iota(a("iq", 16 * h, 16 * h + 8 * n), [[1, 8], [0, n]], 8 * h, 0)
-        iota(a("iu", 8 * h, 8 * h + 8), [[-1, 8]], 8 - 16 * h, 0)
-        ts(a("iu", 8 * h, 8 * h + 8), a("iu", 8 * h, 8 * h + 8), a("l15", 0, 1), Op.mult)
-        tt(a("iq", 16 * h + n - 1, 16 * h + 8 * n, n), a("iq", 16 * h + n - 1, 16 * h + 8 * n, n), a("iu", 8 * h, 8 * h + 8), Op.add)
-        copy(a("bl", 16 * h, 16 * h + 8 * n), a("iq", 16 * h, 16 * h + 8 * n))
     for sb in range(2):
         ts(a("lutf", 2 + sb, 256, 4), a("i4", 64 * sb, 64 * sb + 64), 0.0, Op.is_equal, 4096.0, Op.mult)
         ts(a("lutk", 2 + sb, 256, 4), a("i4", 128, 192), 0.0, Op.is_equal, 4096.0, Op.mult)
         ts(a("lutq", 2 + sb, 256, 4), a("i4", 128, 192), 0.0, Op.is_equal)
     ts(a("rp"), a("ri"), a("lf", 0, 1), Op.add)
+    fill(a("sc"), 0.0)
+    fill(a("sc", 1, 256, 2), -128.0)
+    fill(a("tm"), 32.0)
+    asel(a("tm"), a("tm"), [[0, 8], [-1, 16], [-32, 2]], Op.is_ge, 31, 1, 16384.0)
+    asel(a("tm", 0, 256, 2), a("tm", 0, 256, 2), [[0, 4], [1, 2], [0, 16]], Op.is_gt, 0, 0, 16384.0)
+    fill(a("tm", 31, 256, 32), HUGE)
+    asel(a("lane"), a("ones"), [[0, 8], [1, 16]], Op.is_equal, 0, -1)
+    fill(a("nr", 0, 816, 408), HUGE)
+    iota(a("iq"), [[1, 8], [0, 2]], 8, 0)
+    iota(a("iu"), [[-1, 8]], -8, 0)
+    ts(a("iu"), a("iu"), a("l15", 0, 1), Op.mult)
+    tt(a("iq", 1, 16, 2), a("iq", 1, 16, 2), a("iu"), Op.add)
+    copy(a("bl"), a("iq"))
+    ts(a("lf", 1, 2), a("lf", 0, 1), 16.0, Op.add)
+    for h in range(2):
+        fill(half("nm", h, 256), 0.0)
+    ts(a("nm", 0, 512, 64), a("nil", 0, 8), 0.0, Op.mult, a("lf", 1, 2), Op.add)
 
-    def lanes(out, z, src, c, first, end, lo=0, w=16, cut=False, n=1):
+    def lanes(out, z, src, c, first, end, lo=0, w=16, cut=False):
         for i in range(16):
-            mm(out, a(z, 15 - i, 143 - i), a3(src, 4 * c, 4 * (c + n), lo + 16 * i, lo + 16 * i + w), first and i == 0, end and i == 15, cut and i == 0)
+            mm(out, a(z, 15 - i, 143 - i), a3(src, 4 * c, 4 * c + 4, lo + 16 * i, lo + 16 * i + w), first and i == 0, end and i == 15, cut and i == 0)
 
     def shifted(t, h):
-        early, wt = len(tasks), "wt%d" % h
-        turn(half("kh", h), half("k16_%d" % t, h), "kh")
+        wt, at = "wt%d" % h, 256 + 128 * h
+        pool(half("kh", h), half("k16_%d" % t, h))
         for u, (x, y) in enumerate((("s15", "s5k"), ("idn", "idk"))):
-            o = half("e3", 2 * h + u, 64) if EB == 3 else half(PSUM[6 + h], 5 + u, 64)
+            o = a("e3", at + 64 * u, at + 64 * u + 64)
             mm(o, a(x), half("kh", 2 * h, 64), True, False)
             mm(o, a(y), half("kh", 2 * h + 1, 64), False, True)
-        fetch(a(wt, 0, 128), half("e3", h) if EB == 3 else a(PSUM[6 + h], 320, 448), wt)
+        act(a(wt, 0, 128), a("e3", at, at + 128))
         w, k = T[wt], T["kd%d" % h]
         dmas("y", "kd%d" % h, [(k[:, 1:17, :], w[:, 64:128]), (k[:, 17:33, :], w[:, 0:64])], [scratch(h)], [a(wt, 0, 128)], 2 ** 16 + 256 * ROW)
         dmas("y", "wd%d" % h, [(w[j:128:16, 128:1152], k[:, 1 + j:17 + j, :]) for j in range(1, 16)] + [(w[:, 1152:1216], k[:, 0:16, :])],
              [a(wt, 128, 1216)], [scratch(h)], 2 ** 19 + 240 * ROW)
-        for x in tasks[early:]:
-            x["lead"] = LEAD
 
     def half_round(t, h):
-        last = t == RO - 1
+        last, table = t == RO - 1, xt(t)
         c0, c1 = 2 * h, 2 * h + 2
         k16, p16, cb, m = "k16_%d" % t, "p16_%d" % t, PSUM[4 + h], PSUM[6 + h]
-        wide = WIDE[h]
-        same, packed, lists = (a(m, 152, 152 + 8 * wide), 24, a(m, 0, 24)) if h else (a(m, 256 - 8 * wide, 256), 256, a(m, 384, 408))
-        signed = a(m, same[2], same[2] + 128)
-        sk, sa, sf = [half("sel", 3 * h + (2 - u if h else u)) for u in range(3)]
-        l8, code, names = half("l8", h, 8), a(cb, 0, 128), half("nr", 48 + 2 * h, 8)
-        at, rows, news = (400, 536, 408) if h else (256 - 8 * wide, 256 - 8 * wide, 256)
-
-        mine, other = (p16, k16) if FIRST[h] == "p" else (k16, p16)
+        sf, sa, sk = [half("sel", 3 * h + u) for u in range(3)]
+        l8, code, lists, at = half("l8", h, 8), a(cb, 0, 128), a(m, 0, 24), 408 * h + 8
 
         now_[0] = "codes%d" % h
         mm(code, a("ones"), a("cj"), True, False, holds=a(cb))
         for c in range(c0, c1):
-            o = half(cb, c - c0, 64)
+            mine, other = (p16, k16) if FIRST[c] == "p" else (k16, p16)
             for lo, hi in PIECES.get(c, ((0, 4),)):
-                act(a("yg", 1024 * c + 256 * lo, 1024 * c + 256 * hi), ind(table, a(mine, 64 * c + 16 * lo, 64 * c + 16 * hi)), AF.Copy)
-                if c in BEHIND:
-                    tasks[-1]["calls"][0][2].append(a3("a3", 4 * BEHIND[c], 4 * BEHIND[c] + 4))
+                act(a("yg", 1024 * c + 256 * lo, 1024 * c + 256 * hi), ind(table, a(mine, 64 * c + 16 * lo, 64 * c + 16 * hi)))
             for q in range(4 * c, 4 * c + 4):
                 tt(row("d3", q), ind(table, half(other, q, 16)), half("yg", q, 256), Op.subtract)
             for lo, hi in PARTS.get(c, ((0, 4),)):
-                if c in RELU:
+                if c == RELU:
                     ts(a3("a3", 4 * c + lo, 4 * c + hi), a3("d3", 4 * c + lo, 4 * c + hi), 0.0, Op.min, -2.0, Op.mult)
                 else:
                     act(a3("a3", 4 * c + lo, 4 * c + hi), a3("d3", 4 * c + lo, 4 * c + hi), AF.Abs)
-            if h not in WHOLE:
-                lanes(a(m, same[2] + 64 * (c - c0), same[2] + 64 * (c - c0 + 1)), "z1", "d3", c, True, True)
-            if c in RELU:
-                lanes(o, "zd", "d3", c, False, False, cut=True)
-            lanes(o, "zd", "a3", c, False, False, cut=True)
-        if h in WHOLE:
-            lanes(signed, "z1", "d3", c0, True, True, n=2)
-        act(half("sn", h), signed, AF.Sign, scale=-1.0 if FIRST[h] == "p" else 1.0, bias=0.5)
-        mm(code, a("i128"), half("sn", h), False, True, cut=True)
+            lanes(a(m, 152 + 64 * (c - c0), 216 + 64 * (c - c0)), "z1", "d3", c, True, True)
+            lanes(half(cb, c - c0, 64), "zd", "a3", c, False, False, cut=True)
+        act(half("sn", h), a(m, 152, 280), AF.Sign)
+        if RELU // 2 == h:
+            act(half("sg", RELU, 64), a(m, 152 + 64 * (RELU - c0), 216 + 64 * (RELU - c0)))
+            mm(half(cb, RELU - c0, 64), a("idd"), half("sg", RELU, 64), False, False, cut=True)
+        for c in range(c0, c1):
+            mm(half(cb, c - c0, 64), a("i128" if FIRST[c] == "k" else "n128"), half("sn", c, 64), False, c == c1 - 1, cut=c == c0)
         shifted(t, h)
 
         now_[0] = "least%d" % h
-        turn(half("ph_", h), half(p16, h), "ph")
-        least = a("mi", 128 * h + 15, 128 * h + 128, 16)
+        pool(half("ph_", h), half(p16, h))
         scan(half("mi", h), a("rst"), code, 0.0, Op.max, Op.min)
-        if SCRATCH["mi"][2] == F:
-            copy(half("cl", h, 8), least)
-            least = half("cl", h, 8)
-        ts(half("v8", h, 8), least, (255 << 11) - 2 ** 31, Op.bitwise_and, 11, Op.arith_shift_right)
-        turn(l8, half("v8", h, 8), "l8%d" % h)
+        ts(half("v8", h, 8), a("mi", 128 * h + 15, 128 * h + 128, 16), (255 << 11) - 2 ** 31, Op.bitwise_and, 11, Op.arith_shift_right)
+        copy(l8, half("v8", h, 8))
         tt(sf, ind(a("lutf"), l8), half("ph_", h), Op.min)
         tt(sk, ind(a("lutk"), l8), half("ph_", h), Op.min)
         tt(sa, ind(a("lutq"), l8), half("kh", h), Op.mult)
         for u, z in enumerate(("z1", "zb")):
-            mm(a(m, packed + 64 * u, packed + 64 * u + 64), a(z, 15, 143), a("sel", sf[2] + 64 * u, sf[2] + 64 * u + 64), True, True)
-        mm(same, a("idn"), a3("tm", wide - 16, wide - 16 + wide // 4), True, False)
-        if wide == 16:
-            mm(same, a("gm"), sk, False, True)
-        for q in range(8 * (wide > 16)):
-            mm(a(m, same[2] + 32 * q + 16 - 16 * (q % 2), same[2] + 32 * q + 32), a("gm"), a("sel", sk[2] + 32 * (q // 2), sk[2] + 16 * q + 16), False, q == 7)
-        mm(a(m, same[2] + wide - 1, same[3], wide), a("idn"), a("ones", 0, 8), True, True)
+            mm(a(m, 24 + 64 * u, 88 + 64 * u), a(z, 15, 143), a("sel", sf[2] + 64 * u, sf[2] + 64 * u + 64), True, True, join=u > 0)
         for i in range(16):
-            mm(lists, a("z1", 15 - i, 143 - i), a("sel", 384 * h + i, 384 * h + 384, 16), i == 0, i == 15)
-        if "pn" in ONS:
-            act(half("pn16", h, 24), lists, AF.Copy)
-        else:
-            copy(half("pn16", h, 24), lists)
-        fetch(a("nr", at, at + 136 + 8 * wide), a(m, 16, 152 + 8 * wide) if h else a(m, at, 392), "nr%d" % h)
+            mm(lists, a("z1", 15 - i, 143 - i), a("sel", 384 * h + i, 384 * h + 384, 16), i == 0, False)
+        mm(a(m, 16, 24), a("ones"), a("qu", 0, 8), False, True)
+        copy(half("pn16", h, 24), lists)
+        mm(a(m, 152, 408), top("lane"), top("tm"), True, False)
+        mm(a(m, 184, 408, 2), a("gm"), a("sel", sk[2], sk[3] - 16), False, False)
+        mm(a(m, 153, 408, 2), a("gm"), sk, False, True)
+        act(a("nr", at, at + 392), a(m, 16, 408))
 
         now_[0] = "near%d" % h
-        act(half("xn", h), ind(table, names16(2, h)), AF.Copy)
+        act(half("xn", h), ind(table, names16(2, h)))
         mm(code, half("xn", h), a("idn"), True, True)
-        fetch(half("xr", h), code, "xr%d" % h)
-        fetch(a("fl", 144 * h, 144 * h + 144, 18), names, "fl%d" % h, 8192.0)
-        for c in range(c1 - 1, c0 - 1, -1):
+        act(half("xr", h), code)
+        pool(a("fl", 144 * h, 144 * h + 144, 18), a("nr", at, at + 8))
+        for c in range(c0, c1) if h else range(c1 - 1, c0 - 1, -1):
             for b in (2 * c, 2 * c + 1):
-                e = a("e%d" % (turns[0] % EB))
+                e = a("e%d" % (turns[0] % 3))
                 turns[0] += 1
                 mm(e, a("idn"), half("yg", b, 512), True, False)
-                if FIRST[h] == "p":
+                if FIRST[c] == "p":
                     mm(e, a("idn"), a3("d3", 2 * b, 2 * b + 2), False, False)
                 mm(e, half("xr", h), half("ex", b % 4, 512), False, True, cut=True)
                 act(a3("ae", 2 * b, 2 * b + 2, 16, 272), e, AF.Abs)
-            if h not in SUMS:
-                o = a(cb, 256 + 72 * (c - c0), 328 + 72 * (c - c0))
-                mm(o, a("idn"), half("fl", c, 72), True, False)
-                lanes(o, "zb", "ae", c, False, True, 15, 18)
-        if h in SUMS:
-            mm(a(cb, 256, 400), a("idn"), half("fl", h, 144), True, False)
-            lanes(a(cb, 256, 400), "zb", "ae", c0, False, True, 15, 18, n=2)
-        for lo, hi in NEARS:
-            if lo // 2 != h:
-                continue
-            scan(back("ms", 72 * lo, 72 * hi), back(cb, 256 + 72 * (lo - c0), 256 + 72 * (hi - c0)), back("rp", 0, 72 * (hi - lo)), -4096.0, Op.min, Op.max)
-            if "o16" in ONS:
-                act(part("o16", lo, hi, 4), a("ms", 72 * lo, 72 * hi, 18), AF.Copy, bias=2048.0)
+            o = a(cb, 256 + 72 * (c - c0), 328 + 72 * (c - c0))
+            mm(o, a("idk"), half("fl", c, 72), True, False)
+            lanes(o, "zb", "ae", c, False, True, 15, 18)
+        scan(back("ms", 144 * h, 144 * h + 144), back(cb, 256, 400), back("rp", 0, 144), -4096.0, Op.min, Op.max)
+        ts(half("o16", h, 8), a("ms", 144 * h, 144 * h + 144, 18), 1.0, Op.mult, 2048.0, Op.add)
+        tt(half("fr", h), ind(a("wt%d" % h), half("o16", h, 8)), a("nr", at + 8, at + 136), Op.add)
+        for c in range(c1 - 1, c0 - 1, -1):
+            to = half("yk32" if last else "ks_%d" % t, c, 64)
+            if c % 2 and not last:
+                ts(to, half("fr", c, 64), 2.0 ** -12, Op.mult, 0.0, Op.add)
             else:
-                ts(part("o16", lo, hi, 4), a("ms", 72 * lo, 72 * hi, 18), 2048.0, Op.add)
-            tt(part("fr", lo, hi), ind(a("wt%d" % h), part("o16", lo, hi, 4)), a("nr", news + 64 * (lo - c0), news + 64 * (hi - c0)), Op.add)
-            for c in range(hi - 1, lo - 1, -1):
-                to = half("yk32" if last else "ks_%d" % t, c, 64)
-                if c % 2 == 0:
-                    ts(half("fu", c, 64), half("fr", c, 64), 4095, Op.bitwise_and)
-                    turn(to, half("fu", c, 64), "ks")
-                elif last:
-                    ts(half("fu", c, 64), half("fr", c, 64), 12, Op.logical_shift_right)
-                    turn(to, half("fu", c, 64), "ks")
-                elif "hi" in ONS:
-                    act(to, half("fr", c, 64), AF.Copy, scale=2.0 ** -12)
-                else:
-                    ts(to, half("fr", c, 64), 2.0 ** -12, Op.mult)
-            if last:
-                dmas("y", "ok%d" % lo, [(T.yk[:, 64 * lo:64 * hi], T.yk32[:, 64 * lo:64 * hi])], [], [part("yk32", lo, hi)], 2 ** 15 * (hi - lo))
-            else:
-                send(part("k16_%d" % (t + 1), lo, hi), part("ks_%d" % t, lo, hi), "k%d_%d" % (t + 1, lo), nxt, prv)
+                ts(half("fu", c, 64), half("fr", c, 64), *((12, Op.logical_shift_right) if c % 2 else (4095, Op.bitwise_and)))
+                (pool if last and h else copy)(to, half("fu", c, 64))
+        if last:
+            dmas("y", "ok%d" % h, [(T.yk[:, 128 * h:128 * h + 128], half("yk32", h)[0])], [], [half("yk32", h)], 2 ** 16)
+        else:
+            send(half("k16_%d" % (t + 1), h), half("ks_%d" % t, h), "k%d_%d" % (h, t + 1), nxt, prv)
 
         now_[0] = "phages%d" % h
-        if "pa" in ONS:
-            act(half("pa", h), sa, AF.Relu, scale=-1.0)
-        else:
-            ts(half("pa", h), sa, -1.0, Op.mult, 0.0, Op.max)
-        for lo, hi in PHAGES:
-            if lo == c0:
-                factor = a("e3", 256 + 64 * lo, 256 + 64 * hi) if EB == 3 else a(m, 320, 448)
-                mm(factor, a("ones"), a("qu", 0, 64 * (hi - lo)), True, False)
-                mm(factor, a("idn"), part("pa", lo, hi), False, True)
-                tt(part("pt", lo, hi), part("ph_", lo, hi), factor, Op.mult)
-                ts(part("pn", lo, hi), part("pt", lo, hi), 5, Op.logical_shift_right, 2047, Op.bitwise_and)
-                if last:
-                    turn(part("yp32", lo, hi), part("pn", lo, hi), "yp")
-                    dmas("y", "op%d" % lo, [(T.yp[:, 64 * lo:64 * hi], T.yp32[:, 64 * lo:64 * hi])], [], [part("yp32", lo, hi)], 2 ** 15 * (hi - lo))
-                else:
-                    turn(part("ps_%d" % t, lo, hi), part("pn", lo, hi), "ps")
-                    send(part("p16_%d" % (t + 1), lo, hi), part("ps_%d" % t, lo, hi), "p%d_%d" % (t + 1, lo), prv, nxt)
+        ts(half("pa", h), sa, -1.0, Op.mult, 0.0, Op.max)
+        mm(a(cb, 128, 256), a("ones"), a("qu"), True, False)
+        mm(a(cb, 128, 256), a("idn"), half("pa", h), False, True)
+        tt(half("pt", h), half("ph_", h), a(cb, 128, 256), Op.mult)
+        ts(half("pn", h), half("pt", h), 5, Op.logical_shift_right, 2047, Op.bitwise_and)
+        pool(half("yp32" if last else "ps_%d" % t, h), half("pn", h))
+        if last:
+            dmas("y", "op%d" % h, [(T.yp[:, 128 * h:128 * h + 128], half("yp32", h)[0])], [], [half("yp32", h)], 2 ** 16)
+        elif h == 0:
+            send(a("p16_%d" % (t + 1)), a("ps_%d" % t), "p_%d" % (t + 1), prv, nxt)
 
         now_[0] = "writes%d" % h
-        for lo, hi in WRITES:
-            if lo == c0:
-                yk, c1_, wv = part("yk_", lo, hi), part("c1", lo, hi), half("ys", 3 * h)
-                if h in FLIP:
-                    dk, turned = a(m, 304, 432), a(cb, 128, 256)
-                    act(half("ys", h, 256), ind(table, half("pn16", 2 * h, 16)), AF.Copy)
-                    act(half("sg", h), wv, AF.Sign, scale=-1.0, bias=127.5)
-                    mm(dk, a("idn"), half("ys", 1 + h), True, False)
-                    mm(dk, a("idm"), wv, False, True)
-                    mm(turned, a("i128"), half("sg", h), True, True)
-                    ts(c1_, dk, ROUND, Op.add, ROUND, Op.is_equal)
-                    tt(half("vv", h), c1_, turned, Op.mult)
-                else:
-                    act(yk, ind(table, names16(0, h)), AF.Copy, bias=-MID)
-                    tt(part("dk", lo, hi), ind(table, names16(1, h)), yk, Op.subtract)
-                    ts(c1_, part("dk", lo, hi), MID, Op.is_equal, -128.0, Op.mult)
-                    tt(wv, ind(table, names16(0, h)), c1_, Op.add)
-                    ts(part("vv", lo, hi), wv, 0.0, Op.is_lt, 256.0, Op.mult)
-        for lo, hi in EQUAL:
-            if lo == c0:
-                x0, x1 = 256 * h, 256 * h + 8 * wide
-                if wide == 16:
-                    act(a("nm", x0 + 14, x1, 16), names, AF.Relu, bias=32.0)
-                else:
-                    act(a("nm", x0 + 62, x1, 64), a("nr", names[2] + 1, names[3], 2), AF.Relu, bias=32.0)
-                    act(a("nm", x0 + 30, x1, 64), a("nr", names[2], names[3], 2), AF.Relu, bias=a("l15", 1, 2))
-                tt(a("eq", x0, x1), ind(a("nr", 384 + 8 * h, 400 + 8 * h), a("bl", 16 * h, 16 * h + wide // 2)), a("nr", rows, rows + 8 * wide), Op.not_equal)
-                scan(back("mw", x0, x1), back("nm", x0, x1), back("eq", x0, x1), 0.0, Op.add, Op.mult)
-                ts(a("w16", 16 * h, 16 * h + 256 // wide, 32 // wide), a("mw", x0, x1, wide), a("lf", 0, 1), Op.max)
+        x0, x1 = 256 * h, 256 * h + 256
+        act(a("cy", x0 + 1, x1, 2), ind(xt(t, 0), names16(0, h)))
+        tt(half("dk", h), ind(table, names16(1, h)), a("cy", x0 + 1, x1, 2), Op.subtract)
+        ts(a("cy", x0, x1, 2), half("dk", h), ROUND, Op.add, ROUND, Op.is_equal)
+        scan(a("ys", x0, x1), a("sc"), a("cy", x0, x1), 0.0, Op.mult, Op.add)
+        ts(half("vv", h), a("ys", x0 + 1, x1, 2), 0.0, Op.is_lt, 256.0, Op.mult)
+        pool(a("nm", x0 + 30, x1, 32), names16(0, h))
+        tt(a("eq", x0, x1), ind(a("nr", at - 8, at + 8), a("bl")), a("nr", at + 136, at + 392), Op.not_equal)
+        scan(back("mw", x0, x1), back("nm", x0, x1), back("eq", x0, x1), 0.0, Op.max, Op.mult)
+        ts(half("w16", h, 8), a("mw", x0, x1, 32), a("lf", 0, 1), Op.max)
 
     turns = [0]
     for t in range(RO):
@@ -471,20 +390,19 @@ def rank_program(g, core, T, topo):
         for h in (1, 0):
             half_round(t, h)
         now_[0] = "table"
-        for h in (1, 0):
-            wide = WIDE[h]
-            for b in range(128 // wide - 1, -1, -1):
-                tt(ind(a("xt"), a("w16", 16 * h + 2 * b, 16 * h + 2 * b + wide // 16)), a("ys", 384 * h + wide * b, 384 * h + wide * b + wide),
-                   a("vv", 128 * h + wide * b, 128 * h + wide * b + wide), Op.add)
+        for u in range(COPY):
+            lo, hi = 32 + 2048 // COPY * u, 32 + 2048 // COPY * (u + 1)
+            pool(xt(t + 1, lo, hi), xt(t, lo, hi))
+        for b in range(7, -1, -1):
+            tt(ind(xt(t + 1, 0), half("w16", b, 2)), a("ys", 64 * b + 1, 64 * b + 64, 2), half("vv", b, 32), Op.add)
         if t == RO - 1:
-            dmas("y", "oy", [(T.yx[:], table[0])], [], [table], 2 ** 19)
+            dmas("y", "oy", [(T.yx[:], xt(RO)[0])], [], [xt(RO)], 2 ** 19)
         else:
-            act(a("jk"), a("nr", 384, 408), AF.Sign, acc=a("ac", t, t + 1), scale=-1.0, bias=-10240.0)
-            for u in range(t + 1):
-                mm(a("m0", 500, 501), a("gmf"), a("ac", u, u + 1), u == 0, u == t)
-            ts(a("aa"), a("big"), a("m0", 500, 501), Op.mult, 384 * 2.0 ** 18 * (t + 1), Op.add)
+            act(a("jk"), a("fl", 0, 288, 18), AF.Sign, acc=a("ac", t, t + 1), scale=-1.0, bias=-10240.0)
+            mm(a("m0", 500, 501), a("gmf"), a("ac", t, t + 1), True, True)
+            ts(a("aa"), a("aa"), a("m0", 500, 501), Op.add, 256 * 2.0 ** 18, Op.add)
             ts(a("ab"), a("aa"), 15 << 19, Op.bitwise_and)
-            ts(a("rst", 0, 128, 16), a("ab"), TOP, Op.add)
+            act(a("rst", 0, 128, 16), a("ab"), bias=TOP)
 
     def clash(hist, q, outs, ins, banks):
         for kind, lst in (("w", outs), ("r", ins)):
@@ -492,7 +410,7 @@ def rank_program(g, core, T, topo):
                 for k2, lo, hi, q2, who in hist.get(x[1], ()):
                     same = q2 == q and q != "dma"
                     if banks and x[1] in PSUM and not same or not (k2 == kind == "r" or hi <= x[2] or lo >= x[3]):
-                        yield who, same and (q == "p" or k2 + kind in FREE)
+                        yield who, same and q == "p"
 
     def note(hist, q, outs, ins, who):
         for kind, lst in (("w", outs), ("r", ins)):
@@ -503,14 +421,14 @@ def rank_program(g, core, T, topo):
                 e.append((kind, x[2], x[3], q, who))
 
     def planned():
-        hist = {}
+        hist, N = {}, len(tasks)
         for n, x in enumerate(tasks):
             q = x["q"] if x["kind"] == "call" else "dma"
             x["needs"], x["gaps"], x["banks"], at = {}, {}, set(), 0
             for call, outs, ins, cost in x["calls"]:
                 for who, free in clash(hist, q, outs, ins, False):
                     if who != n and (0 if free else HOP) - at > x["needs"].get(who, -1e9):
-                        x["needs"][who], x["gaps"][who] = (0 if free else HOP) - at, (0 if free else HOP, at)
+                        x["needs"][who], x["gaps"][who] = (0 if free else HOP) - at, (0 if free else 1, at)
                 note(hist, q, outs, ins, n)
                 x["banks"].update(y[1] for y in outs + ins if y[1] in PSUM)
                 at += cost
@@ -521,142 +439,172 @@ def rank_program(g, core, T, topo):
             for w in x:
                 nexts[w].append(n)
 
-        def in_order(key):
-            key = list(key)
-            for n in range(len(key) - 1, -1, -1):
-                for w in before[n]:
-                    if key[w] > key[n]:
-                        key[w] = key[n]
-            return [n for k, n in sorted(zip(key, range(len(key))))]
-
-        def place(key):
-            end, busy = {}, {}
-            for n in in_order(key):
-                x = tasks[n]
-                at = max([0] + [end[w] + d for w, d in before[n].items()])
-                held = busy.get(x["q"], []) + [(lo - HOP, hi + HOP) for b in x["banks"] for lo, hi, q in busy.get(b, []) if q != x["q"]]
-                if x["moves"]:
-                    held += [(lo - sum(x["moves"]) + x["cost"], hi - x["moves"][0]) for lo, hi in busy.get("engines", [])]
-                for lo, hi in sorted(held):
-                    if hi > at:
-                        if lo >= at + x["cost"]:
-                            break
-                        at = hi
-                end[n] = at + x["cost"]
-                busy.setdefault(x["q"], []).append((at, end[n]))
-                if x["moves"]:
-                    busy.setdefault("engines", []).append((at + x["moves"][0], at + sum(x["moves"])))
-                for b in x["banks"]:
-                    busy.setdefault(b, []).append((at, end[n], x["q"]))
-            return end
-
-        way = [0] * len(tasks)
-        for n in range(len(tasks) - 1, -1, -1):
-            way[n] = tasks[n]["cost"] + max([tasks[n]["after"]] + [way[w] + before[w][n] for w in nexts[n]])
-        ends = place([-way[n] - x["lead"] for n, x in enumerate(tasks)])
-        start = [ends[n] - x["cost"] for n, x in enumerate(tasks)]
-
         def direct(n, w):
             return not any(w in before[u] and before[u][w] >= 0 and d >= 0 and before[u][w] + tasks[u]["cost"] + d >= before[n][w] for u, d in before[n].items())
 
-        briefs = [[(x["q"], (x["cost"] + (pick - 1) * x["picks"]) * (far if x["moves"] else slow * {"p": pe, "s": sc}.get(x["q"], 1)),
-                    [(w, tasks[w]["after"] * far + d * hop - e * slow * pe) for w, (d, e) in x["gaps"].items() if direct(n, w)], tuple(sorted(x["banks"])),
-                    x["moves"] and (x["moves"][0] * far, sum(x["moves"]) * far)) for n, x in enumerate(tasks)] for slow, far, pe, pick, sc, hop in SPEEDS]
-        finals = [n for n in range(len(tasks)) if not nexts[n]]
+        needs = [[w for w in before[n] if direct(n, w)] for n in range(N)]
+        upon = [(n, needs[n]) for n in range(N - 1, -1, -1) if needs[n]]
 
-        def length(order, mix, old=None, same=0):
-            brief, far, hop = briefs[mix], SPEEDS[mix][1], HOP * SPEEDS[mix][5]
-            if old:
-                marks = old[3][:same // MARK + 1]
-                end, why, free, bank, engines = old[2][:], old[1][:], dict(marks[-1][0]), dict(marks[-1][1]), marks[-1][2]
-                marks = marks[:-1]
+        def in_order(key):
+            for n, ws in upon:
+                k = key[n]
+                for w in ws:
+                    if key[w] > k:
+                        key[w] = k
+            return [n for k, n in sorted(zip(key, range(N)))]
+
+        queues = list(Q)
+        scale = [6 / len(SPEEDS) / (s[0] + s[1]) for s in SPEEDS]
+        costs = [[(x["cost"] + ((sc if x["stage"] == "table" else pick) - 1) * x["picks"]) * (far if x["moves"] else slow * (pe if x["q"] == "p" else 1)) * z
+                  for x in tasks] for (slow, far, pe, pick, sc, hop), z in zip(SPEEDS, scale)]
+        gaps = [[{w: (tasks[w]["after"] * far + x["gaps"][w][0] * HOP * hop - x["gaps"][w][1] * slow * pe) * z for w in needs[n]} for n, x in enumerate(tasks)]
+                for (slow, far, pe, pick, sc, hop), z in zip(SPEEDS, scale)]
+        hops = [HOP * s[5] * z for s, z in zip(SPEEDS, scale)]
+        fars = [s[1] * z for s, z in zip(SPEEDS, scale)]
+        banks = [tuple(PSUM.index(b) for b in sorted(x["banks"])) for x in tasks]
+        trios = [(k, k + 1, k + 2) for k in range(0, len(SPEEDS), 3)]
+        briefs = [[(queues.index(x["q"]),) + tuple(costs[m][n] for m in trio) + ([(w,) + tuple(gaps[m][n][w] for m in trio) for w in needs[n]], banks[n],
+                    x["moves"] and [(x["moves"][0] * fars[m], sum(x["moves"]) * fars[m]) for m in trio]) for n, x in enumerate(tasks)] for trio in trios]
+        finals = [n for n in range(N) if not nexts[n]]
+
+        def length(order, k3, old, same, check, limit):
+            brief = briefs[k3]
+            h0, h1, h2 = (hops[m] for m in trios[k3])
+            if same:
+                marks = old[1][:same // MARK + 1]
+                free, bank, engines = marks.pop()
+                end, free, bank = old[0][:], free[:], bank[:]
             else:
-                end, why, free, bank, engines = [0] * (len(tasks) + 1), [-1] * (len(tasks) + 1), dict.fromkeys(Q, (0, -1)), dict.fromkeys(PSUM, ("p", 0, -1)), (0, -1)
-                marks = []
-            for k in range(MARK * len(marks), len(order), MARK):
-                marks.append((dict(free), dict(bank), engines))
+                marks, end, free, bank, engines = [], [0] * N, [(0, 0, 0)] * 5, [(2, 0, 0, 0)] * 8, (0, 0, 0)
+            for k in range(MARK * len(marks), N, MARK):
+                if k > check:
+                    x, y = old[1][len(marks)][0], free
+                    if min(sum(y[0]) - sum(x[0]), sum(y[1]) - sum(x[1])) > limit:
+                        return None
+                marks.append((free[:], bank[:], engines))
                 for n in order[k:k + MARK]:
-                    q, cost, needs, banks, moves = brief[n]
-                    at, who = free[q]
-                    for w, d in needs:
-                        d += end[w]
-                        if d > at:
-                            at, who = d, w
-                    if banks:
-                        for b in banks:
-                            o = bank[b]
-                            if o[1] > at and o[0] != q:
-                                at, who = o[1:]
-                        o = (q, at + cost + hop, n)
-                        for b in banks:
+                    q, c0, c1, c2, need, bk, moves = brief[n]
+                    a0, a1, a2 = free[q]
+                    for w, d0, d1, d2 in need:
+                        e0, e1, e2 = end[w]
+                        e0 += d0
+                        if e0 > a0:
+                            a0 = e0
+                        e1 += d1
+                        if e1 > a1:
+                            a1 = e1
+                        e2 += d2
+                        if e2 > a2:
+                            a2 = e2
+                    if bk:
+                        for b in bk:
+                            o, e0, e1, e2 = bank[b]
+                            if o != q:
+                                if e0 > a0:
+                                    a0 = e0
+                                if e1 > a1:
+                                    a1 = e1
+                                if e2 > a2:
+                                    a2 = e2
+                        o = (q, a0 + c0 + h0, a1 + c1 + h1, a2 + c2 + h2)
+                        for b in bk:
                             bank[b] = o
-                    free[q] = (at + cost, n)
                     if moves:
-                        if engines[0] - moves[0] > at:
-                            at, who = engines[0] - moves[0], engines[1]
-                        engines = (at + moves[1], n)
-                    end[n] = at + cost
-                    why[n] = who
-            last, why[-1] = max((end[n] + tasks[n]["after"] * far, n) for n in finals)
-            return last, why, end, marks
+                        free[q] = (a0 + c0, a1 + c1, a2 + c2)
+                        a0, a1, a2 = max(a0, engines[0] - moves[0][0]), max(a1, engines[1] - moves[1][0]), max(a2, engines[2] - moves[2][0])
+                        engines = (a0 + moves[0][1], a1 + moves[1][1], a2 + moves[2][1])
+                        end[n] = (a0 + c0, a1 + c1, a2 + c2)
+                    else:
+                        free[q] = end[n] = (a0 + c0, a1 + c1, a2 + c2)
+            lasts = [max((end[n][u] + tasks[n]["after"] * fars[m], n) for n in finals) for u, m in enumerate(trios[k3])]
+            return end, marks, lasts, sum(x[0] for x in lasts)
 
-        def total(order, mixes=range(6), limit=None, same=0):
+        runs, tried = [None] * len(trios), []
+
+        def total(order, limit=1e12, same=0, check=1e9):
             new, gap = [], 0
-            for k, mix in enumerate(mixes):
-                new.append(length(order, mix, runs[k] if same else None, same))
-                if limit is not None:
-                    gap += (new[k][0] - runs[k][0]) / sum(SPEEDS[mix][:2]) * 6 / len(mixes)
-                    if gap > limit + SLACK * (len(mixes) - 1 - k):
+            for k3 in range(len(trios)):
+                r = length(order, k3, runs[k3], same, check, limit + SLACK - gap)
+                if r is None:
+                    return 1e12
+                if limit < 1e12:
+                    gap += r[3] - runs[k3][3]
+                    if gap > limit + SLACK * (len(trios) - 1 - k3):
                         return 1e12
+                new.append(r)
             tried[:] = new
-            return sum(r[0] / sum(SPEEDS[x][:2]) for r, x in zip(new, mixes)) * 6 / len(mixes)
+            return sum(r[3] for r in new)
 
         def blocks(order):
-            found = []
             runs[:] = tried
-            for run in runs:
-                why = run[1]
-                n = why[-1]
-                while why[n] >= 0:
-                    if why[n] not in before[n]:
-                        found.append((why[n], n))
-                    n = why[n]
+            held, ahead, found = {}, [None] * N, []
+            for n in order:
+                q = tasks[n]["q"]
+                ahead[n] = [held.get(q)] + [held.get(b) for b in banks[n]] + [held.get("engines")] * bool(tasks[n]["moves"])
+                held[q] = n
+                for b in banks[n]:
+                    held[b] = n
+                if tasks[n]["moves"]:
+                    held["engines"] = n
+            for k3, trio in enumerate(trios):
+                end = runs[k3][0]
+                for u, m in enumerate(trio):
+                    n = runs[k3][2][u][1]
+                    while n is not None:
+                        at, who = end[n][u] - costs[m][n] - 1e-6, None
+                        for w, d in gaps[m][n].items():
+                            if end[w][u] + d >= at:
+                                who = w
+                        if who is None and at > 0:
+                            who = max((end[w][u] + hops[m] * (tasks[w]["q"] != tasks[n]["q"]), w) for w in ahead[n] if w is not None)[1]
+                            if tasks[n]["moves"] and ahead[n][-1] is not None and end[who][u] < at:
+                                who = ahead[n][-1]
+                        if who is not None and who not in before[n]:
+                            found.append((who, n))
+                        n = who
             return found
-
-        runs, tried = [], []
 
         rng = np.random.default_rng(SEED)
 
-        step, seen_, table_ = [], {}, {}
+        step, seen_ = [], {}
         for x in tasks:
             o = (x["calls"][0][1] + x["calls"][0][2])[0]
-            name = (x["stage"], x["q"], "e" if o[1] in PSUM[:EB] else o[1].rstrip("0123") if "_" in o[1][2:-1] else o[1], o[2])
+            name = "%s%s:%s%s%d" % (x["stage"][0], x["stage"][-1], x["q"], "e" if o[1] in PSUM[:3] else o[1].rstrip("0123") if "_" in o[1][2:-1] else o[1], o[2])
             seen_[name, x["round"]] = seen_.get((name, x["round"]), 0) + 1
-            step.append(name + (seen_[name, x["round"]],))
-        first = [min(start[n] for n, x in enumerate(tasks) if x["round"] == t and step[n][2] == "yg") for t in range(RO)]
-        for t in (3, 0, 2, 1):
-            table_.update({step[n]: start[n] - first[t] * (x["stage"] != "start") for n, x in enumerate(tasks) if x["round"] == t})
-        names = sorted(table_)
+            step.append(name + ".%d" % seen_[name, x["round"]])
+        names = sorted(set(step))
         where = np.array([names.index(x) for x in step])
-        times = np.array([table_[x] for x in names])
-        shift = np.array([first[0] * (x["stage"] != "start") + (first[2] - first[1]) * x["round"] for x in tasks])
-        if HAND:
-            shift = np.array([first[0] * (x["stage"] != "start") + HAND["period"] * x["round"] for x in tasks])
-            for k, x in enumerate(names):
-                if x[0] != "start":
-                    v = HAND.get("%s%s%d" % x[1:4], 3000)
-                    times[k] = 12 * (v[x[4] - 1] if isinstance(v, list) else v)
+        rounds = np.array([x["round"] + (x["stage"] != "start") for x in tasks])
+        opens = [[n for n in range(N) if rounds[n] == t + 1 and ":vd3" in step[n]] for t in range(RO)]
+
+        def timetable(where, own):
+            start = sum(np.array([e[u] for e in runs[k3][0]]) - np.array(costs[m]) for k3, trio in enumerate(trios) for u, m in enumerate(trio)) / 3
+            first = np.array([0] + [min(start[n] for n in opens[t]) for t in range(RO)])
+            times = np.zeros(3 * len(names))
+            for t in ((4, 1, 3, 2, 0) if not own else (3, 4, 1, 2, 0)):
+                times[where[rounds == t]] = start[rounds == t] - first[t]
+            if not own:
+                first[1:] = first[1] + (first[3] - first[2]) * np.arange(RO)
+            return times, first[rounds]
+
+        given = {k: 10 * float(v) for k, v in (x.split("=") for x in TIMES.split())}
+        times = np.array([given[x] for x in names])
+        shift = (given["first"] + given["period"] * (rounds - 1)) * (rounds > 0)
         order = in_order((times[where] + shift).tolist())
-        best = now = (total(order, SOME), order, times)
-        INFO["first"] = now[0]
-        pairs = blocks(order)
+        best = now = (total(order), order)
+        pairs, own, kept = blocks(order), False, (times, shift)
         for n in range(STEPS):
             if n == STEPS - APART:
-                own = np.array([where[k] + len(names) * CLASS[x["round"]] for k, x in enumerate(tasks)])
-                now, times, where = best[:2], np.tile(best[2], 3), own
-                best = now + (times,)
-                total(now[1], SOME)
+                times, shift = np.tile(kept[0][:len(names)], 3), kept[1]
+                where, own, now = where + len(names) * np.array((0,) + CLASS)[rounds], True, best
+                total(now[1])
                 pairs = blocks(now[1])
+            elif n % ANEW == 0:
+                new, moved = timetable(where, own)
+                order = in_order((new[where] + moved).tolist())
+                cost = total(order)
+                if cost <= now[0] + 100 + LOOSE * max(0, 0.7 - n / (STEPS - APART)):
+                    now, times, shift, pairs = (cost, order), new, moved, blocks(order)
             new = times.copy()
             if rng.random() < AIM:
                 u, v = pairs[int(rng.integers(len(pairs)))]
@@ -671,120 +619,22 @@ def rank_program(g, core, T, topo):
                             key[w], new[where[w]] = at, at - shift[w]
                             todo += nexts[w]
             else:
-                at = int(rng.integers(len(tasks)))
+                at = int(rng.integers(N))
                 new[np.unique(where[at:at + (1 if rng.random() < 0.6 else int(rng.integers(2, 12)))])] += rng.normal() * (150, 500, 1500)[int(rng.integers(3))]
             order = in_order((new[where] + shift).tolist())
             if order == now[1]:
                 times = new
                 continue
-            limit = (WARM * (1 - n / (STEPS - APART)) if n < STEPS - APART else MILD * (STEPS - n) / APART) * rng.exponential()
-            cost = total(order, SOME, limit)
+            limit = (WARM * (1 - n / (STEPS - APART)) if not own else MILD * (STEPS - n) / APART) * rng.exponential()
+            same = next(k for k, (u, v) in enumerate(zip(order, now[1])) if u != v)
+            cost = total(order, limit, same, same + 2 * AFTER)
             if cost <= now[0] + limit:
                 pairs = blocks(order)
                 now, times = (cost, order), new
                 if cost < best[0]:
-                    best = (cost, order, new)
-        INFO["steps"] = best[0]
+                    best, kept = now, (new, shift)
 
-        def pack(key, mix, back_):
-            brief, far, hop = briefs[mix], SPEEDS[mix][1], HOP * SPEEDS[mix][5]
-            order = in_order(key) if not back_ else in_order([-k for k in key])[::-1]
-            busy = {r: ([], [], []) for r in list(Q) + list(PSUM) + ["engines"]}
-            end = [0] * len(tasks)
-            for n in order:
-                q, cost, needs, banks, moves = brief[n]
-                at = tasks[n]["after"] * far if back_ else 0
-                for w, d in (later[mix][n] if back_ else needs):
-                    d += end[w]
-                    if d > at:
-                        at = d
-                held = [(busy[q], 0, cost, None)] + [(busy[b], -hop, cost + hop, q) for b in banks]
-                if moves:
-                    held.append((busy["engines"], cost - moves[1], cost - moves[0], None) if back_ else (busy["engines"], moves[0], moves[1], None))
-                again = True
-                while again:
-                    again = False
-                    for (los, his, qs), lo, hi, mine in held:
-                        k = find(his, at + lo)
-                        while k < len(los) and los[k] < at + hi:
-                            if qs[k] != mine:
-                                at, again = his[k] - lo, True
-                            k += 1
-                for (los, his, qs), lo, hi, mine in held:
-                    if mine:
-                        lo, hi = 0, cost
-                    k = find(his, at + lo)
-                    los.insert(k, at + lo)
-                    his.insert(k, at + hi)
-                    qs.insert(k, q)
-                end[n] = at + cost
-            return end
-
-        def find(xs, x):
-            lo, hi = 0, len(xs)
-            while lo < hi:
-                mid = (lo + hi) // 2
-                if xs[mid] > x + 1e-6:
-                    hi = mid
-                else:
-                    lo = mid + 1
-            return lo
-
-        later = [[[] for x in tasks] for b in briefs]
-        for mix, brief in enumerate(briefs):
-            for n, x in enumerate(brief):
-                for w, d in x[2]:
-                    later[mix][w].append((n, d))
-        def decoded(times):
-            end = pack((times[where] + shift).tolist(), BASE, False)
-            order = in_order([e - x[1] for e, x in zip(end, briefs[BASE])])
-            return (total(order, SOME), order, times)
-
-        if TRIES:
-            now = best = decoded(best[2])
-            pairs = blocks(now[1])
-        for n in range(TRIES):
-            if n == TRIES - TRIES // 4:
-                own = np.array([where[k] + len(names) * CLASS[x["round"]] for k, x in enumerate(tasks)])
-                where = own
-                now = best = best[:2] + (np.tile(best[2], 3),)
-            new = now[2].copy()
-            if rng.random() < AIM2:
-                u, v = pairs[int(rng.integers(len(pairs)))]
-                key = new[where] + shift
-                if rng.random() < 0.5:
-                    new[where[v]] = min(key[u], key[v]) - 1 - rng.exponential() * 100 - shift[v]
-                else:
-                    at, todo = max(key[u], key[v]) + 1 + rng.exponential() * 100, [u]
-                    while todo:
-                        w = todo.pop()
-                        if key[w] < at:
-                            key[w], new[where[w]] = at, at - shift[w]
-                            todo += nexts[w]
-            else:
-                at = int(rng.integers(len(tasks)))
-                new[np.unique(where[at:at + (1 if rng.random() < 0.5 else int(rng.integers(2, 20)))])] += rng.normal() * (200, 700, 2000)[int(rng.integers(3))]
-            new = decoded(new)
-            if new[0] <= now[0] + WARM2 * (1 - n / TRIES) * rng.exponential():
-                pairs, now = blocks(new[1]) or pairs, new
-                if new[0] < best[0]:
-                    best = new
-        best = (total(best[1]), best[1])
-        INFO["tries"] = best[0]
-        now = best = best[:2]
-        for n in range(PACKS):
-            mix = MIXES[int(rng.integers(len(MIXES)))]
-            end = length(now[1], mix)[2]
-            noise = rng.normal(size=len(tasks)) * NOISE[int(rng.integers(len(NOISE)))] * (rng.random(len(tasks)) < SHARE)
-            end = pack([-end[k] + noise[k] for k in range(len(tasks))], mix, True)
-            end = pack([-e for e in end], mix, False)
-            order = in_order([e - x[1] for e, x in zip(end, briefs[mix])])
-            new = (total(order), order)
-            if new[0] <= now[0] + LOOSE * (1 - n / PACKS) * rng.exponential():
-                now, best = new, min(best, new)
-        INFO["packs"] = best[0]
-
-        now = best = best[:2]
+        now = best
         total(now[1])
         pairs = blocks(now[1])
         for n in range(MOVES):
@@ -793,8 +643,8 @@ def rank_program(g, core, T, topo):
                 u, v = pairs[int(rng.integers(len(pairs)))]
                 lo, hi = sorted((order.index(u), order.index(v)))
             else:
-                lo = int(rng.integers(len(order) - 1))
-                hi = min(len(order) - 1, lo + 1 + int(rng.exponential() * REACH))
+                lo = int(rng.integers(N - 1))
+                hi = min(N - 1, lo + 1 + int(rng.exponential() * REACH))
             run = order[lo:hi + 1]
             if rng.random() < 0.5:
                 moved = {run[-1]}
@@ -812,15 +662,12 @@ def rank_program(g, core, T, topo):
             if order == now[1]:
                 continue
             limit = HEAT * (1 - n / MOVES) * rng.exponential()
-            new = (total(order, range(6), limit, lo), order)
+            new = (total(order, limit, lo, hi + AFTER), order)
             if new[0] <= now[0] + limit:
                 pairs = blocks(order)
                 now, best = new, min(best, new)
-        INFO["total"] = best[0]
-        INFO["best"] = [int(length(best[1], mix)[0] * 0.83) for mix in range(len(SPEEDS))]
-        end = length(best[1], SHOW)[2]
-        INFO["line"] = [(int((end[n] - briefs[SHOW][n][1]) * 0.83), int(briefs[SHOW][n][1] * 0.83), tasks[n]["q"], step[n][2], step[n][3], tasks[n]["round"]) for n in best[1]]
-        INFO["all"] = [{q: int(sum(b[1] for b in br if b[0] == q) * 0.83) for q in Q} for br in briefs]
+        INFO["total"] = total(best[1])
+        INFO["best"] = [int(tried[m // 3][2][m % 3][0] * 0.83 / scale[m]) for m in range(len(SPEEDS))]
         return best[1]
 
     if not PLAN:

import numpy as np
from concourse.mybir import AluOpType as Op, ActivationFunctionType as AF

RO = 4
F, B, H, I, U = "float32", "bfloat16", "float16", "int32", "uint16"
SCRATCH = {}
for _n, _w, _d in (
        ("xt_0", 2080, B), ("xt_1", 2080, B), ("nk", 256, I), ("np_", 256, I), ("yg", 4096, B), ("ph_", 256, H), ("kh", 256, H),
        ("sn", 256, B), ("sg", 256, H), ("mi", 256, I), ("v8", 16, I), ("l8", 16, U), ("sel", 768, H), ("pn16", 48, U), ("nr", 816, F),
        ("xn", 256, B), ("xr", 256, B), ("fl", 288, B), ("ms", 288, F), ("o16", 16, U), ("wt0", 1216, F), ("wt1", 1216, F),
        ("fr", 256, I), ("fu", 256, I), ("yk32", 256, F), ("pa", 256, H), ("pt", 256, I), ("pn", 256, I), ("yp32", 256, F),
        ("cy", 512, B), ("dk", 256, B), ("ys", 512, B), ("vv", 256, B), ("eq", 512, B), ("nm", 512, U), ("mw", 512, U),
        ("w16", 16, U), ("jk", 16, B), ("ac", 4, F), ("aa", 8, I), ("ab", 8, I),
        ("pi", 2, I), ("li", 2, I), ("lf", 2, F), ("l15", 2, F), ("ones", 128, B), ("neg", 512, B), ("gm", 128, B), ("idn", 128, B),
        ("idk", 128, B), ("idd", 128, B), ("i128", 128, B), ("n128", 128, B), ("gmf", 128, F), ("s15", 128, B), ("s5k", 128, B),
        ("qu", 128, B), ("z1", 143, B), ("zd", 143, B), ("zb", 143, B), ("cj", 128, B), ("rst", 128, F), ("ri", 144, I), ("rp", 144, F),
        ("ex", 2048, B), ("tm", 256, B), ("lane", 128, B), ("ij", 128, I), ("i3", 192, I), ("i4", 192, I), ("nil", 64, F), ("sc", 256, B),
        ("iq", 16, I), ("iu", 8, I), ("bl", 16, U), ("lutf", 256, B), ("lutk", 256, B), ("lutq", 256, B)):
    SCRATCH[_n] = ("sbuf", [128, _w], _d)
for _n, _w in (("d3", 256), ("a3", 256), ("ae", 288)):
    SCRATCH[_n] = ("sbuf", [128, 16, _w], B)
for _h in range(2):
    SCRATCH["kd%d" % _h] = ("dram", [8, 33, 64], F)
for _t in range(RO):
    for _n in ("k16_%d", "p16_%d") + (("ks_%d", "ps_%d") if _t < RO - 1 else ()):
        SCRATCH[_n % _t] = ("sbuf", [128, 256], U)
PSUM = ("e0", "e1", "e2", "e3", "c0", "c1_", "m0", "m1")
for _n in PSUM:
    SCRATCH[_n] = ("psum", [128, 512], F)
SEMAPHORES = (["v", "s", "p", "g", "lx", "oy", "kz"] + [x + h for x in ("lp", "lk", "kd", "wd", "ok", "op") for h in "01"]
              + ["%s%s%d" % (y, x, t) for x in ("k0_", "k1_", "p_") for t in range(1, RO) for y in "al"])
FIRST = "pkpk"
RELU = 2
PIECES = {2: ((0, 1), (1, 4)), 3: ((0, 1), (1, 4))}
PARTS = {1: ((0, 2), (2, 4))}
COPY = 4
SPARE = ("nm", "ae", "rst", "lutf", "lutk")
AIM, REACH, HEAT, WARM, MILD, LOOSE = 0.8, 8, 40, 250, 100, 1500
STEPS, APART, MOVES, SEED, CLASS = 8000, 2500, 3500, 3, (0, 1, 1, 2)
MARK, SLACK, AFTER, ANEW = 32, 400, 128, 1000
TIMES = """first=661 period=2517 c0:gkh0.1=419 c0:pc00.1=-47 c0:pc00.2=858 c0:pc00.3=1186 c0:pc064.1=1052 c0:pe3256.1=460 c0:pe3320.1=456
c0:pm0152.1=858 c0:pm0216.1=1057 c0:sa30.1=1145 c0:sa31024.1=875 c0:sa31536.1=897 c0:ssn0.1=1006 c0:swt00.1=1047 c0:syg0.1=176
c0:syg1024.1=286 c0:vd30.1=720 c0:vd31024.1=898 c0:vd31280.1=862 c0:vd31536.1=863 c0:vd31792.1=1063 c0:vd3256.1=533 c0:vd3512.1=536
c0:vd3768.1=542 c0:ykd00.1=740 c0:ywt0128.1=1186 c1:gkh128.1=287 c1:pc1_0.1=-171 c1:pc1_0.2=729 c1:pc1_0.3=836 c1:pc1_0.4=810
c1:pc1_64.1=855 c1:pe3384.1=487 c1:pe3448.1=225 c1:pm1152.1=454 c1:pm1216.1=485 c1:sa33072.1=730 c1:ssg128.1=773 c1:ssn128.1=785
c1:swt10.1=271 c1:syg2048.1=136 c1:syg2304.1=175 c1:syg3072.1=176 c1:syg3328.1=169 c1:va32048.1=483 c1:vd32048.1=206 c1:vd32304.1=203
c1:vd32560.1=9 c1:vd32816.1=12 c1:vd33072.1=232 c1:vd33328.1=227 c1:vd33584.1=222 c1:vd33840.1=209 c1:ykd10.1=382 c1:ywt1128.1=934
l0:gph_0.1=419 l0:pm00.1=1447 l0:pm0152.1=1322 l0:pm024.1=1315 l0:snr8.1=1794 l0:vl80.1=1356 l0:vmi0.1=1229 l0:vpn160.1=1529
l0:vsel0.1=1351 l0:vsel128.1=1325 l0:vsel256.1=1320 l0:vv80.1=1098 l1:gph_128.1=1034 l1:pm10.1=1098 l1:pm1152.1=1303 l1:pm124.1=1305
l1:snr416.1=1340 l1:vl88.1=1067 l1:vmi128.1=883 l1:vpn1624.1=1171 l1:vsel384.1=949 l1:vsel512.1=957 l1:vsel640.1=954 l1:vv88.1=910
n0:gfl0.1=1951 n0:gk16_0.1=2519 n0:pc00.1=1770 n0:pc0256.1=2211 n0:pc0328.1=2187 n0:pe0.1=1726 n0:pe0.2=1936 n0:pe0.3=1753
n0:pe0.4=1800 n0:pe0.5=1973 n0:pe0.6=1984 n0:pe0.7=2091 n0:pe0.8=1992 n0:sae0.1=2039 n0:sae1152.1=1799 n0:sae1728.1=2038
n0:sae576.1=2219 n0:sxn0.1=1665 n0:sxr0.1=1848 n0:vfr0.1=2328 n0:vfu0.1=2330 n0:vfu64.1=2329 n0:vks_0.1=2556 n0:vks_64.1=2549
n0:vms0.1=2247 n0:vo160.1=2309 n0:vyk320.1=2443 n0:vyk3264.1=2342 n0:yyk320.1=2607 n1:gfl144.1=1485 n1:gk16_128.1=2135
n1:gyk32128.1=2087 n1:gyk32192.1=2149 n1:pc1_0.1=1307 n1:pc1_256.1=1752 n1:pc1_328.1=1794 n1:pe0.1=446 n1:pe0.2=1325 n1:pe0.3=56
n1:pe0.4=1440 n1:pe0.5=231 n1:pe0.6=1452 n1:pe0.7=1534 n1:pe0.8=1728 n1:sae2304.1=1453 n1:sae2880.1=1533 n1:sae3456.1=1600
n1:sae4032.1=1728 n1:sxn128.1=1271 n1:sxr128.1=1380 n1:vfr128.1=2028 n1:vfu128.1=2077 n1:vfu192.1=2071 n1:vks_128.1=2189
n1:vks_192.1=2080 n1:vms144.1=1906 n1:vo168.1=1975 n1:yyk32128.1=2080 p0:gp16_0.1=1832 p0:gps_0.1=1827 p0:gyp320.1=1835
p0:pc0128.1=1535 p0:vpa0.1=1536 p0:vpn0.1=1627 p0:vpt0.1=1596 p0:yyp320.1=1835 p1:gps_128.1=1485 p1:gyp32128.1=1440
p1:pc1_128.1=1134 p1:vpa128.1=1087 p1:vpn128.1=1374 p1:vpt128.1=1358 p1:yyp32128.1=1440 st:gex0.1=1171 st:gex1024.1=193
st:gex1536.1=2013 st:gex512.1=1934 st:ggm0.1=-46 st:ggm0.2=136 st:gi30.1=276 st:gi3128.1=182 st:gi364.1=277 st:gidn0.1=-42
st:gij0.1=-46 st:giq0.1=949 st:giu0.1=-47 st:gk16_0.1=1150 st:glane0.1=1753 st:gp16_0.1=949 st:gpi0.1=-146 st:gri0.1=2426
st:gtm0.1=1052 st:gtm0.2=1499 st:sae0.1=96 st:sae0.2=347 st:sgmf0.1=1826 st:si1280.1=316 st:sidd0.1=431 st:sidk0.1=430
st:slutf0.1=88 st:slutk0.1=146 st:slutk0.2=937 st:sn1280.1=292 st:snm0.1=225 st:snm256.1=1804 st:snp_128.1=32 st:srst0.1=243
st:srst0.2=1433 st:ss5k0.1=432 st:szb0.1=1839 st:szd0.1=836 st:vaa0.1=179 st:vbl0.1=2026 st:vcj0.1=137 st:vcj0.2=413 st:vfl0.1=133
st:vfl17.1=298 st:vi40.1=414 st:viq1.1=2020 st:viu0.1=887 st:vk16_128.1=601 st:vl150.1=182 st:vlf0.1=281 st:vlf1.1=1145 st:vli0.1=71
st:vlutf2.1=420 st:vlutf3.1=602 st:vlutk2.1=611 st:vlutk3.1=718 st:vlutq0.1=184 st:vlutq0.2=190 st:vlutq2.1=629 st:vlutq3.1=719
st:vneg0.1=-12 st:vnil0.1=8 st:vnm0.1=2032 st:vnr0.1=1671 st:vones0.1=1 st:vp16_128.1=263 st:vqu0.1=914 st:vrp0.1=2464
st:vs150.1=313 st:vsc0.1=183 st:vsc1.1=185 st:vtm0.1=192 st:vtm31.1=1577 st:vxt_0.1=250 st:vxt_0.2=357 st:vz10.1=264 st:vz115.1=207
st:ynk0.1=385 st:ynk128.1=350 st:ynp_0.1=383 st:ywt0128.1=422 st:yxt_32.1=39 te:gxt_1056.1=-164 te:gxt_1568.1=734 te:gxt_32.1=1272
te:gxt_544.1=1090 te:pm0500.1=2297 te:sjk0.1=2236 te:srst0.1=3296 te:vaa0.1=2324 te:vab0.1=2328 te:vxt_0.1=1618 te:vxt_0.2=1635
te:vxt_0.3=1802 te:vxt_0.4=1839 te:vxt_0.5=2058 te:vxt_0.6=2374 te:vxt_0.7=2562 te:vxt_0.8=2137 te:yxt_32.1=2097 w0:gnm30.1=1604
w0:scy1.1=1606 w0:vcy0.1=1801 w0:vdk0.1=1632 w0:veq0.1=1878 w0:vmw0.1=1927 w0:vvv0.1=1977 w0:vw160.1=1999 w0:vys0.1=1803
w1:gnm286.1=1350 w1:scy257.1=1272 w1:vcy256.1=1525 w1:vdk128.1=1363 w1:veq256.1=1527 w1:vmw256.1=1550 w1:vvv128.1=1587
w1:vw168.1=1584 w1:vys256.1=1581"""
PLAN, INFO = [], {}
SPEEDS = ((1.03, 0.95, 0.87, 1.0, 1.1, 1.2), (1.3, 0.8, 0.87, 1.3, 0.7, 1.2), (1.45, 1.1, 0.87, 1.0, 1.2, 0.9),
          (1.2, 1.0, 1.45, 1.1, 0.8, 1.0), (1.05, 1.3, 1.35, 0.85, 1.3, 1.4), (1.4, 0.8, 1.25, 1.0, 1.0, 0.8),
          (1.05, 1.4, 0.87, 0.8, 1.5, 1.4), (1.5, 0.8, 0.87, 1.25, 1.5, 0.8), (1.5, 0.9, 0.87, 0.9, 1.0, 1.0))
TOP = 192 * 2.0 ** 17 + 2048
HUGE = 2.0 ** 40
ROUND = 1.5 * 2.0 ** 29
HOP, CALL, PICK, ACT, GATHER, SCATTER, ISSUE, LOCAL, REMOTE, FAR, BYTES, MATMUL, COLUMN, ROWS, ROW = 176, 40, 88, 77, 1.45, 3.5, 242, 1300, 588, 2800, 152, 10, 0.45, 2000, 150


def rank_program(g, core, T, topo):
    rank = T.rank_of(core)
    if rank is None:
        return
    n_ranks = len(T.cores)
    Q = {"v": g.vector, "s": g.scalar, "p": g.tensor, "g": g, "y": g.sync}
    V, S, P = g.vector, g.scalar, g.tensor

    def a(name, lo=0, hi=None, step=None):
        hi = SCRATCH[name][1][1] if hi is None else hi
        return (T[name][:, lo:hi] if step is None else T[name][:, lo:hi:step], name, lo, hi, len(range(lo, hi, step or 1)))

    def back(name, lo, hi):
        return (T[name][:, hi - 1:(lo - 1 if lo else None):-1], name, lo, hi, hi - lo)

    def a3(name, q0, q1, c0=None, c1=None):
        w = SCRATCH[name][1][2]
        return (T[name][:, q0:q1, :] if c0 is None else T[name][:, q0:q1, c0:c1], name, w * q0, w * q1, (q1 - q0) * (w if c0 is None else c1 - c0))

    def row(name, q):
        w = SCRATCH[name][1][2]
        return (T[name][:, q], name, w * q, w * q + w, w)

    def half(name, h, w=128):
        return a(name, w * h, w * h + w)

    def top(name):
        return (T[name][0:16, :],) + a(name)[1:]

    def names16(u, h):
        return half("pn16", 3 * h + 2 - u, 8)

    def ind(win, off):
        return (win[0].indirect(off[0]), win, off)

    def flat(lst):
        r = []
        for x in lst:
            r += [x] if isinstance(x[1], str) else [x[1], x[2]]
        return r

    tasks, now_ = [], ["start", 0]

    def task(q, kind, call, outs, ins, cost, after=0, more=False, moves=None, picks=0):
        if not more:
            tasks.append(dict(q=q, kind=kind, calls=[], after=after, moves=moves, stage=now_[0], round=now_[1], picks=picks))
        tasks[-1]["calls"].append((call, flat(outs), flat(ins), cost + picks))

    def vec(fn, out, ins, rate):
        if isinstance(out[1], tuple):
            task("v", "call", fn, [out[1]], ins + [out[2]], PICK, picks=SCATTER * ins[0][4])
        elif ins and isinstance(ins[0][1], tuple):
            task("v", "call", fn, [out], ins, PICK, picks=GATHER * out[4])
        else:
            task("v", "call", fn, [out], ins, CALL + max(64, rate * out[4]))

    def narrow(*x):
        return 0.5 if all(isinstance(y[1], str) and SCRATCH[y[1]][2] in (B, H, U) for y in x) else 1

    def copy(out, in_):
        vec(lambda: V.tensor_copy(out[0], in_[0]), out, [in_], narrow(out, in_))

    def tt(out, x, y, op):
        vec(lambda: V.tensor_tensor(out[0], x[0], y[0], op), out, [x, y], 1 if y[1] in PSUM else 2)

    def ts(out, x, s1, op0, s2=None, op1=None):
        ins = [x] + [s for s in (s1, s2) if isinstance(s, tuple)]
        c = [s[0] if isinstance(s, tuple) else s for s in (s1, s2)]
        if op1 is None:
            vec(lambda: V.tensor_scalar(out[0], x[0], c[0], None, op0), out, ins, narrow(out, x))
        else:
            vec(lambda: V.tensor_scalar(out[0], x[0], c[0], c[1], op0, op1), out, ins, narrow(out, x))

    def scan(out, d0, d1, first, op0, op1):
        vec(lambda: V.tensor_tensor_scan(out[0], d0[0], d1[0], first, op0, op1), out, [d0, d1], narrow(out, d0, d1))

    def fill(out, val):
        if out[1] in SPARE:
            act(out, a("neg", 0, out[4]), AF.Copy, scale=-val)
        else:
            vec(lambda: V.memset(out[0], val), out, [], narrow(out))

    def act(out, in_, func=AF.Copy, acc=None, **kw):
        cost, picks = (80, GATHER * out[4]) if isinstance(in_[1], tuple) else (ACT + out[4], 0)
        if acc is None:
            task("s", "call", lambda: S.activation(out[0], in_[0], func, **kw), [out], [in_], cost, picks=picks)
        else:
            task("s", "call", lambda: S.activation(out[0], in_[0], func, accum_out=acc[0], **kw), [out, acc], [in_], cost)

    def mm(out, l, r, start, stop, cut=False, holds=None, join=False):
        task("p", "call", lambda: P.matmul(out[0], l[0], r[0], start, stop), [holds or out], [l, r],
             MATMUL + max(64, r[4]) * (4 if SCRATCH[l[1]][2] == F else 1) * COLUMN, more=join or not (start or cut))

    def iota(out, pattern, base, cm):
        task("g", "call", lambda: g.iota(out[0], pattern, base, cm), [out], [], 160 + 2 * out[4])

    def asel(out, in_, pattern, cop, base, cm, other=0.0):
        task("g", "call", lambda: g.affine_select(out[0], in_[0], pattern, cop, other, base, cm), [out], [in_], 200 + 2 * out[4])

    def pool(out, in_):
        asel(out, in_, [[0, out[4]]], Op.is_equal, 0, 0)

    def dmas(q, sem, pairs, outs, ins, size):
        task(q, "dma", (sem, pairs), outs, ins, ISSUE * len(pairs), max(LOCAL, LOCAL + size / BYTES - ISSUE * (len(pairs) - 1)),
             moves=(ISSUE + LOCAL / 2, size / BYTES))

    def scratch(h):
        return (None, "kd%d" % h, 0, 1, 0)

    nxt, prv = T.cores[(rank + 1) % n_ranks], T.cores[(rank - 1) % n_ranks]

    def send(to, names, sem, dst, src):
        task("g", "send", ("a" + sem, "l" + sem, dst, src), [to], [names], REMOTE, FAR, moves=(REMOTE, ROWS))

    def xt(t, lo=32, hi=2080):
        return a("xt_%d" % (t % 2), lo, hi)

    dmas("s", "lp1", [(T.np_[:, 128:256], T.ph[:, 128:256])], [half("np_", 1)], [], 2 ** 16)
    dmas("y", "lx", [(xt(0)[0], T.x0[:])], [xt(0)], [], 2 ** 19)
    dmas("y", "lk1", [(T.nk[:, 128:256], T.ka[:, 128:256])], [half("nk", 1)], [], 2 ** 16 + 128 * ROW)
    dmas("y", "lp0", [(T.np_[:, 0:128], T.ph[:, 0:128])], [half("np_", 0)], [], 2 ** 16 + 128 * ROW)
    dmas("y", "lk0", [(T.nk[:, 0:128], T.ka[:, 0:128])], [half("nk", 0)], [], 2 ** 16 + 128 * ROW)
    for h, turn in ((1, copy), (0, pool)):
        turn(half("p16_0", h), half("np_", h))
        turn(half("k16_0", h), half("nk", h))

    fill(a("ones"), 1.0)
    fill(a("neg"), -1.0)
    iota(a("pi"), [[0, 2]], 0, 1)
    asel(a("gm"), a("ones"), [[-16, 8], [0, 16]], Op.is_ge, 0, 1)
    asel(a("gm"), a("gm"), [[16, 8], [0, 16]], Op.is_ge, 15, -1)
    asel(a("idn"), a("ones"), [[1, 128]], Op.is_equal, 0, -1)
    iota(a("ij"), [[0, 8], [1, 16]], 0, 0)
    iota(a("i3", 0, 64), [[1, 4], [1, 16]], 129, -1)
    iota(a("i3", 64, 128), [[-1, 4], [1, 16]], 127, -1)
    iota(a("i3", 128, 192), [[0, 4], [1, 16]], 128, -1)
    iota(a("ri"), [[0, 2], [16, 4], [64, 18]], 64 - 2048, 0)
    for b in range(4):
        asel(a("ex", 512 * b, 512 * b + 512), a("neg"), [[1, 32], [0, 16]], Op.is_equal, 32 * b, -1)
    for x, val in ((a("nil"), 0.0), (a("z1"), 0.0), (a("qu"), 0.25), (a("fl"), -1040.0), (a("fl", 17, 288, 18), -2.0 ** 14), (a("rst"), -4e9),
                   (a("rst", 0, 128, 16), TOP), (a("aa"), 0), (a("lutf"), 0.0), (a("lutk"), -512.0), (a("lutk", 0, 1), -768.0), (a("lutq"), 0.0),
                   (a("lutq", 0, 1), -1.0), (xt(0, 0, 32), 0.0), (xt(1, 0, 32), 0.0), (a3("ae", 0, 16, 0, 16), 0.0), (a3("ae", 0, 16, 272, 288), 0.0)):
        fill(x, val)
    dmas("y", "kz", [(T["kd%d" % h][:, 0, :], T.nil[0:8, :]) for h in range(2)] + [(T["wt%d" % h][0:128:16, 128:1152], T.nil[:]) for h in range(2)],
         [a("wt0", 128, 1152), a("wt1", 128, 1152), scratch(0), scratch(1)], [a("nil")], 2 ** 16 + 256 * ROW)
    ts(a("li"), a("pi"), 15, Op.bitwise_and)
    copy(a("lf"), a("li"))
    ts(a("l15", 0, 1), a("lf", 0, 1), 15.0, Op.is_equal)
    copy(a("z1", 15, 143, 16), a("gm", 0, 128, 16))
    ts(a("s15"), a("gm"), a("l15", 0, 1), Op.mult)
    for z, x, w in (("gmf", "gm", 2.0 ** 18), ("s5k", "s15", 4096.0), ("idk", "idn", 4096.0), ("zd", "z1", 2.0 ** 17), ("zb", "z1", 4096.0),
                    ("n128", "idn", -128.0), ("i128", "idn", 128.0), ("idd", "idn", 2.0 ** 17)):
        act(a(z), a(x), scale=w)
    vec(lambda: V.memset(T.cj[0:64, :], -13.0 * 2 ** 17), a("cj"), [], 0.5)
    vec(lambda: V.tensor_scalar(T.cj[64:128, :], T.ij[64:128, :], 128.0, 96.0, Op.mult, Op.add), a("cj"), [a("ij")], 1)
    ts(a("i4"), a("i3"), 15, Op.bitwise_and)
    for sb in range(2):
        ts(a("lutf", 2 + sb, 256, 4), a("i4", 64 * sb, 64 * sb + 64), 0.0, Op.is_equal, 4096.0, Op.mult)
        ts(a("lutk", 2 + sb, 256, 4), a("i4", 128, 192), 0.0, Op.is_equal, 4096.0, Op.mult)
        ts(a("lutq", 2 + sb, 256, 4), a("i4", 128, 192), 0.0, Op.is_equal)
    ts(a("rp"), a("ri"), a("lf", 0, 1), Op.add)
    fill(a("sc"), 0.0)
    fill(a("sc", 1, 256, 2), -128.0)
    fill(a("tm"), 32.0)
    asel(a("tm"), a("tm"), [[0, 8], [-1, 16], [-32, 2]], Op.is_ge, 31, 1, 16384.0)
    asel(a("tm", 0, 256, 2), a("tm", 0, 256, 2), [[0, 4], [1, 2], [0, 16]], Op.is_gt, 0, 0, 16384.0)
    fill(a("tm", 31, 256, 32), HUGE)
    asel(a("lane"), a("ones"), [[0, 8], [1, 16]], Op.is_equal, 0, -1)
    fill(a("nr", 0, 816, 408), HUGE)
    iota(a("iq"), [[1, 8], [0, 2]], 8, 0)
    iota(a("iu"), [[-1, 8]], -8, 0)
    ts(a("iu"), a("iu"), a("l15", 0, 1), Op.mult)
    tt(a("iq", 1, 16, 2), a("iq", 1, 16, 2), a("iu"), Op.add)
    copy(a("bl"), a("iq"))
    ts(a("lf", 1, 2), a("lf", 0, 1), 16.0, Op.add)
    for h in range(2):
        fill(half("nm", h, 256), 0.0)
    ts(a("nm", 0, 512, 64), a("nil", 0, 8), 0.0, Op.mult, a("lf", 1, 2), Op.add)

    def lanes(out, z, src, c, first, end, lo=0, w=16, cut=False):
        for i in range(16):
            mm(out, a(z, 15 - i, 143 - i), a3(src, 4 * c, 4 * c + 4, lo + 16 * i, lo + 16 * i + w), first and i == 0, end and i == 15, cut and i == 0)

    def shifted(t, h):
        wt, at = "wt%d" % h, 256 + 128 * h
        pool(half("kh", h), half("k16_%d" % t, h))
        for u, (x, y) in enumerate((("s15", "s5k"), ("idn", "idk"))):
            o = a("e3", at + 64 * u, at + 64 * u + 64)
            mm(o, a(x), half("kh", 2 * h, 64), True, False)
            mm(o, a(y), half("kh", 2 * h + 1, 64), False, True)
        act(a(wt, 0, 128), a("e3", at, at + 128))
        w, k = T[wt], T["kd%d" % h]
        dmas("y", "kd%d" % h, [(k[:, 1:17, :], w[:, 64:128]), (k[:, 17:33, :], w[:, 0:64])], [scratch(h)], [a(wt, 0, 128)], 2 ** 16 + 256 * ROW)
        dmas("y", "wd%d" % h, [(w[j:128:16, 128:1152], k[:, 1 + j:17 + j, :]) for j in range(1, 16)] + [(w[:, 1152:1216], k[:, 0:16, :])],
             [a(wt, 128, 1216)], [scratch(h)], 2 ** 19 + 240 * ROW)

    def half_round(t, h):
        last, table = t == RO - 1, xt(t)
        c0, c1 = 2 * h, 2 * h + 2
        k16, p16, cb, m = "k16_%d" % t, "p16_%d" % t, PSUM[4 + h], PSUM[6 + h]
        sf, sa, sk = [half("sel", 3 * h + u) for u in range(3)]
        l8, code, lists, at = half("l8", h, 8), a(cb, 0, 128), a(m, 0, 24), 408 * h + 8

        now_[0] = "codes%d" % h
        mm(code, a("ones"), a("cj"), True, False, holds=a(cb))
        for c in range(c0, c1):
            mine, other = (p16, k16) if FIRST[c] == "p" else (k16, p16)
            for lo, hi in PIECES.get(c, ((0, 4),)):
                act(a("yg", 1024 * c + 256 * lo, 1024 * c + 256 * hi), ind(table, a(mine, 64 * c + 16 * lo, 64 * c + 16 * hi)))
            for q in range(4 * c, 4 * c + 4):
                tt(row("d3", q), ind(table, half(other, q, 16)), half("yg", q, 256), Op.subtract)
            for lo, hi in PARTS.get(c, ((0, 4),)):
                if c == RELU:
                    ts(a3("a3", 4 * c + lo, 4 * c + hi), a3("d3", 4 * c + lo, 4 * c + hi), 0.0, Op.min, -2.0, Op.mult)
                else:
                    act(a3("a3", 4 * c + lo, 4 * c + hi), a3("d3", 4 * c + lo, 4 * c + hi), AF.Abs)
            lanes(a(m, 152 + 64 * (c - c0), 216 + 64 * (c - c0)), "z1", "d3", c, True, True)
            lanes(half(cb, c - c0, 64), "zd", "a3", c, False, False, cut=True)
        act(half("sn", h), a(m, 152, 280), AF.Sign)
        if RELU // 2 == h:
            act(half("sg", RELU, 64), a(m, 152 + 64 * (RELU - c0), 216 + 64 * (RELU - c0)))
            mm(half(cb, RELU - c0, 64), a("idd"), half("sg", RELU, 64), False, False, cut=True)
        for c in range(c0, c1):
            mm(half(cb, c - c0, 64), a("i128" if FIRST[c] == "k" else "n128"), half("sn", c, 64), False, c == c1 - 1, cut=c == c0)
        shifted(t, h)

        now_[0] = "least%d" % h
        pool(half("ph_", h), half(p16, h))
        scan(half("mi", h), a("rst"), code, 0.0, Op.max, Op.min)
        ts(half("v8", h, 8), a("mi", 128 * h + 15, 128 * h + 128, 16), (255 << 11) - 2 ** 31, Op.bitwise_and, 11, Op.arith_shift_right)
        copy(l8, half("v8", h, 8))
        tt(sf, ind(a("lutf"), l8), half("ph_", h), Op.min)
        tt(sk, ind(a("lutk"), l8), half("ph_", h), Op.min)
        tt(sa, ind(a("lutq"), l8), half("kh", h), Op.mult)
        for u, z in enumerate(("z1", "zb")):
            mm(a(m, 24 + 64 * u, 88 + 64 * u), a(z, 15, 143), a("sel", sf[2] + 64 * u, sf[2] + 64 * u + 64), True, True, join=u > 0)
        for i in range(16):
            mm(lists, a("z1", 15 - i, 143 - i), a("sel", 384 * h + i, 384 * h + 384, 16), i == 0, False)
        mm(a(m, 16, 24), a("ones"), a("qu", 0, 8), False, True)
        copy(half("pn16", h, 24), lists)
        mm(a(m, 152, 408), top("lane"), top("tm"), True, False)
        mm(a(m, 184, 408, 2), a("gm"), a("sel", sk[2], sk[3] - 16), False, False)
        mm(a(m, 153, 408, 2), a("gm"), sk, False, True)
        act(a("nr", at, at + 392), a(m, 16, 408))

        now_[0] = "near%d" % h
        act(half("xn", h), ind(table, names16(2, h)))
        mm(code, half("xn", h), a("idn"), True, True)
        act(half("xr", h), code)
        pool(a("fl", 144 * h, 144 * h + 144, 18), a("nr", at, at + 8))
        for c in range(c0, c1) if h else range(c1 - 1, c0 - 1, -1):
            for b in (2 * c, 2 * c + 1):
                e = a("e%d" % (turns[0] % 3))
                turns[0] += 1
                mm(e, a("idn"), half("yg", b, 512), True, False)
                if FIRST[c] == "p":
                    mm(e, a("idn"), a3("d3", 2 * b, 2 * b + 2), False, False)
                mm(e, half("xr", h), half("ex", b % 4, 512), False, True, cut=True)
                act(a3("ae", 2 * b, 2 * b + 2, 16, 272), e, AF.Abs)
            o = a(cb, 256 + 72 * (c - c0), 328 + 72 * (c - c0))
            mm(o, a("idk"), half("fl", c, 72), True, False)
            lanes(o, "zb", "ae", c, False, True, 15, 18)
        scan(back("ms", 144 * h, 144 * h + 144), back(cb, 256, 400), back("rp", 0, 144), -4096.0, Op.min, Op.max)
        ts(half("o16", h, 8), a("ms", 144 * h, 144 * h + 144, 18), 1.0, Op.mult, 2048.0, Op.add)
        tt(half("fr", h), ind(a("wt%d" % h), half("o16", h, 8)), a("nr", at + 8, at + 136), Op.add)
        for c in range(c1 - 1, c0 - 1, -1):
            to = half("yk32" if last else "ks_%d" % t, c, 64)
            if c % 2 and not last:
                ts(to, half("fr", c, 64), 2.0 ** -12, Op.mult, 0.0, Op.add)
            else:
                ts(half("fu", c, 64), half("fr", c, 64), *((12, Op.logical_shift_right) if c % 2 else (4095, Op.bitwise_and)))
                (pool if last and h else copy)(to, half("fu", c, 64))
        if last:
            dmas("y", "ok%d" % h, [(T.yk[:, 128 * h:128 * h + 128], half("yk32", h)[0])], [], [half("yk32", h)], 2 ** 16)
        else:
            send(half("k16_%d" % (t + 1), h), half("ks_%d" % t, h), "k%d_%d" % (h, t + 1), nxt, prv)

        now_[0] = "phages%d" % h
        ts(half("pa", h), sa, -1.0, Op.mult, 0.0, Op.max)
        mm(a(cb, 128, 256), a("ones"), a("qu"), True, False)
        mm(a(cb, 128, 256), a("idn"), half("pa", h), False, True)
        tt(half("pt", h), half("ph_", h), a(cb, 128, 256), Op.mult)
        ts(half("pn", h), half("pt", h), 5, Op.logical_shift_right, 2047, Op.bitwise_and)
        pool(half("yp32" if last else "ps_%d" % t, h), half("pn", h))
        if last:
            dmas("y", "op%d" % h, [(T.yp[:, 128 * h:128 * h + 128], half("yp32", h)[0])], [], [half("yp32", h)], 2 ** 16)
        elif h == 0:
            send(a("p16_%d" % (t + 1)), a("ps_%d" % t), "p_%d" % (t + 1), prv, nxt)

        now_[0] = "writes%d" % h
        x0, x1 = 256 * h, 256 * h + 256
        act(a("cy", x0 + 1, x1, 2), ind(xt(t, 0), names16(0, h)))
        tt(half("dk", h), ind(table, names16(1, h)), a("cy", x0 + 1, x1, 2), Op.subtract)
        ts(a("cy", x0, x1, 2), half("dk", h), ROUND, Op.add, ROUND, Op.is_equal)
        scan(a("ys", x0, x1), a("sc"), a("cy", x0, x1), 0.0, Op.mult, Op.add)
        ts(half("vv", h), a("ys", x0 + 1, x1, 2), 0.0, Op.is_lt, 256.0, Op.mult)
        pool(a("nm", x0 + 30, x1, 32), names16(0, h))
        tt(a("eq", x0, x1), ind(a("nr", at - 8, at + 8), a("bl")), a("nr", at + 136, at + 392), Op.not_equal)
        scan(back("mw", x0, x1), back("nm", x0, x1), back("eq", x0, x1), 0.0, Op.max, Op.mult)
        ts(half("w16", h, 8), a("mw", x0, x1, 32), a("lf", 0, 1), Op.max)

    turns = [0]
    for t in range(RO):
        now_[1] = t
        for h in (1, 0):
            half_round(t, h)
        now_[0] = "table"
        for u in range(COPY):
            lo, hi = 32 + 2048 // COPY * u, 32 + 2048 // COPY * (u + 1)
            pool(xt(t + 1, lo, hi), xt(t, lo, hi))
        for b in range(7, -1, -1):
            tt(ind(xt(t + 1, 0), half("w16", b, 2)), a("ys", 64 * b + 1, 64 * b + 64, 2), half("vv", b, 32), Op.add)
        if t == RO - 1:
            dmas("y", "oy", [(T.yx[:], xt(RO)[0])], [], [xt(RO)], 2 ** 19)
        else:
            act(a("jk"), a("fl", 0, 288, 18), AF.Sign, acc=a("ac", t, t + 1), scale=-1.0, bias=-10240.0)
            mm(a("m0", 500, 501), a("gmf"), a("ac", t, t + 1), True, True)
            ts(a("aa"), a("aa"), a("m0", 500, 501), Op.add, 256 * 2.0 ** 18, Op.add)
            ts(a("ab"), a("aa"), 15 << 19, Op.bitwise_and)
            act(a("rst", 0, 128, 16), a("ab"), bias=TOP)

    def clash(hist, q, outs, ins, banks):
        for kind, lst in (("w", outs), ("r", ins)):
            for x in lst:
                for k2, lo, hi, q2, who in hist.get(x[1], ()):
                    same = q2 == q and q != "dma"
                    if banks and x[1] in PSUM and not same or not (k2 == kind == "r" or hi <= x[2] or lo >= x[3]):
                        yield who, same and q == "p"

    def note(hist, q, outs, ins, who):
        for kind, lst in (("w", outs), ("r", ins)):
            for x in lst:
                e = hist.setdefault(x[1], [])
                if kind == "w":
                    e[:] = [y for y in e if not (y[1] >= x[2] and y[2] <= x[3])]
                e.append((kind, x[2], x[3], q, who))

    def planned():
        hist, N = {}, len(tasks)
        for n, x in enumerate(tasks):
            q = x["q"] if x["kind"] == "call" else "dma"
            x["needs"], x["gaps"], x["banks"], at = {}, {}, set(), 0
            for call, outs, ins, cost in x["calls"]:
                for who, free in clash(hist, q, outs, ins, False):
                    if who != n and (0 if free else HOP) - at > x["needs"].get(who, -1e9):
                        x["needs"][who], x["gaps"][who] = (0 if free else HOP) - at, (0 if free else 1, at)
                note(hist, q, outs, ins, n)
                x["banks"].update(y[1] for y in outs + ins if y[1] in PSUM)
                at += cost
            x["cost"] = at
        before = [{w: d + tasks[w]["after"] for w, d in x["needs"].items()} for x in tasks]
        nexts = [[] for x in tasks]
        for n, x in enumerate(before):
            for w in x:
                nexts[w].append(n)

        def direct(n, w):
            return not any(w in before[u] and before[u][w] >= 0 and d >= 0 and before[u][w] + tasks[u]["cost"] + d >= before[n][w] for u, d in before[n].items())

        needs = [[w for w in before[n] if direct(n, w)] for n in range(N)]
        upon = [(n, needs[n]) for n in range(N - 1, -1, -1) if needs[n]]

        def in_order(key):
            for n, ws in upon:
                k = key[n]
                for w in ws:
                    if key[w] > k:
                        key[w] = k
            return [n for k, n in sorted(zip(key, range(N)))]

        queues = list(Q)
        scale = [6 / len(SPEEDS) / (s[0] + s[1]) for s in SPEEDS]
        costs = [[(x["cost"] + ((sc if x["stage"] == "table" else pick) - 1) * x["picks"]) * (far if x["moves"] else slow * (pe if x["q"] == "p" else 1)) * z
                  for x in tasks] for (slow, far, pe, pick, sc, hop), z in zip(SPEEDS, scale)]
        gaps = [[{w: (tasks[w]["after"] * far + x["gaps"][w][0] * HOP * hop - x["gaps"][w][1] * slow * pe) * z for w in needs[n]} for n, x in enumerate(tasks)]
                for (slow, far, pe, pick, sc, hop), z in zip(SPEEDS, scale)]
        hops = [HOP * s[5] * z for s, z in zip(SPEEDS, scale)]
        fars = [s[1] * z for s, z in zip(SPEEDS, scale)]
        banks = [tuple(PSUM.index(b) for b in sorted(x["banks"])) for x in tasks]
        trios = [(k, k + 1, k + 2) for k in range(0, len(SPEEDS), 3)]
        briefs = [[(queues.index(x["q"]),) + tuple(costs[m][n] for m in trio) + ([(w,) + tuple(gaps[m][n][w] for m in trio) for w in needs[n]], banks[n],
                    x["moves"] and [(x["moves"][0] * fars[m], sum(x["moves"]) * fars[m]) for m in trio]) for n, x in enumerate(tasks)] for trio in trios]
        finals = [n for n in range(N) if not nexts[n]]

        def length(order, k3, old, same, check, limit):
            brief = briefs[k3]
            h0, h1, h2 = (hops[m] for m in trios[k3])
            if same:
                marks = old[1][:same // MARK + 1]
                free, bank, engines = marks.pop()
                end, free, bank = old[0][:], free[:], bank[:]
            else:
                marks, end, free, bank, engines = [], [0] * N, [(0, 0, 0)] * 5, [(2, 0, 0, 0)] * 8, (0, 0, 0)
            for k in range(MARK * len(marks), N, MARK):
                if k > check:
                    x, y = old[1][len(marks)][0], free
                    if min(sum(y[0]) - sum(x[0]), sum(y[1]) - sum(x[1])) > limit:
                        return None
                marks.append((free[:], bank[:], engines))
                for n in order[k:k + MARK]:
                    q, c0, c1, c2, need, bk, moves = brief[n]
                    a0, a1, a2 = free[q]
                    for w, d0, d1, d2 in need:
                        e0, e1, e2 = end[w]
                        e0 += d0
                        if e0 > a0:
                            a0 = e0
                        e1 += d1
                        if e1 > a1:
                            a1 = e1
                        e2 += d2
                        if e2 > a2:
                            a2 = e2
                    if bk:
                        for b in bk:
                            o, e0, e1, e2 = bank[b]
                            if o != q:
                                if e0 > a0:
                                    a0 = e0
                                if e1 > a1:
                                    a1 = e1
                                if e2 > a2:
                                    a2 = e2
                        o = (q, a0 + c0 + h0, a1 + c1 + h1, a2 + c2 + h2)
                        for b in bk:
                            bank[b] = o
                    if moves:
                        free[q] = (a0 + c0, a1 + c1, a2 + c2)
                        a0, a1, a2 = max(a0, engines[0] - moves[0][0]), max(a1, engines[1] - moves[1][0]), max(a2, engines[2] - moves[2][0])
                        engines = (a0 + moves[0][1], a1 + moves[1][1], a2 + moves[2][1])
                        end[n] = (a0 + c0, a1 + c1, a2 + c2)
                    else:
                        free[q] = end[n] = (a0 + c0, a1 + c1, a2 + c2)
            lasts = [max((end[n][u] + tasks[n]["after"] * fars[m], n) for n in finals) for u, m in enumerate(trios[k3])]
            return end, marks, lasts, sum(x[0] for x in lasts)

        runs, tried = [None] * len(trios), []

        def total(order, limit=1e12, same=0, check=1e9):
            new, gap = [], 0
            for k3 in range(len(trios)):
                r = length(order, k3, runs[k3], same, check, limit + SLACK - gap)
                if r is None:
                    return 1e12
                if limit < 1e12:
                    gap += r[3] - runs[k3][3]
                    if gap > limit + SLACK * (len(trios) - 1 - k3):
                        return 1e12
                new.append(r)
            tried[:] = new
            return sum(r[3] for r in new)

        def blocks(order):
            runs[:] = tried
            held, ahead, found = {}, [None] * N, []
            for n in order:
                q = tasks[n]["q"]
                ahead[n] = [held.get(q)] + [held.get(b) for b in banks[n]] + [held.get("engines")] * bool(tasks[n]["moves"])
                held[q] = n
                for b in banks[n]:
                    held[b] = n
                if tasks[n]["moves"]:
                    held["engines"] = n
            for k3, trio in enumerate(trios):
                end = runs[k3][0]
                for u, m in enumerate(trio):
                    n = runs[k3][2][u][1]
                    while n is not None:
                        at, who = end[n][u] - costs[m][n] - 1e-6, None
                        for w, d in gaps[m][n].items():
                            if end[w][u] + d >= at:
                                who = w
                        if who is None and at > 0:
                            who = max((end[w][u] + hops[m] * (tasks[w]["q"] != tasks[n]["q"]), w) for w in ahead[n] if w is not None)[1]
                            if tasks[n]["moves"] and ahead[n][-1] is not None and end[who][u] < at:
                                who = ahead[n][-1]
                        if who is not None and who not in before[n]:
                            found.append((who, n))
                        n = who
            return found

        rng = np.random.default_rng(SEED)

        step, seen_ = [], {}
        for x in tasks:
            o = (x["calls"][0][1] + x["calls"][0][2])[0]
            name = "%s%s:%s%s%d" % (x["stage"][0], x["stage"][-1], x["q"], "e" if o[1] in PSUM[:3] else o[1].rstrip("0123") if "_" in o[1][2:-1] else o[1], o[2])
            seen_[name, x["round"]] = seen_.get((name, x["round"]), 0) + 1
            step.append(name + ".%d" % seen_[name, x["round"]])
        names = sorted(set(step))
        where = np.array([names.index(x) for x in step])
        rounds = np.array([x["round"] + (x["stage"] != "start") for x in tasks])
        opens = [[n for n in range(N) if rounds[n] == t + 1 and ":vd3" in step[n]] for t in range(RO)]

        def timetable(where, own):
            start = sum(np.array([e[u] for e in runs[k3][0]]) - np.array(costs[m]) for k3, trio in enumerate(trios) for u, m in enumerate(trio)) / 3
            first = np.array([0] + [min(start[n] for n in opens[t]) for t in range(RO)])
            times = np.zeros(3 * len(names))
            for t in ((4, 1, 3, 2, 0) if not own else (3, 4, 1, 2, 0)):
                times[where[rounds == t]] = start[rounds == t] - first[t]
            if not own:
                first[1:] = first[1] + (first[3] - first[2]) * np.arange(RO)
            return times, first[rounds]

        given = {k: 10 * float(v) for k, v in (x.split("=") for x in TIMES.split())}
        times = np.array([given[x] for x in names])
        shift = (given["first"] + given["period"] * (rounds - 1)) * (rounds > 0)
        order = in_order((times[where] + shift).tolist())
        best = now = (total(order), order)
        pairs, own, kept = blocks(order), False, (times, shift)
        for n in range(STEPS):
            if n == STEPS - APART:
                times, shift = np.tile(kept[0][:len(names)], 3), kept[1]
                where, own, now = where + len(names) * np.array((0,) + CLASS)[rounds], True, best
                total(now[1])
                pairs = blocks(now[1])
            elif n % ANEW == 0:
                new, moved = timetable(where, own)
                order = in_order((new[where] + moved).tolist())
                cost = total(order)
                if cost <= now[0] + 100 + LOOSE * max(0, 0.7 - n / (STEPS - APART)):
                    now, times, shift, pairs = (cost, order), new, moved, blocks(order)
            new = times.copy()
            if rng.random() < AIM:
                u, v = pairs[int(rng.integers(len(pairs)))]
                key = new[where] + shift
                if rng.random() < 0.5:
                    new[where[v]] = min(key[u], key[v]) - 1 - rng.exponential() * 30 - shift[v]
                else:
                    at, todo = max(key[u], key[v]) + 1 + rng.exponential() * 30, [u]
                    while todo:
                        w = todo.pop()
                        if key[w] < at:
                            key[w], new[where[w]] = at, at - shift[w]
                            todo += nexts[w]
            else:
                at = int(rng.integers(N))
                new[np.unique(where[at:at + (1 if rng.random() < 0.6 else int(rng.integers(2, 12)))])] += rng.normal() * (150, 500, 1500)[int(rng.integers(3))]
            order = in_order((new[where] + shift).tolist())
            if order == now[1]:
                times = new
                continue
            limit = (WARM * (1 - n / (STEPS - APART)) if not own else MILD * (STEPS - n) / APART) * rng.exponential()
            same = next(k for k, (u, v) in enumerate(zip(order, now[1])) if u != v)
            cost = total(order, limit, same, same + 2 * AFTER)
            if cost <= now[0] + limit:
                pairs = blocks(order)
                now, times = (cost, order), new
                if cost < best[0]:
                    best, kept = now, (new, shift)

        now = best
        total(now[1])
        pairs = blocks(now[1])
        for n in range(MOVES):
            order = now[1]
            if rng.random() < AIM:
                u, v = pairs[int(rng.integers(len(pairs)))]
                lo, hi = sorted((order.index(u), order.index(v)))
            else:
                lo = int(rng.integers(N - 1))
                hi = min(N - 1, lo + 1 + int(rng.exponential() * REACH))
            run = order[lo:hi + 1]
            if rng.random() < 0.5:
                moved = {run[-1]}
                for w in run[-2::-1]:
                    if any(x in moved for x in nexts[w]):
                        moved.add(w)
                run = [w for w in run if w in moved] + [w for w in run if w not in moved]
            else:
                moved = {run[0]}
                for w in run[1:]:
                    if any(x in moved for x in before[w]):
                        moved.add(w)
                run = [w for w in run if w not in moved] + [w for w in run if w in moved]
            order = order[:lo] + run + order[hi + 1:]
            if order == now[1]:
                continue
            limit = HEAT * (1 - n / MOVES) * rng.exponential()
            new = (total(order, limit, lo, hi + AFTER), order)
            if new[0] <= now[0] + limit:
                pairs = blocks(order)
                now, best = new, min(best, new)
        INFO["total"] = total(best[1])
        INFO["best"] = [int(tried[m // 3][2][m % 3][0] * 0.83 / scale[m]) for m in range(len(SPEEDS))]
        return best[1]

    if not PLAN:
        PLAN.extend(planned())

    hist, seen, known, count, left = {}, {q: {} for q in Q}, {}, {}, []

    def waits(q, needs):
        want = {}
        for (sem, val), free_ in needs:
            if not free_:
                want[sem] = max(want.get(sem, 0), val)
        for sem, val in sorted(want.items()):
            if seen[q].get(sem, 0) < val:
                Q[q].wait_ge(T.sem[sem], val)
                seen[q][sem] = val
                for s2, v2 in known.get((sem, val), {}).items():
                    seen[q][s2] = max(seen[q].get(s2, 0), v2)

    for n in PLAN:
        q, kind = tasks[n]["q"], tasks[n]["kind"]
        for call, outs, ins, cost in tasks[n]["calls"]:
            waits(q, clash(hist, q if kind == "call" else "dma", outs, ins, True))
            if kind == "call":
                sem, count[q] = q, count.get(q, 0) + 1
                call().then_inc(T.sem[q], 1)
            elif kind == "dma":
                sem = call[0]
                for out, in_ in call[1]:
                    Q[q].dma_start(out, in_).then_inc(T.sem[sem], 16)
                    count[sem] = count.get(sem, 0) + 16
            else:
                sem, gone, dst, src = call
                rid, pid = topo.addr(dst, core)
                g.remote_dma(outs[0][0], ins[0][0], T.sem[sem], T.sem[gone], pid, rid, topo.mask(core, dst))
                left.append((gone, len(topo.engines(core, dst))))
                count[sem], ins = len(topo.engines(src, core)), []
            known[(sem, count[sem])] = dict(seen[q]) if kind != "send" else {}
            note(hist, q if kind == "call" else "dma", outs, ins, (sem, count[sem]))
    for sem, val in left:
        g.wait_ge(T.sem[sem], val)
    for sem in count:
        if sem[0] == "o" or len(sem) == 1:
            if seen["y"].get(sem, 0) < count[sem]:
                g.sync.wait_ge(T.sem[sem], count[sem])
